import numpy as np
import ml_dtypes


def mxq(x, axis, fmt="e4m3"):
    dtype, down = {"e4m3": (ml_dtypes.float8_e4m3fn, 7), "e5m2": (ml_dtypes.float8_e5m2, 14)}[fmt]
    v = np.moveaxis(np.asarray(x, np.float32).astype(ml_dtypes.bfloat16).astype(np.float64), axis, -1)
    blocks = v.reshape(v.shape[:-1] + (-1, 32))
    amax = np.abs(blocks).max(-1, keepdims=True)
    byte = np.maximum(np.where(amax > 0, np.frexp(amax)[1] - 1 + 127, 0) - down, 1)
    scale = np.exp2(byte - 127.0)
    codes = (blocks / scale).astype(np.float32).astype(dtype).astype(np.float64)
    return np.moveaxis((codes * scale).reshape(v.shape), -1, axis)


WIDE = False


def mx_kscale(k):
    if not WIDE:
        return np.ones(k)
    levels = np.array([10, -10, 5, -5, 0])
    if k % 512:
        return np.exp2(np.random.permutation(np.resize(levels, k // 32))).repeat(32)
    a = np.empty((k // 512, 16))
    for p in range(k // 512):
        a[p, :8] = np.random.permutation(np.resize(levels, 8))
        for g in range(8):
            far = levels[np.abs(levels - a[p, g]) >= 10]
            a[p, g + 8] = far[np.random.randint(len(far))]
    return np.exp2(a.ravel()).repeat(32)


def f64(x):
    return np.asarray(x).astype(np.float64)


def striped(idx):
    return np.tile(idx.reshape(-1, 16).T, (8, 1)).astype(np.uint16)


def unstriped(offs):
    return offs[:16].T.reshape(-1).astype(np.int64)


E2M1 = np.array([0.0, 0.5, 1.0, 1.5, 2.0, 3.0, 4.0, 6.0, -0.0, -0.5, -1.0, -1.5, -2.0, -3.0, -4.0, -6.0])


def pack_weight(w, fmt):
    k, n = w.shape
    w = f64(np.asarray(w, np.float32).astype(ml_dtypes.bfloat16)).reshape(k // 32, 32, n)
    amax = np.abs(w).max(1)
    if fmt == "e4m3":
        byte = np.frexp(amax)[1] - 1 + 127 - 7
    else:
        mant, ex = np.frexp(amax / 6.0)
        byte = np.where(mant > 0.5, ex, ex - 1) + 127
    byte = np.clip(np.where(amax > 0, byte, 1), 1, 254)
    scaled = (w * np.exp2(127.0 - byte)[:, None, :]).reshape(k, n).astype(np.float32)
    by_word = np.ascontiguousarray(scaled.reshape(k // 512, 128, 4, n).transpose(0, 1, 3, 2))
    if fmt == "e4m3":
        words = by_word.astype(ml_dtypes.float8_e4m3fn).view(np.uint8)
    else:
        c = by_word.astype(ml_dtypes.float4_e2m1fn).view(np.uint8) & 0xF
        words = (c[..., 0::2] | (c[..., 1::2] << 4)).reshape(k // 512, 128, 2 * n)
    return np.ascontiguousarray(words), np.ascontiguousarray(byte.astype(np.uint8).reshape(k // 512, 16, n))


def unpack_weight(words, scales, fmt):
    g, _, n = scales.shape
    words = np.ascontiguousarray(words).reshape(g, 128, n, -1)
    if fmt == "e4m3":
        vals = words.view(ml_dtypes.float8_e4m3fn).astype(np.float64)
    else:
        nib = np.empty((g, 128, n, 4), np.uint8)
        nib[..., 0::2] = words & 0xF
        nib[..., 1::2] = words >> 4
        vals = E2M1[nib]
    vals = vals * np.repeat(np.exp2(scales.astype(np.float64) - 127.0), 8, axis=1)[..., None]
    return vals.transpose(0, 1, 3, 2).reshape(g * 512, n)


K, T, E, B, H, N = 1024, 1024, 8, 4, 512, 256


def setup_inputs():
    n = np.random.standard_normal
    s = mx_kscale(K)
    u = mx_kscale(H)
    slot_token = np.random.permutation(T)[:128 * B]
    block = np.sort(np.random.randint(E, size=B))
    x = pack_weight(n((K, T)) * s[:, None], "e4m3")
    w = pack_weight(n((K, N)) / np.sqrt(K) / s[:, None], "e4m3")
    wa = pack_weight(n((K, E * H)) / np.sqrt(K) / s[:, None] * np.tile(u, E), "e4m3")
    wb = pack_weight(n((H, E * N)) / np.sqrt(H) / u[:, None], "e4m3")
    return {
        "x_words": x[0],
        "x_scales": x[1],
        "w_words": w[0],
        "w_scales": w[1],
        "wa_words": wa[0],
        "wa_scales": wa[1],
        "wb_words": wb[0],
        "wb_scales": wb[1],
        "gate": (np.tile(np.random.uniform(0.2, 1.0, 128 * B), (128, 1))).astype(np.float32),
        "offs": striped(slot_token),
        "offs2": striped((block[:, None] * H + np.arange(H)).reshape(-1)),
        "offs3": striped((block[:, None] * N + np.arange(N)).reshape(-1)),
    }


def reference(x_words, x_scales, w_words, w_scales, wa_words, wa_scales, wb_words, wb_scales, gate, offs, offs2, offs3):
    w = unpack_weight(w_words, w_scales, "e4m3")
    idx, idx2, idx3 = unstriped(offs), unstriped(offs2), unstriped(offs3)
    x = unpack_weight(x_words, x_scales, "e4m3")
    out = w.T @ x
    wa = unpack_weight(wa_words, wa_scales, "e4m3")[:, idx2]
    wb = unpack_weight(wb_words, wb_scales, "e4m3")[:, idx3]
    xq = x[:, idx]
    h = np.concatenate([wa[:, m * H:(m + 1) * H].T @ xq[:, 128 * m:128 * m + 128] for m in range(B)], axis=1)
    hq = mxq(h, 0, "e4m3")
    y = np.concatenate([wb[:, m * N:(m + 1) * N].T @ hq[:, 128 * m:128 * m + 128] for m in range(B)], axis=1)
    out[:, idx] += f64(gate[:1]) * y
    return out

@@ -1,0 +1,187 @@
+from contextlib import ExitStack
+
+import concourse.mybir as mybir
+from concourse.masks import make_identity
+
+K, T, E, B, H, N = 1024, 1024, 8, 4, 512, 256
+P = 128
+SLOTS = P * B
+FLOPS = 2 * K * N * T + 2 * K * H * SLOTS + 2 * H * N * SLOTS
+
+F32 = mybir.dt.float32
+BF16 = mybir.dt.bfloat16
+I32 = mybir.dt.int32
+U32 = mybir.dt.uint32
+U16 = mybir.dt.uint16
+U8 = mybir.dt.uint8
+FP8X4 = mybir.dt.float8_e4m3fn_x4
+MULT = mybir.AluOpType.mult
+ADD = mybir.AluOpType.add
+
+X_ROW = (0, 4)
+W_ROW = (0, 4)
+WA_ROW = (8, 12)
+WB_ROW = 8
+
+
+def tile_moe_dyl_none_kernel(
+    tc, x_words, x_scales, w_words, w_scales, wa_words, wa_scales, wb_words, wb_scales, gate, offs, offs2, offs3, out
+):
+    nc = tc.nc
+    with ExitStack() as ctx:
+        keep = ctx.enter_context(tc.tile_pool(name="keep", bufs=1))
+        psum = ctx.enter_context(tc.psum_pool(name="psum", bufs=1))
+
+        def sb(name, shape, dtype):
+            return keep.tile(shape, dtype, name=name, align_bytes=64)
+
+        def load_words(tile, words):
+            nc.sync.dma_start(tile, words.rearrange("p n t -> p (n t)").bitcast(I32))
+
+        def load_scales(queue, plane, scales, first_row):
+            rows = 4 * scales.shape[0]
+            for q in range(4):
+                queue.dma_start(
+                    plane[32 * q + first_row : 32 * q + first_row + rows, :].bitcast(I32),
+                    scales[:, 4 * q : 4 * q + 4, :].bitcast(I32),
+                )
+
+        def gather(dst, window, offsets, first, count):
+            nc.vector.tensor_copy(dst, window.indirect(offsets[:, first // 16 : (first + count) // 16]))
+
+        def mm(acc, lhs, lhs_plane, lhs_row, lhs_cols, rhs, rhs_plane, rhs_row, rhs_cols, start, stop):
+            nc.tensor.matmul_mx(
+                out=acc,
+                lhsT=lhs[:, lhs_cols].bitcast(FP8X4),
+                lhsT_scale=lhs_plane[lhs_row:P, lhs_cols],
+                rhs=rhs[:, rhs_cols].bitcast(FP8X4),
+                rhs_scale=rhs_plane[rhs_row:P, rhs_cols],
+                start=start,
+                stop=stop,
+            )
+
+        idx = sb("idx", [P, SLOTS // 16], U16)
+        idx2 = sb("idx2", [P, B * H // 16], U16)
+        idx3 = sb("idx3", [P, B * N // 16], U16)
+        x_w = [sb("x_w%d" % s, [P, T], I32) for s in range(2)]
+        w_w = sb("w_w", [P, 2, N], I32)
+        wa_w = [sb("wa_w%d" % s, [P, E * H], I32) for s in range(2)]
+        wb_w = sb("wb_w", [P, E * N], I32)
+        x_s = sb("x_s", [P, T], U8)
+        w_s = sb("w_s", [P, N], U8)
+        wa_s = sb("wa_s", [P, E * H], U8)
+        wb_s = sb("wb_s", [P, E * N], U8)
+        gate_sb = sb("gate_sb", [P, SLOTS], F32)
+        ident = sb("ident", [P, P], F32)
+
+        for plane in (x_s, wa_s, w_s, wb_s):
+            nc.vector.memset(plane[:].bitcast(I32), 0)
+
+        nc.sync.dma_start(idx[:], offs)
+        load_words(x_w[0][:], x_words[0])
+        nc.sync.dma_start(idx2[:], offs2)
+        load_scales(nc.scalar, x_s, x_scales, X_ROW[0])
+        load_scales(nc.gpsimd, wa_s, wa_scales, WA_ROW[0])
+        load_words(x_w[1][:], x_words[1])
+        nc.sync.dma_start(idx3[:], offs3)
+        load_words(wa_w[0][:], wa_words[0])
+        nc.sync.dma_start(w_w[:], w_words.rearrange("s p n t -> p s (n t)").bitcast(I32))
+        load_scales(nc.scalar, w_s, w_scales, W_ROW[0])
+        load_scales(nc.gpsimd, wb_s, wb_scales, WB_ROW)
+        load_words(wa_w[1][:], wa_words[1])
+        load_words(wb_w[:], wb_words[0])
+        nc.sync.dma_start(gate_sb[:], gate)
+        make_identity(nc, ident[:])
+
+        xq_w = [sb("xq_w%d" % s, [P, SLOTS], U32) for s in range(2)]
+        xq_s = sb("xq_s", [P, SLOTS], U8)
+        waq_w = [sb("waq_w%d" % s, [P, B * H], U32) for s in range(2)]
+        waq_s = sb("waq_s", [P, B * H], U8)
+        wbq_w = sb("wbq_w", [P, B * N], U32)
+        wbq_s = sb("wbq_s", [P, B * N], U8)
+
+        for s in range(2):
+            gather(xq_w[s][:], x_w[s][:].bitcast(U32), idx, 0, SLOTS)
+        gather(xq_s[:], x_s[:], idx, 0, SLOTS)
+        for pair in range(2):
+            gather(waq_s[:, pair * 2 * H : (pair + 1) * 2 * H], wa_s[:], idx2, pair * 2 * H, 2 * H)
+        for pair in range(2):
+            gather(waq_w[0][:, pair * 2 * H : (pair + 1) * 2 * H], wa_w[0][:].bitcast(U32), idx2, pair * 2 * H, 2 * H)
+        gather(wbq_s[:], wb_s[:], idx3, 0, B * N)
+
+        result = [sb("result%d" % j, [P, T], F32) for j in range(2)]
+        for j in range(2):
+            for half in range(2):
+                cols = slice(half * 512, (half + 1) * 512)
+                acc = psum.tile([P, 512], F32, name="acc", tag="wide", bufs=4)
+                for s in range(2):
+                    mm(acc[:], w_w[:, s, :], w_s, W_ROW[s], slice(j * P, (j + 1) * P),
+                       x_w[s], x_s, X_ROW[s], cols, s == 0, s == 1)
+                nc.scalar.copy(result[j][:, cols], acc[:])
+
+        base_slots = sb("base_slots", [P, 2, SLOTS], F32)
+        for j in range(2):
+            acc = psum.tile([P, 512], F32, name="acc2", tag="turn", bufs=2)
+            for s in range(2):
+                mm(acc[:], w_w[:, s, :], w_s, W_ROW[s], slice(j * P, (j + 1) * P),
+                   xq_w[s], xq_s, X_ROW[s], slice(0, SLOTS), s == 0, s == 1)
+            nc.scalar.copy(base_slots[:, j, :], acc[:])
+
+        h_acc = []
+        for m in range(B):
+            acc = psum.tile([P, 512], F32, name="h_acc", tag="wide", bufs=4)
+            mm(acc[:], xq_w[0], xq_s, X_ROW[0], slice(m * P, (m + 1) * P),
+               waq_w[0], waq_s, WA_ROW[0], slice(m * H, (m + 1) * H), True, False)
+            h_acc.append(acc)
+
+        for m in range(B):
+            gather(waq_w[1][:, m * H : (m + 1) * H], wa_w[1][:].bitcast(U32), idx2, m * H, H)
+        for pair in range(2):
+            gather(wbq_w[:, pair * 2 * N : (pair + 1) * 2 * N], wb_w[:].bitcast(U32), idx3, pair * 2 * N, 2 * N)
+
+        h_grouped = []
+        for pair in range(2):
+            turned = psum.tile([P, 2, 2, P], F32, name="turned", tag="turn", bufs=2)
+            for mb in range(2):
+                m = 2 * pair + mb
+                mm(h_acc[m][:], xq_w[1], xq_s, X_ROW[1], slice(m * P, (m + 1) * P),
+                   waq_w[1], waq_s, WA_ROW[1], slice(m * H, (m + 1) * H), False, True)
+                h_bf = sb("h_bf%d" % m, [P, 2, P, 2], BF16)
+                nc.scalar.copy(h_bf[:], h_acc[m][:].rearrange("s (p u e) -> s u p e", u=2, e=2))
+                h_words = h_bf[:].rearrange("s u p e -> s (u p e)").bitcast(F32)
+                for u in range(2):
+                    nc.tensor.transpose(turned[:, mb, u, :], h_words[:, u * P : (u + 1) * P], ident[:])
+            grouped = sb("grouped%d" % pair, [P, 2, P, 2], F32)
+            nc.scalar.copy(grouped[:], turned[:].rearrange("p b u s -> p b s u"))
+            h_grouped.append(grouped)
+
+        y_acc = []
+        for pair in range(2):
+            hq_w = sb("hq_w%d" % pair, [P, 2 * P], U32)
+            hq_s = sb("hq_s%d" % pair, [P, 2 * P], U8)
+            nc.vector.quantize_mx(
+                out=hq_w[:].bitcast(FP8X4),
+                scales=hq_s[:],
+                in_=h_grouped[pair][:].rearrange("p b s u -> p (b s u)").bitcast(BF16),
+            )
+            acc = psum.tile([P, 2, 2 * P], F32, name="y_acc", tag="y", bufs=2)
+            for mb in range(2):
+                m = 2 * pair + mb
+                for j in range(2):
+                    mm(acc[:, j, mb * P : (mb + 1) * P], wbq_w, wbq_s, WB_ROW,
+                       slice(m * N + j * P, m * N + (j + 1) * P),
+                       hq_w, hq_s, 0, slice(mb * P, (mb + 1) * P), True, True)
+            y_acc.append(acc)
+
+        values = sb("values", [P, 2, SLOTS], F32)
+        for pair in range(2):
+            cols = slice(pair * 2 * P, (pair + 1) * 2 * P)
+            gated = sb("gated%d" % pair, [P, 2, 2 * P], F32)
+            nc.vector.tensor_tensor(
+                gated[:], y_acc[pair][:], gate_sb[:, cols].unsqueeze(1).to_broadcast([P, 2, 2 * P]), MULT
+            )
+            nc.vector.tensor_tensor(values[:, :, cols], gated[:], base_slots[:, :, cols], ADD)
+            nc.vector.tensor_copy(result[0][:].indirect(idx[:, pair * 16 : (pair + 1) * 16]), values[:, 0, cols])
+        nc.sync.dma_start(out[0:P, :], result[0][:])
+        nc.vector.tensor_copy(result[1][:].indirect(idx[:]), values[:, 1, :])
+        nc.sync.dma_start(out[P : 2 * P, :], result[1][:])

@@ -15,8 +15,7 @@ U32 = mybir.dt.uint32
 U16 = mybir.dt.uint16
 U8 = mybir.dt.uint8
 FP8X4 = mybir.dt.float8_e4m3fn_x4
-MULT = mybir.AluOpType.mult
-ADD = mybir.AluOpType.add
+COPY = mybir.ActivationFunctionType.Copy
 
 X_ROW = (0, 4)
 W_ROW = (0, 4)
@@ -30,6 +29,7 @@ def tile_moe_dyl_none_kernel(
     nc = tc.nc
     with ExitStack() as ctx:
         keep = ctx.enter_context(tc.tile_pool(name="keep", bufs=1))
+        shared = ctx.enter_context(tc.tile_pool(name="shared", bufs=1))
         psum = ctx.enter_context(tc.psum_pool(name="psum", bufs=1))
 
         def sb(name, shape, dtype):
@@ -71,117 +71,147 @@ def tile_moe_dyl_none_kernel(
         w_s = sb("w_s", [P, N], U8)
         wa_s = sb("wa_s", [P, E * H], U8)
         wb_s = sb("wb_s", [P, E * N], U8)
-        gate_sb = sb("gate_sb", [P, SLOTS], F32)
+        gate_col = sb("gate_col", [P, B], F32)
         ident = sb("ident", [P, P], F32)
 
-        for plane in (x_s, wa_s, w_s, wb_s):
+        waq_s = sb("waq_s", [P, B * H], U8)
+        for plane in (wa_s, w_s, x_s, wb_s, waq_s):
             nc.vector.memset(plane[:].bitcast(I32), 0)
 
         nc.sync.dma_start(idx[:], offs)
         load_words(x_w[0][:], x_words[0])
         nc.sync.dma_start(idx2[:], offs2)
-        load_scales(nc.scalar, x_s, x_scales, X_ROW[0])
-        load_scales(nc.gpsimd, wa_s, wa_scales, WA_ROW[0])
-        load_words(x_w[1][:], x_words[1])
-        nc.sync.dma_start(idx3[:], offs3)
-        load_words(wa_w[0][:], wa_words[0])
-        nc.sync.dma_start(w_w[:], w_words.rearrange("s p n t -> p s (n t)").bitcast(I32))
+        nc.sync.dma_start(wa_s[0:P:4, :].bitcast(I32), wa_scales.rearrange("s b c -> (s b) c").bitcast(I32))
         load_scales(nc.scalar, w_s, w_scales, W_ROW[0])
-        load_scales(nc.gpsimd, wb_s, wb_scales, WB_ROW)
+        load_words(x_w[1][:], x_words[1])
+        load_scales(nc.sync, x_s, x_scales, X_ROW[0])
+        nc.sync.dma_start(w_w[:], w_words.rearrange("s p n t -> p s (n t)").bitcast(I32))
+        load_words(wa_w[0][:], wa_words[0])
+        nc.sync.dma_start(idx3[:], offs3)
+        load_scales(nc.sync, wb_s, wb_scales, WB_ROW)
         load_words(wa_w[1][:], wa_words[1])
-        load_words(wb_w[:], wb_words[0])
-        nc.sync.dma_start(gate_sb[:], gate)
         make_identity(nc, ident[:])
 
         xq_w = [sb("xq_w%d" % s, [P, SLOTS], U32) for s in range(2)]
         xq_s = sb("xq_s", [P, SLOTS], U8)
         waq_w = [sb("waq_w%d" % s, [P, B * H], U32) for s in range(2)]
-        waq_s = sb("waq_s", [P, B * H], U8)
-        wbq_w = sb("wbq_w", [P, B * N], U32)
-        wbq_s = sb("wbq_s", [P, B * N], U8)
+        waq_rows = sb("waq_rows", [P, B * H], U8)
 
+        def block(m, width):
+            return slice(m * width, (m + 1) * width)
+
+        gather(xq_w[0][:], x_w[0][:].bitcast(U32), idx, 0, SLOTS)
+        for pair in range(2):
+            gather(waq_rows[:, block(pair, 2 * H)], wa_s[:], idx2, pair * 2 * H, 2 * H)
         for s in range(2):
-            gather(xq_w[s][:], x_w[s][:].bitcast(U32), idx, 0, SLOTS)
+            for r in range(4):
+                nc.sync.dma_start(
+                    waq_s[WA_ROW[s] + r : P : 32, :].bitcast(I32),
+                    waq_rows[64 * s + 4 * r : 64 * s + 64 : 16, :].bitcast(I32),
+                )
+        load_words(wb_w[:], wb_words[0])
+        with nc.allow_non_contiguous_dma(reason="one gate value for each slot, slots on the partitions"):
+            nc.sync.dma_start(gate_col[:], gate[0, :].rearrange("(m p) -> p m", p=P))
+        gather(xq_w[1][:], x_w[1][:].bitcast(U32), idx, 0, SLOTS)
         gather(xq_s[:], x_s[:], idx, 0, SLOTS)
+        wbq_s = [sb("wbq_s0", [P, 2 * N], U8)]
+        gather(wbq_s[0][:], wb_s[:], idx3, 0, 2 * N)
         for pair in range(2):
-            gather(waq_s[:, pair * 2 * H : (pair + 1) * 2 * H], wa_s[:], idx2, pair * 2 * H, 2 * H)
-        for pair in range(2):
-            gather(waq_w[0][:, pair * 2 * H : (pair + 1) * 2 * H], wa_w[0][:].bitcast(U32), idx2, pair * 2 * H, 2 * H)
-        gather(wbq_s[:], wb_s[:], idx3, 0, B * N)
+            gather(waq_w[0][:, block(pair, 2 * H)], wa_w[0][:].bitcast(U32), idx2, pair * 2 * H, 2 * H)
 
         result = [sb("result%d" % j, [P, T], F32) for j in range(2)]
         for j in range(2):
             for half in range(2):
-                cols = slice(half * 512, (half + 1) * 512)
-                acc = psum.tile([P, 512], F32, name="acc", tag="wide", bufs=4)
+                acc = psum.tile([P, 512], F32, name="acc", tag=("turn", "y")[half], bufs=2)
                 for s in range(2):
-                    mm(acc[:], w_w[:, s, :], w_s, W_ROW[s], slice(j * P, (j + 1) * P),
-                       x_w[s], x_s, X_ROW[s], cols, s == 0, s == 1)
-                nc.scalar.copy(result[j][:, cols], acc[:])
+                    mm(acc[:], w_w[:, s, :], w_s, W_ROW[s], block(j, P),
+                       x_w[s], x_s, X_ROW[s], block(half, 512), s == 0, s == 1)
+                nc.scalar.copy(result[j][:, block(half, 512)], acc[:])
 
-        base_slots = sb("base_slots", [P, 2, SLOTS], F32)
-        for j in range(2):
-            acc = psum.tile([P, 512], F32, name="acc2", tag="turn", bufs=2)
-            for s in range(2):
-                mm(acc[:], w_w[:, s, :], w_s, W_ROW[s], slice(j * P, (j + 1) * P),
-                   xq_w[s], xq_s, X_ROW[s], slice(0, SLOTS), s == 0, s == 1)
-            nc.scalar.copy(base_slots[:, j, :], acc[:])
+        base_slots = sb("base_slots", [P, B, N], F32)
+        for pair in range(2):
+            acc = psum.tile([P, 2, N], F32, name="acc2", tag="sum", bufs=2)
+            for mb in range(2):
+                for s in range(2):
+                    mm(acc[:, mb, :], xq_w[s], xq_s, X_ROW[s], block(2 * pair + mb, P),
+                       w_w[:, s, :], w_s, W_ROW[s], slice(0, N), s == 0, s == 1)
+            nc.scalar.copy(base_slots[:, 2 * pair : 2 * pair + 2, :], acc[:])
+
+        def h_pass(acc, m, s):
+            mm(acc[:], xq_w[s], xq_s, X_ROW[s], block(m, P), waq_w[s], waq_s, WA_ROW[s], block(m, H), s == 0, s == 1)
 
         h_acc = []
-        for m in range(B):
-            acc = psum.tile([P, 512], F32, name="h_acc", tag="wide", bufs=4)
-            mm(acc[:], xq_w[0], xq_s, X_ROW[0], slice(m * P, (m + 1) * P),
-               waq_w[0], waq_s, WA_ROW[0], slice(m * H, (m + 1) * H), True, False)
+        for m in range(2):
+            acc = psum.tile([P, 512], F32, name="h_acc", tag="wide", bufs=2)
+            h_pass(acc, m, 0)
             h_acc.append(acc)
 
         for m in range(B):
-            gather(waq_w[1][:, m * H : (m + 1) * H], wa_w[1][:].bitcast(U32), idx2, m * H, H)
-        for pair in range(2):
-            gather(wbq_w[:, pair * 2 * N : (pair + 1) * 2 * N], wb_w[:].bitcast(U32), idx3, pair * 2 * N, 2 * N)
+            gather(waq_w[1][:, block(m, H)], wa_w[1][:].bitcast(U32), idx2, m * H, H)
+        wbq_w = [sb("wbq_w0", [P, 2 * N], U32)]
+        gather(wbq_w[0][:], wb_w[:].bitcast(U32), idx3, 0, 2 * N)
 
-        h_grouped = []
-        for pair in range(2):
-            turned = psum.tile([P, 2, 2, P], F32, name="turned", tag="turn", bufs=2)
-            for mb in range(2):
-                m = 2 * pair + mb
-                mm(h_acc[m][:], xq_w[1], xq_s, X_ROW[1], slice(m * P, (m + 1) * P),
-                   waq_w[1], waq_s, WA_ROW[1], slice(m * H, (m + 1) * H), False, True)
-                h_bf = sb("h_bf%d" % m, [P, 2, P, 2], BF16)
-                nc.scalar.copy(h_bf[:], h_acc[m][:].rearrange("s (p u e) -> s u p e", u=2, e=2))
-                h_words = h_bf[:].rearrange("s u p e -> s (u p e)").bitcast(F32)
-                for u in range(2):
-                    nc.tensor.transpose(turned[:, mb, u, :], h_words[:, u * P : (u + 1) * P], ident[:])
-            grouped = sb("grouped%d" % pair, [P, 2, P, 2], F32)
-            nc.scalar.copy(grouped[:], turned[:].rearrange("p b u s -> p b s u"))
-            h_grouped.append(grouped)
+        grouped = [
+            shared.tile([P, 2, P, 2], F32, name="grouped0", align_bytes=64, offset=0),
+            sb("grouped1", [P, 2, P, 2], F32),
+        ]
 
-        y_acc = []
+        def turn(m):
+            h_bf = sb("h_bf%d" % m, [P, 2, P, 2], BF16)
+            nc.scalar.copy(h_bf[:], h_acc[m][:].rearrange("s (p u e) -> s u p e", u=2, e=2))
+            h_words = h_bf[:].rearrange("s u p e -> s (u p e)").bitcast(F32)
+            turned = psum.tile([P, 2, P], F32, name="turned", tag="turn", bufs=2)
+            for u in range(2):
+                nc.tensor.transpose(turned[:, u, :], h_words[:, block(u, P)], ident[:])
+            nc.scalar.copy(grouped[m // 2][:, m % 2, :, :], turned[:].rearrange("p u s -> p s u"))
+
+        h_pass(h_acc[0], 0, 1)
+        h_pass(h_acc[1], 1, 1)
+        for m in range(B):
+            turn(m)
+            if m + 2 < B:
+                acc = psum.tile([P, 512], F32, name="h_acc", tag="wide", bufs=2)
+                for s in range(2):
+                    h_pass(acc, m + 2, s)
+                h_acc.append(acc)
+
+        values = sb("values", [P, 2, SLOTS], F32)
+
+        def scatter(j, first, count):
+            nc.vector.tensor_copy(
+                result[j][:].indirect(idx[:, first // 16 : (first + count) // 16]), values[:, j, first : first + count]
+            )
+
         for pair in range(2):
             hq_w = sb("hq_w%d" % pair, [P, 2 * P], U32)
             hq_s = sb("hq_s%d" % pair, [P, 2 * P], U8)
             nc.vector.quantize_mx(
                 out=hq_w[:].bitcast(FP8X4),
                 scales=hq_s[:],
-                in_=h_grouped[pair][:].rearrange("p b s u -> p (b s u)").bitcast(BF16),
+                in_=grouped[pair][:].rearrange("p b s u -> p (b s u)").bitcast(BF16),
             )
-            acc = psum.tile([P, 2, 2 * P], F32, name="y_acc", tag="y", bufs=2)
+            if pair == 0:
+                wbq_s.append(shared.tile([P, 2 * N], U8, name="wbq_s1", align_bytes=64, offset=0))
+                wbq_w.append(shared.tile([P, 2 * N], U32, name="wbq_w1", align_bytes=64, offset=2 * N))
+                gather(wbq_s[1][:], wb_s[:], idx3, 2 * N, 2 * N)
+                gather(wbq_w[1][:], wb_w[:].bitcast(U32), idx3, 2 * N, 2 * N)
             for mb in range(2):
                 m = 2 * pair + mb
+                y_acc = psum.tile([P, N], F32, name="y_acc", tag="y", bufs=2)
+                mm(y_acc[:], hq_w, hq_s, 0, block(mb, P), wbq_w[pair], wbq_s[pair], WB_ROW, block(mb, N), True, True)
+                gated = sb("gated%d" % m, [P, N], F32)
+                nc.scalar.activation(gated[:], y_acc[:], COPY, scale=gate_col[:, m : m + 1])
+                total = psum.tile([P, 2, P], F32, name="total", tag="sum", bufs=2)
                 for j in range(2):
-                    mm(acc[:, j, mb * P : (mb + 1) * P], wbq_w, wbq_s, WB_ROW,
-                       slice(m * N + j * P, m * N + (j + 1) * P),
-                       hq_w, hq_s, 0, slice(mb * P, (mb + 1) * P), True, True)
-            y_acc.append(acc)
+                    nc.tensor.matmul(total[:, j, :], base_slots[:, m, block(j, P)], ident[:],
+                                     start=True, stop=False, is_transpose=True)
+                    nc.tensor.matmul(total[:, j, :], gated[:, block(j, P)], ident[:],
+                                     start=False, stop=True, is_transpose=True)
+                nc.scalar.copy(values[:, :, block(m, P)], total[:])
 
-        values = sb("values", [P, 2, SLOTS], F32)
-        for pair in range(2):
-            cols = slice(pair * 2 * P, (pair + 1) * 2 * P)
-            gated = sb("gated%d" % pair, [P, 2, 2 * P], F32)
-            nc.vector.tensor_tensor(
-                gated[:], y_acc[pair][:], gate_sb[:, cols].unsqueeze(1).to_broadcast([P, 2, 2 * P]), MULT
-            )
-            nc.vector.tensor_tensor(values[:, :, cols], gated[:], base_slots[:, :, cols], ADD)
-            nc.vector.tensor_copy(result[0][:].indirect(idx[:, pair * 16 : (pair + 1) * 16]), values[:, 0, cols])
-        nc.sync.dma_start(out[0:P, :], result[0][:])
-        nc.vector.tensor_copy(result[1][:].indirect(idx[:]), values[:, 1, :])
-        nc.sync.dma_start(out[P : 2 * P, :], result[1][:])
+        for m in range(2):
+            for j in range(2):
+                scatter(j, m * P, P)
+        for j in range(2):
+            scatter(j, 2 * P, 2 * P)
+            nc.sync.dma_start(out[block(j, P), :], result[j][:])

@@ -15,7 +15,8 @@ U32 = mybir.dt.uint32
 U16 = mybir.dt.uint16
 U8 = mybir.dt.uint8
 FP8X4 = mybir.dt.float8_e4m3fn_x4
-COPY = mybir.ActivationFunctionType.Copy
+MULT = mybir.AluOpType.mult
+ADD = mybir.AluOpType.add
 
 X_ROW = (0, 4)
 W_ROW = (0, 4)
@@ -60,22 +61,28 @@ def tile_moe_dyl_none_kernel(
                 stop=stop,
             )
 
+        def block(m, width):
+            return slice(m * width, (m + 1) * width)
+
+        def on_shared(name, shape, dtype, offset):
+            return shared.tile(shape, dtype, name=name, align_bytes=64, offset=offset)
+
         idx = sb("idx", [P, SLOTS // 16], U16)
         idx2 = sb("idx2", [P, B * H // 16], U16)
         idx3 = sb("idx3", [P, B * N // 16], U16)
         x_w = [sb("x_w%d" % s, [P, T], I32) for s in range(2)]
         w_w = sb("w_w", [P, 2, N], I32)
-        wa_w = [sb("wa_w%d" % s, [P, E * H], I32) for s in range(2)]
+        wa_w = [sb("wa_w0", [P, E * H], I32), on_shared("wa_w1", [P, E * H], I32, 4096)]
         wb_w = sb("wb_w", [P, E * N], I32)
         x_s = sb("x_s", [P, T], U8)
         w_s = sb("w_s", [P, N], U8)
         wa_s = sb("wa_s", [P, E * H], U8)
         wb_s = sb("wb_s", [P, E * N], U8)
-        gate_col = sb("gate_col", [P, B], F32)
+        waq_s = [sb("waq_s%d" % s, [P, B * H], U8) for s in range(2)]
+        gate_sb = sb("gate_sb", [P, SLOTS], F32)
         ident = sb("ident", [P, P], F32)
 
-        waq_s = sb("waq_s", [P, B * H], U8)
-        for plane in (wa_s, w_s, x_s, wb_s, waq_s):
+        for plane in (wa_s, w_s, x_s, wb_s, waq_s[0], waq_s[1]):
             nc.vector.memset(plane[:].bitcast(I32), 0)
 
         nc.sync.dma_start(idx[:], offs)
@@ -83,12 +90,12 @@ def tile_moe_dyl_none_kernel(
         nc.sync.dma_start(idx2[:], offs2)
         nc.sync.dma_start(wa_s[0:P:4, :].bitcast(I32), wa_scales.rearrange("s b c -> (s b) c").bitcast(I32))
         load_scales(nc.scalar, w_s, w_scales, W_ROW[0])
+        load_scales(nc.gpsimd, wb_s, wb_scales, WB_ROW)
         load_words(x_w[1][:], x_words[1])
         load_scales(nc.sync, x_s, x_scales, X_ROW[0])
         nc.sync.dma_start(w_w[:], w_words.rearrange("s p n t -> p s (n t)").bitcast(I32))
-        load_words(wa_w[0][:], wa_words[0])
         nc.sync.dma_start(idx3[:], offs3)
-        load_scales(nc.sync, wb_s, wb_scales, WB_ROW)
+        load_words(wa_w[0][:], wa_words[0])
         load_words(wa_w[1][:], wa_words[1])
         make_identity(nc, ident[:])
 
@@ -97,27 +104,19 @@ def tile_moe_dyl_none_kernel(
         waq_w = [sb("waq_w%d" % s, [P, B * H], U32) for s in range(2)]
         waq_rows = sb("waq_rows", [P, B * H], U8)
 
-        def block(m, width):
-            return slice(m * width, (m + 1) * width)
-
         gather(xq_w[0][:], x_w[0][:].bitcast(U32), idx, 0, SLOTS)
-        for pair in range(2):
-            gather(waq_rows[:, block(pair, 2 * H)], wa_s[:], idx2, pair * 2 * H, 2 * H)
-        for s in range(2):
+        gather(waq_rows[:], wa_s[:], idx2, 0, B * H)
+        for s, queue in enumerate((nc.gpsimd, nc.sync)):
             for r in range(4):
-                nc.sync.dma_start(
-                    waq_s[WA_ROW[s] + r : P : 32, :].bitcast(I32),
+                queue.dma_start(
+                    waq_s[s][WA_ROW[s] + r : P : 32, :].bitcast(I32),
                     waq_rows[64 * s + 4 * r : 64 * s + 64 : 16, :].bitcast(I32),
                 )
         load_words(wb_w[:], wb_words[0])
-        with nc.allow_non_contiguous_dma(reason="one gate value for each slot, slots on the partitions"):
-            nc.sync.dma_start(gate_col[:], gate[0, :].rearrange("(m p) -> p m", p=P))
+        nc.sync.dma_start(gate_sb[:], gate)
         gather(xq_w[1][:], x_w[1][:].bitcast(U32), idx, 0, SLOTS)
         gather(xq_s[:], x_s[:], idx, 0, SLOTS)
-        wbq_s = [sb("wbq_s0", [P, 2 * N], U8)]
-        gather(wbq_s[0][:], wb_s[:], idx3, 0, 2 * N)
-        for pair in range(2):
-            gather(waq_w[0][:, block(pair, 2 * H)], wa_w[0][:].bitcast(U32), idx2, pair * 2 * H, 2 * H)
+        gather(waq_w[0][:], wa_w[0][:].bitcast(U32), idx2, 0, B * H)
 
         result = [sb("result%d" % j, [P, T], F32) for j in range(2)]
         for j in range(2):
@@ -128,35 +127,32 @@ def tile_moe_dyl_none_kernel(
                        x_w[s], x_s, X_ROW[s], block(half, 512), s == 0, s == 1)
                 nc.scalar.copy(result[j][:, block(half, 512)], acc[:])
 
-        base_slots = sb("base_slots", [P, B, N], F32)
-        for pair in range(2):
-            acc = psum.tile([P, 2, N], F32, name="acc2", tag="sum", bufs=2)
-            for mb in range(2):
-                for s in range(2):
-                    mm(acc[:, mb, :], xq_w[s], xq_s, X_ROW[s], block(2 * pair + mb, P),
-                       w_w[:, s, :], w_s, W_ROW[s], slice(0, N), s == 0, s == 1)
-            nc.scalar.copy(base_slots[:, 2 * pair : 2 * pair + 2, :], acc[:])
+        base_slots = sb("base_slots", [P, 2, SLOTS], F32)
+        for j in range(2):
+            acc = psum.tile([P, 512], F32, name="acc2", tag=("turn", "y")[j], bufs=2)
+            for s in range(2):
+                mm(acc[:], w_w[:, s, :], w_s, W_ROW[s], block(j, P),
+                   xq_w[s], xq_s, X_ROW[s], slice(0, SLOTS), s == 0, s == 1)
+            nc.scalar.copy(base_slots[:, j, :], acc[:])
 
-        def h_pass(acc, m, s):
-            mm(acc[:], xq_w[s], xq_s, X_ROW[s], block(m, P), waq_w[s], waq_s, WA_ROW[s], block(m, H), s == 0, s == 1)
+        def h_pass(m, s):
+            mm(h_acc[m][:], xq_w[s], xq_s, X_ROW[s], block(m, P),
+               waq_w[s], waq_s[s], WA_ROW[s], block(m, H), s == 0, s == 1)
 
-        h_acc = []
-        for m in range(2):
-            acc = psum.tile([P, 512], F32, name="h_acc", tag="wide", bufs=2)
-            h_pass(acc, m, 0)
-            h_acc.append(acc)
+        h_acc = [psum.tile([P, H], F32, name="h_acc%d" % m) for m in range(B)]
+        for m in range(B):
+            h_pass(m, 0)
 
         for m in range(B):
             gather(waq_w[1][:, block(m, H)], wa_w[1][:].bitcast(U32), idx2, m * H, H)
+        wbq_s = [on_shared("wbq_s0", [P, 2 * N], U8, 4096)]
         wbq_w = [sb("wbq_w0", [P, 2 * N], U32)]
+        gather(wbq_s[0][:], wb_s[:], idx3, 0, 2 * N)
         gather(wbq_w[0][:], wb_w[:].bitcast(U32), idx3, 0, 2 * N)
 
-        grouped = [
-            shared.tile([P, 2, P, 2], F32, name="grouped0", align_bytes=64, offset=0),
-            sb("grouped1", [P, 2, P, 2], F32),
-        ]
-
-        def turn(m):
+        grouped = [on_shared("grouped0", [P, 2, P, 2], F32, 0), sb("grouped1", [P, 2, P, 2], F32)]
+        for m in range(B):
+            h_pass(m, 1)
             h_bf = sb("h_bf%d" % m, [P, 2, P, 2], BF16)
             nc.scalar.copy(h_bf[:], h_acc[m][:].rearrange("s (p u e) -> s u p e", u=2, e=2))
             h_words = h_bf[:].rearrange("s u p e -> s (u p e)").bitcast(F32)
@@ -165,23 +161,7 @@ def tile_moe_dyl_none_kernel(
                 nc.tensor.transpose(turned[:, u, :], h_words[:, block(u, P)], ident[:])
             nc.scalar.copy(grouped[m // 2][:, m % 2, :, :], turned[:].rearrange("p u s -> p s u"))
 
-        h_pass(h_acc[0], 0, 1)
-        h_pass(h_acc[1], 1, 1)
-        for m in range(B):
-            turn(m)
-            if m + 2 < B:
-                acc = psum.tile([P, 512], F32, name="h_acc", tag="wide", bufs=2)
-                for s in range(2):
-                    h_pass(acc, m + 2, s)
-                h_acc.append(acc)
-
-        values = sb("values", [P, 2, SLOTS], F32)
-
-        def scatter(j, first, count):
-            nc.vector.tensor_copy(
-                result[j][:].indirect(idx[:, first // 16 : (first + count) // 16]), values[:, j, first : first + count]
-            )
-
+        y_acc = []
         for pair in range(2):
             hq_w = sb("hq_w%d" % pair, [P, 2 * P], U32)
             hq_s = sb("hq_s%d" % pair, [P, 2 * P], U8)
@@ -191,27 +171,26 @@ def tile_moe_dyl_none_kernel(
                 in_=grouped[pair][:].rearrange("p b s u -> p (b s u)").bitcast(BF16),
             )
             if pair == 0:
-                wbq_s.append(shared.tile([P, 2 * N], U8, name="wbq_s1", align_bytes=64, offset=0))
-                wbq_w.append(shared.tile([P, 2 * N], U32, name="wbq_w1", align_bytes=64, offset=2 * N))
+                wbq_s.append(on_shared("wbq_s1", [P, 2 * N], U8, 0))
+                wbq_w.append(on_shared("wbq_w1", [P, 2 * N], U32, 2 * N))
                 gather(wbq_s[1][:], wb_s[:], idx3, 2 * N, 2 * N)
                 gather(wbq_w[1][:], wb_w[:].bitcast(U32), idx3, 2 * N, 2 * N)
+            acc = psum.tile([P, 2, 2 * P], F32, name="y_acc", tag="y", bufs=2)
             for mb in range(2):
-                m = 2 * pair + mb
-                y_acc = psum.tile([P, N], F32, name="y_acc", tag="y", bufs=2)
-                mm(y_acc[:], hq_w, hq_s, 0, block(mb, P), wbq_w[pair], wbq_s[pair], WB_ROW, block(mb, N), True, True)
-                gated = sb("gated%d" % m, [P, N], F32)
-                nc.scalar.activation(gated[:], y_acc[:], COPY, scale=gate_col[:, m : m + 1])
-                total = psum.tile([P, 2, P], F32, name="total", tag="sum", bufs=2)
                 for j in range(2):
-                    nc.tensor.matmul(total[:, j, :], base_slots[:, m, block(j, P)], ident[:],
-                                     start=True, stop=False, is_transpose=True)
-                    nc.tensor.matmul(total[:, j, :], gated[:, block(j, P)], ident[:],
-                                     start=False, stop=True, is_transpose=True)
-                nc.scalar.copy(values[:, :, block(m, P)], total[:])
+                    mm(acc[:, j, block(mb, P)], wbq_w[pair], wbq_s[pair], WB_ROW, block(2 * mb + j, P),
+                       hq_w, hq_s, 0, block(mb, P), True, True)
+            y_acc.append(acc)
 
-        for m in range(2):
+        for pair in range(2):
+            cols = block(pair, 2 * P)
+            gated = sb("gated%d" % pair, [P, 2, 2 * P], F32)
+            nc.vector.tensor_tensor(
+                gated[:], y_acc[pair][:], gate_sb[:, cols].unsqueeze(1).to_broadcast([P, 2, 2 * P]), MULT
+            )
             for j in range(2):
-                scatter(j, m * P, P)
-        for j in range(2):
-            scatter(j, 2 * P, 2 * P)
-            nc.sync.dma_start(out[block(j, P), :], result[j][:])
+                nc.vector.tensor_tensor(
+                    result[j][:].indirect(idx[:, block(pair, 16)]), gated[:, j, :], base_slots[:, j, cols], ADD
+                )
+                if pair == 1:
+                    nc.sync.dma_start(out[block(j, P), :], result[j][:])

@@ -30,7 +30,6 @@ def tile_moe_dyl_none_kernel(
     nc = tc.nc
     with ExitStack() as ctx:
         keep = ctx.enter_context(tc.tile_pool(name="keep", bufs=1))
-        shared = ctx.enter_context(tc.tile_pool(name="shared", bufs=1))
         psum = ctx.enter_context(tc.psum_pool(name="psum", bufs=1))
 
         def sb(name, shape, dtype):
@@ -64,59 +63,52 @@ def tile_moe_dyl_none_kernel(
         def block(m, width):
             return slice(m * width, (m + 1) * width)
 
-        def on_shared(name, shape, dtype, offset):
-            return shared.tile(shape, dtype, name=name, align_bytes=64, offset=offset)
-
         idx = sb("idx", [P, SLOTS // 16], U16)
         idx2 = sb("idx2", [P, B * H // 16], U16)
         idx3 = sb("idx3", [P, B * N // 16], U16)
         x_w = [sb("x_w%d" % s, [P, T], I32) for s in range(2)]
         w_w = sb("w_w", [P, 2, N], I32)
-        wa_w = [sb("wa_w0", [P, E * H], I32), on_shared("wa_w1", [P, E * H], I32, 4096)]
+        wa_w = [sb("wa_w%d" % s, [P, E * H], I32) for s in range(2)]
         wb_w = sb("wb_w", [P, E * N], I32)
         x_s = sb("x_s", [P, T], U8)
         w_s = sb("w_s", [P, N], U8)
         wa_s = sb("wa_s", [P, E * H], U8)
         wb_s = sb("wb_s", [P, E * N], U8)
-        waq_s = [sb("waq_s%d" % s, [P, B * H], U8) for s in range(2)]
         gate_sb = sb("gate_sb", [P, SLOTS], F32)
         ident = sb("ident", [P, P], F32)
 
-        for plane in (wa_s, w_s, x_s, wb_s, waq_s[0], waq_s[1]):
+        for plane in (wa_s, x_s, w_s, wb_s):
             nc.vector.memset(plane[:].bitcast(I32), 0)
 
         nc.sync.dma_start(idx[:], offs)
         load_words(x_w[0][:], x_words[0])
         nc.sync.dma_start(idx2[:], offs2)
-        nc.sync.dma_start(wa_s[0:P:4, :].bitcast(I32), wa_scales.rearrange("s b c -> (s b) c").bitcast(I32))
-        load_scales(nc.scalar, w_s, w_scales, W_ROW[0])
-        load_scales(nc.gpsimd, wb_s, wb_scales, WB_ROW)
+        load_scales(nc.scalar, x_s, x_scales, X_ROW[0])
+        load_scales(nc.gpsimd, wa_s, wa_scales, WA_ROW[0])
         load_words(x_w[1][:], x_words[1])
-        load_scales(nc.sync, x_s, x_scales, X_ROW[0])
         nc.sync.dma_start(w_w[:], w_words.rearrange("s p n t -> p s (n t)").bitcast(I32))
         nc.sync.dma_start(idx3[:], offs3)
         load_words(wa_w[0][:], wa_words[0])
+        load_scales(nc.scalar, w_s, w_scales, W_ROW[0])
+        load_scales(nc.gpsimd, wb_s, wb_scales, WB_ROW)
         load_words(wa_w[1][:], wa_words[1])
+        load_words(wb_w[:], wb_words[0])
+        nc.sync.dma_start(gate_sb[:], gate)
         make_identity(nc, ident[:])
 
         xq_w = [sb("xq_w%d" % s, [P, SLOTS], U32) for s in range(2)]
         xq_s = sb("xq_s", [P, SLOTS], U8)
         waq_w = [sb("waq_w%d" % s, [P, B * H], U32) for s in range(2)]
-        waq_rows = sb("waq_rows", [P, B * H], U8)
+        waq_s = sb("waq_s", [P, B * H], U8)
+        wbq_w = sb("wbq_w", [P, B * N], U32)
+        wbq_s = sb("wbq_s", [P, B * N], U8)
 
-        gather(xq_w[0][:], x_w[0][:].bitcast(U32), idx, 0, SLOTS)
-        gather(waq_rows[:], wa_s[:], idx2, 0, B * H)
-        for s, queue in enumerate((nc.gpsimd, nc.sync)):
-            for r in range(4):
-                queue.dma_start(
-                    waq_s[s][WA_ROW[s] + r : P : 32, :].bitcast(I32),
-                    waq_rows[64 * s + 4 * r : 64 * s + 64 : 16, :].bitcast(I32),
-                )
-        load_words(wb_w[:], wb_words[0])
-        nc.sync.dma_start(gate_sb[:], gate)
-        gather(xq_w[1][:], x_w[1][:].bitcast(U32), idx, 0, SLOTS)
+        for s in range(2):
+            gather(xq_w[s][:], x_w[s][:].bitcast(U32), idx, 0, SLOTS)
         gather(xq_s[:], x_s[:], idx, 0, SLOTS)
+        gather(waq_s[:], wa_s[:], idx2, 0, B * H)
         gather(waq_w[0][:], wa_w[0][:].bitcast(U32), idx2, 0, B * H)
+        gather(wbq_s[:], wb_s[:], idx3, 0, B * N)
 
         result = [sb("result%d" % j, [P, T], F32) for j in range(2)]
         for j in range(2):
@@ -137,7 +129,7 @@ def tile_moe_dyl_none_kernel(
 
         def h_pass(m, s):
             mm(h_acc[m][:], xq_w[s], xq_s, X_ROW[s], block(m, P),
-               waq_w[s], waq_s[s], WA_ROW[s], block(m, H), s == 0, s == 1)
+               waq_w[s], waq_s, WA_ROW[s], block(m, H), s == 0, s == 1)
 
         h_acc = [psum.tile([P, H], F32, name="h_acc%d" % m) for m in range(B)]
         for m in range(B):
@@ -145,21 +137,23 @@ def tile_moe_dyl_none_kernel(
 
         for m in range(B):
             gather(waq_w[1][:, block(m, H)], wa_w[1][:].bitcast(U32), idx2, m * H, H)
-        wbq_s = [on_shared("wbq_s0", [P, 2 * N], U8, 4096)]
-        wbq_w = [sb("wbq_w0", [P, 2 * N], U32)]
-        gather(wbq_s[0][:], wb_s[:], idx3, 0, 2 * N)
-        gather(wbq_w[0][:], wb_w[:].bitcast(U32), idx3, 0, 2 * N)
+        for pair in range(2):
+            gather(wbq_w[:, block(pair, 2 * N)], wb_w[:].bitcast(U32), idx3, pair * 2 * N, 2 * N)
 
-        grouped = [on_shared("grouped0", [P, 2, P, 2], F32, 0), sb("grouped1", [P, 2, P, 2], F32)]
-        for m in range(B):
-            h_pass(m, 1)
-            h_bf = sb("h_bf%d" % m, [P, 2, P, 2], BF16)
-            nc.scalar.copy(h_bf[:], h_acc[m][:].rearrange("s (p u e) -> s u p e", u=2, e=2))
-            h_words = h_bf[:].rearrange("s u p e -> s (u p e)").bitcast(F32)
-            turned = psum.tile([P, 2, P], F32, name="turned", tag="turn", bufs=2)
-            for u in range(2):
-                nc.tensor.transpose(turned[:, u, :], h_words[:, block(u, P)], ident[:])
-            nc.scalar.copy(grouped[m // 2][:, m % 2, :, :], turned[:].rearrange("p u s -> p s u"))
+        grouped = []
+        for pair in range(2):
+            turned = psum.tile([P, 2, 2, P], F32, name="turned", tag="turn", bufs=2)
+            for mb in range(2):
+                m = 2 * pair + mb
+                h_pass(m, 1)
+                h_bf = sb("h_bf%d" % m, [P, 2, P, 2], BF16)
+                nc.scalar.copy(h_bf[:], h_acc[m][:].rearrange("s (p u e) -> s u p e", u=2, e=2))
+                h_words = h_bf[:].rearrange("s u p e -> s (u p e)").bitcast(F32)
+                for u in range(2):
+                    nc.tensor.transpose(turned[:, mb, u, :], h_words[:, block(u, P)], ident[:])
+            words = sb("grouped%d" % pair, [P, 2, P, 2], F32)
+            nc.scalar.copy(words[:], turned[:].rearrange("p b u s -> p b s u"))
+            grouped.append(words)
 
         y_acc = []
         for pair in range(2):
@@ -170,15 +164,10 @@ def tile_moe_dyl_none_kernel(
                 scales=hq_s[:],
                 in_=grouped[pair][:].rearrange("p b s u -> p (b s u)").bitcast(BF16),
             )
-            if pair == 0:
-                wbq_s.append(on_shared("wbq_s1", [P, 2 * N], U8, 0))
-                wbq_w.append(on_shared("wbq_w1", [P, 2 * N], U32, 2 * N))
-                gather(wbq_s[1][:], wb_s[:], idx3, 2 * N, 2 * N)
-                gather(wbq_w[1][:], wb_w[:].bitcast(U32), idx3, 2 * N, 2 * N)
             acc = psum.tile([P, 2, 2 * P], F32, name="y_acc", tag="y", bufs=2)
             for mb in range(2):
                 for j in range(2):
-                    mm(acc[:, j, block(mb, P)], wbq_w[pair], wbq_s[pair], WB_ROW, block(2 * mb + j, P),
+                    mm(acc[:, j, block(mb, P)], wbq_w, wbq_s, WB_ROW, block(4 * pair + 2 * mb + j, P),
                        hq_w, hq_s, 0, block(mb, P), True, True)
             y_acc.append(acc)
 

@@ -6,6 +6,7 @@ from concourse.masks import make_identity
 K, T, E, B, H, N = 1024, 1024, 8, 4, 512, 256
 P = 128
 SLOTS = P * B
+BANK = 512
 FLOPS = 2 * K * N * T + 2 * K * H * SLOTS + 2 * H * N * SLOTS
 
 F32 = mybir.dt.float32
@@ -23,6 +24,8 @@ W_ROW = (0, 4)
 WA_ROW = (8, 12)
 WB_ROW = 8
 
+MOVES_ON_SYNC = 5
+
 
 def tile_moe_dyl_none_kernel(
     tc, x_words, x_scales, w_words, w_scales, wa_words, wa_scales, wb_words, wb_scales, gate, offs, offs2, offs3, out
@@ -30,38 +33,42 @@ def tile_moe_dyl_none_kernel(
     nc = tc.nc
     with ExitStack() as ctx:
         keep = ctx.enter_context(tc.tile_pool(name="keep", bufs=1))
+        shared = ctx.enter_context(tc.tile_pool(name="shared", bufs=1))
         psum = ctx.enter_context(tc.psum_pool(name="psum", bufs=1))
 
         def sb(name, shape, dtype):
             return keep.tile(shape, dtype, name=name, align_bytes=64)
 
+        def on_shared(name, shape, dtype, offset):
+            return shared.tile(shape, dtype, name=name, align_bytes=64, offset=offset)
+
+        def part(index, width):
+            return slice(index * width, (index + 1) * width)
+
         def load_words(tile, words):
             nc.sync.dma_start(tile, words.rearrange("p n t -> p (n t)").bitcast(I32))
 
-        def load_scales(queue, plane, scales, first_row):
+        def load_scales(queue, tile, scales, first_row):
             rows = 4 * scales.shape[0]
             for q in range(4):
                 queue.dma_start(
-                    plane[32 * q + first_row : 32 * q + first_row + rows, :].bitcast(I32),
+                    tile[32 * q + first_row : 32 * q + first_row + rows, :].bitcast(I32),
                     scales[:, 4 * q : 4 * q + 4, :].bitcast(I32),
                 )
 
         def gather(dst, window, offsets, first, count):
             nc.vector.tensor_copy(dst, window.indirect(offsets[:, first // 16 : (first + count) // 16]))
 
-        def mm(acc, lhs, lhs_plane, lhs_row, lhs_cols, rhs, rhs_plane, rhs_row, rhs_cols, start, stop):
+        def mm(acc, lhs, lhs_scales, lhs_row, lhs_cols, rhs, rhs_scales, rhs_row, rhs_cols, start, stop):
             nc.tensor.matmul_mx(
                 out=acc,
                 lhsT=lhs[:, lhs_cols].bitcast(FP8X4),
-                lhsT_scale=lhs_plane[lhs_row:P, lhs_cols],
+                lhsT_scale=lhs_scales[lhs_row:P, lhs_cols],
                 rhs=rhs[:, rhs_cols].bitcast(FP8X4),
-                rhs_scale=rhs_plane[rhs_row:P, rhs_cols],
+                rhs_scale=rhs_scales[rhs_row:P, rhs_cols],
                 start=start,
                 stop=stop,
             )
-
-        def block(m, width):
-            return slice(m * width, (m + 1) * width)
 
         idx = sb("idx", [P, SLOTS // 16], U16)
         idx2 = sb("idx2", [P, B * H // 16], U16)
@@ -69,76 +76,89 @@ def tile_moe_dyl_none_kernel(
         x_w = [sb("x_w%d" % s, [P, T], I32) for s in range(2)]
         w_w = sb("w_w", [P, 2, N], I32)
         wa_w = [sb("wa_w%d" % s, [P, E * H], I32) for s in range(2)]
-        wb_w = sb("wb_w", [P, E * N], I32)
         x_s = sb("x_s", [P, T], U8)
         w_s = sb("w_s", [P, N], U8)
-        wa_s = sb("wa_s", [P, E * H], U8)
+        wb_bytes = 4 * E * N
+        wa_s = on_shared("wa_s", [P, E * H], U8, wb_bytes - E * H // 2)
         wb_s = sb("wb_s", [P, E * N], U8)
-        gate_sb = sb("gate_sb", [P, SLOTS], F32)
+        waq_s = [sb("waq_s%d" % s, [P, B * H], U8) for s in range(2)]
         ident = sb("ident", [P, P], F32)
 
-        for plane in (wa_s, x_s, w_s, wb_s):
-            nc.vector.memset(plane[:].bitcast(I32), 0)
+        for tile in (x_s, wa_s, w_s, wb_s, waq_s[0], waq_s[1]):
+            nc.vector.memset(tile[:].bitcast(I32), 0)
 
         nc.sync.dma_start(idx[:], offs)
         load_words(x_w[0][:], x_words[0])
         nc.sync.dma_start(idx2[:], offs2)
-        load_scales(nc.scalar, x_s, x_scales, X_ROW[0])
-        load_scales(nc.gpsimd, wa_s, wa_scales, WA_ROW[0])
-        load_words(x_w[1][:], x_words[1])
-        nc.sync.dma_start(w_w[:], w_words.rearrange("s p n t -> p s (n t)").bitcast(I32))
-        nc.sync.dma_start(idx3[:], offs3)
-        load_words(wa_w[0][:], wa_words[0])
+        nc.sync.dma_start(wa_s[0:P:4, :].bitcast(I32), wa_scales.rearrange("s b c -> (s b) c").bitcast(I32))
+        load_scales(nc.gpsimd, x_s, x_scales, X_ROW[0])
         load_scales(nc.scalar, w_s, w_scales, W_ROW[0])
         load_scales(nc.gpsimd, wb_s, wb_scales, WB_ROW)
+        load_words(x_w[1][:], x_words[1])
+        nc.sync.dma_start(w_w[:], w_words.rearrange("s p n t -> p s (n t)").bitcast(I32))
+        load_words(wa_w[0][:], wa_words[0])
         load_words(wa_w[1][:], wa_words[1])
-        load_words(wb_w[:], wb_words[0])
-        nc.sync.dma_start(gate_sb[:], gate)
+        nc.sync.dma_start(idx3[:], offs3)
         make_identity(nc, ident[:])
 
         xq_w = [sb("xq_w%d" % s, [P, SLOTS], U32) for s in range(2)]
         xq_s = sb("xq_s", [P, SLOTS], U8)
         waq_w = [sb("waq_w%d" % s, [P, B * H], U32) for s in range(2)]
-        waq_s = sb("waq_s", [P, B * H], U8)
-        wbq_w = sb("wbq_w", [P, B * N], U32)
+        waq_rows = sb("waq_rows", [P, B * H], U8)
         wbq_s = sb("wbq_s", [P, B * N], U8)
+        wbq_w = sb("wbq_w", [P, B * N], U32)
+
+        gather(xq_w[0][:], x_w[0][:].bitcast(U32), idx, 0, SLOTS)
+        gather(waq_rows[:], wa_s[:], idx2, 0, B * H)
 
         for s in range(2):
-            gather(xq_w[s][:], x_w[s][:].bitcast(U32), idx, 0, SLOTS)
+            for r in range(4):
+                queue = nc.sync if 4 * s + r < MOVES_ON_SYNC else nc.gpsimd
+                queue.dma_start(
+                    waq_s[s][WA_ROW[s] + r : P : 32, :].bitcast(I32),
+                    waq_rows[64 * s + 4 * r : 64 * s + 64 : 16, :].bitcast(I32),
+                )
+
+        wb_w = on_shared("wb_w", [P, E * N], I32, 0)
+        gate_sb = on_shared("gate_sb", [P, SLOTS], F32, wb_bytes)
+        load_words(wb_w[:], wb_words[0])
+        nc.sync.dma_start(gate_sb[:], gate)
+
+        gather(xq_w[1][:], x_w[1][:].bitcast(U32), idx, 0, SLOTS)
         gather(xq_s[:], x_s[:], idx, 0, SLOTS)
-        gather(waq_s[:], wa_s[:], idx2, 0, B * H)
         gather(waq_w[0][:], wa_w[0][:].bitcast(U32), idx2, 0, B * H)
         gather(wbq_s[:], wb_s[:], idx3, 0, B * N)
 
+        late_banks = ("turn", "y")
         result = [sb("result%d" % j, [P, T], F32) for j in range(2)]
         for j in range(2):
             for half in range(2):
-                acc = psum.tile([P, 512], F32, name="acc", tag=("turn", "y")[half], bufs=2)
+                acc = psum.tile([P, BANK], F32, name="base_acc", tag=late_banks[half], bufs=2)
                 for s in range(2):
-                    mm(acc[:], w_w[:, s, :], w_s, W_ROW[s], block(j, P),
-                       x_w[s], x_s, X_ROW[s], block(half, 512), s == 0, s == 1)
-                nc.scalar.copy(result[j][:, block(half, 512)], acc[:])
+                    mm(acc[:], w_w[:, s, :], w_s, W_ROW[s], part(j, P),
+                       x_w[s], x_s, X_ROW[s], part(half, BANK), s == 0, s == 1)
+                nc.scalar.copy(result[j][:, part(half, BANK)], acc[:])
 
         base_slots = sb("base_slots", [P, 2, SLOTS], F32)
         for j in range(2):
-            acc = psum.tile([P, 512], F32, name="acc2", tag=("turn", "y")[j], bufs=2)
+            acc = psum.tile([P, SLOTS], F32, name="slot_acc", tag=late_banks[j], bufs=2)
             for s in range(2):
-                mm(acc[:], w_w[:, s, :], w_s, W_ROW[s], block(j, P),
+                mm(acc[:], w_w[:, s, :], w_s, W_ROW[s], part(j, P),
                    xq_w[s], xq_s, X_ROW[s], slice(0, SLOTS), s == 0, s == 1)
             nc.scalar.copy(base_slots[:, j, :], acc[:])
 
         def h_pass(m, s):
-            mm(h_acc[m][:], xq_w[s], xq_s, X_ROW[s], block(m, P),
-               waq_w[s], waq_s, WA_ROW[s], block(m, H), s == 0, s == 1)
+            mm(h_acc[m][:], xq_w[s], xq_s, X_ROW[s], part(m, P),
+               waq_w[s], waq_s[s], WA_ROW[s], part(m, H), s == 0, s == 1)
 
         h_acc = [psum.tile([P, H], F32, name="h_acc%d" % m) for m in range(B)]
         for m in range(B):
             h_pass(m, 0)
 
         for m in range(B):
-            gather(waq_w[1][:, block(m, H)], wa_w[1][:].bitcast(U32), idx2, m * H, H)
+            gather(waq_w[1][:, part(m, H)], wa_w[1][:].bitcast(U32), idx2, m * H, H)
         for pair in range(2):
-            gather(wbq_w[:, block(pair, 2 * N)], wb_w[:].bitcast(U32), idx3, pair * 2 * N, 2 * N)
+            gather(wbq_w[:, part(pair, 2 * N)], wb_w[:].bitcast(U32), idx3, pair * 2 * N, 2 * N)
 
         grouped = []
         for pair in range(2):
@@ -150,7 +170,7 @@ def tile_moe_dyl_none_kernel(
                 nc.scalar.copy(h_bf[:], h_acc[m][:].rearrange("s (p u e) -> s u p e", u=2, e=2))
                 h_words = h_bf[:].rearrange("s u p e -> s (u p e)").bitcast(F32)
                 for u in range(2):
-                    nc.tensor.transpose(turned[:, mb, u, :], h_words[:, block(u, P)], ident[:])
+                    nc.tensor.transpose(turned[:, mb, u, :], h_words[:, part(u, P)], ident[:])
             words = sb("grouped%d" % pair, [P, 2, P, 2], F32)
             nc.scalar.copy(words[:], turned[:].rearrange("p b u s -> p b s u"))
             grouped.append(words)
@@ -167,19 +187,19 @@ def tile_moe_dyl_none_kernel(
             acc = psum.tile([P, 2, 2 * P], F32, name="y_acc", tag="y", bufs=2)
             for mb in range(2):
                 for j in range(2):
-                    mm(acc[:, j, block(mb, P)], wbq_w, wbq_s, WB_ROW, block(4 * pair + 2 * mb + j, P),
-                       hq_w, hq_s, 0, block(mb, P), True, True)
+                    mm(acc[:, j, part(mb, P)], wbq_w, wbq_s, WB_ROW, part(4 * pair + 2 * mb + j, P),
+                       hq_w, hq_s, 0, part(mb, P), True, True)
             y_acc.append(acc)
 
         for pair in range(2):
-            cols = block(pair, 2 * P)
+            cols = part(pair, 2 * P)
             gated = sb("gated%d" % pair, [P, 2, 2 * P], F32)
             nc.vector.tensor_tensor(
                 gated[:], y_acc[pair][:], gate_sb[:, cols].unsqueeze(1).to_broadcast([P, 2, 2 * P]), MULT
             )
             for j in range(2):
                 nc.vector.tensor_tensor(
-                    result[j][:].indirect(idx[:, block(pair, 16)]), gated[:, j, :], base_slots[:, j, cols], ADD
+                    result[j][:].indirect(idx[:, part(pair, 2 * P // 16)]), gated[:, j, :], base_slots[:, j, cols], ADD
                 )
                 if pair == 1:
-                    nc.sync.dma_start(out[block(j, P), :], result[j][:])
+                    nc.sync.dma_start(out[part(j, P), :], result[j][:])

@@ -24,7 +24,7 @@ W_ROW = (0, 4)
 WA_ROW = (8, 12)
 WB_ROW = 8
 
-MOVES_ON_SYNC = 5
+WA_RAW = 96
 
 
 def tile_moe_dyl_none_kernel(
@@ -33,14 +33,10 @@ def tile_moe_dyl_none_kernel(
     nc = tc.nc
     with ExitStack() as ctx:
         keep = ctx.enter_context(tc.tile_pool(name="keep", bufs=1))
-        shared = ctx.enter_context(tc.tile_pool(name="shared", bufs=1))
         psum = ctx.enter_context(tc.psum_pool(name="psum", bufs=1))
 
         def sb(name, shape, dtype):
             return keep.tile(shape, dtype, name=name, align_bytes=64)
-
-        def on_shared(name, shape, dtype, offset):
-            return shared.tile(shape, dtype, name=name, align_bytes=64, offset=offset)
 
         def part(index, width):
             return slice(index * width, (index + 1) * width)
@@ -73,61 +69,57 @@ def tile_moe_dyl_none_kernel(
         idx = sb("idx", [P, SLOTS // 16], U16)
         idx2 = sb("idx2", [P, B * H // 16], U16)
         idx3 = sb("idx3", [P, B * N // 16], U16)
-        x_w = [sb("x_w%d" % s, [P, T], I32) for s in range(2)]
+        x_both = sb("x_w", [P, 2, T], I32)
+        x_w = [x_both[:, s, :] for s in range(2)]
         w_w = sb("w_w", [P, 2, N], I32)
-        wa_w = [sb("wa_w%d" % s, [P, E * H], I32) for s in range(2)]
         x_s = sb("x_s", [P, T], U8)
         w_s = sb("w_s", [P, N], U8)
-        wb_bytes = 4 * E * N
-        wa_s = on_shared("wa_s", [P, E * H], U8, wb_bytes - E * H // 2)
+        wa_s = sb("wa_s", [P, E * H], U8)
         wb_s = sb("wb_s", [P, E * N], U8)
-        waq_s = [sb("waq_s%d" % s, [P, B * H], U8) for s in range(2)]
+        waq_s = sb("waq_s", [P, B * H], U8)
         ident = sb("ident", [P, P], F32)
 
-        for tile in (x_s, wa_s, w_s, wb_s, waq_s[0], waq_s[1]):
-            nc.vector.memset(tile[:].bitcast(I32), 0)
+        for tile in (x_s[:], w_s[:], wa_s[0:WA_RAW, :], wb_s[:], waq_s[:]):
+            nc.vector.memset(tile.bitcast(I32), 0)
 
-        nc.sync.dma_start(idx[:], offs)
-        load_words(x_w[0][:], x_words[0])
         nc.sync.dma_start(idx2[:], offs2)
-        nc.sync.dma_start(wa_s[0:P:4, :].bitcast(I32), wa_scales.rearrange("s b c -> (s b) c").bitcast(I32))
-        load_scales(nc.gpsimd, x_s, x_scales, X_ROW[0])
+        nc.sync.dma_start(wa_s[WA_RAW:P, :].bitcast(I32), wa_scales.rearrange("s b c -> (s b) c").bitcast(I32))
+        nc.sync.dma_start(idx[:], offs)
+        load_scales(nc.scalar, x_s, x_scales, X_ROW[0])
+        nc.sync.dma_start(x_both[:], x_words.rearrange("s p n t -> p s (n t)").bitcast(I32))
         load_scales(nc.scalar, w_s, w_scales, W_ROW[0])
-        load_scales(nc.gpsimd, wb_s, wb_scales, WB_ROW)
-        load_words(x_w[1][:], x_words[1])
         nc.sync.dma_start(w_w[:], w_words.rearrange("s p n t -> p s (n t)").bitcast(I32))
-        load_words(wa_w[0][:], wa_words[0])
-        load_words(wa_w[1][:], wa_words[1])
+        wa_w = [sb("wa_w%d" % s, [P, E * H], I32) for s in range(2)]
+        for s in range(2):
+            load_words(wa_w[s][:], wa_words[s])
         nc.sync.dma_start(idx3[:], offs3)
+        wb_w = sb("wb_w", [P, E * N], I32)
+        gate_sb = sb("gate_sb", [P, SLOTS], F32)
+        load_words(wb_w[:], wb_words[0])
+        nc.sync.dma_start(gate_sb[:], gate)
+        load_scales(nc.gpsimd, wb_s, wb_scales, WB_ROW)
         make_identity(nc, ident[:])
 
         xq_w = [sb("xq_w%d" % s, [P, SLOTS], U32) for s in range(2)]
         xq_s = sb("xq_s", [P, SLOTS], U8)
         waq_w = [sb("waq_w%d" % s, [P, B * H], U32) for s in range(2)]
         waq_rows = sb("waq_rows", [P, B * H], U8)
-        wbq_s = sb("wbq_s", [P, B * N], U8)
         wbq_w = sb("wbq_w", [P, B * N], U32)
 
-        gather(xq_w[0][:], x_w[0][:].bitcast(U32), idx, 0, SLOTS)
         gather(waq_rows[:], wa_s[:], idx2, 0, B * H)
 
         for s in range(2):
             for r in range(4):
-                queue = nc.sync if 4 * s + r < MOVES_ON_SYNC else nc.gpsimd
-                queue.dma_start(
-                    waq_s[s][WA_ROW[s] + r : P : 32, :].bitcast(I32),
-                    waq_rows[64 * s + 4 * r : 64 * s + 64 : 16, :].bitcast(I32),
+                first = WA_RAW + 16 * s
+                (nc.scalar, nc.gpsimd)[s].dma_start(
+                    waq_s[WA_ROW[s] + r : P : 32, :].bitcast(I32),
+                    waq_rows[first + r : first + 16 : 4, :].bitcast(I32),
                 )
 
-        wb_w = on_shared("wb_w", [P, E * N], I32, 0)
-        gate_sb = on_shared("gate_sb", [P, SLOTS], F32, wb_bytes)
-        load_words(wb_w[:], wb_words[0])
-        nc.sync.dma_start(gate_sb[:], gate)
-
-        gather(xq_w[1][:], x_w[1][:].bitcast(U32), idx, 0, SLOTS)
         gather(xq_s[:], x_s[:], idx, 0, SLOTS)
+        for s in range(2):
+            gather(xq_w[s][:], x_w[s].bitcast(U32), idx, 0, SLOTS)
         gather(waq_w[0][:], wa_w[0][:].bitcast(U32), idx2, 0, B * H)
-        gather(wbq_s[:], wb_s[:], idx3, 0, B * N)
 
         late_banks = ("turn", "y")
         result = [sb("result%d" % j, [P, T], F32) for j in range(2)]
@@ -149,7 +141,7 @@ def tile_moe_dyl_none_kernel(
 
         def h_pass(m, s):
             mm(h_acc[m][:], xq_w[s], xq_s, X_ROW[s], part(m, P),
-               waq_w[s], waq_s[s], WA_ROW[s], part(m, H), s == 0, s == 1)
+               waq_w[s], waq_s, WA_ROW[s], part(m, H), s == 0, s == 1)
 
         h_acc = [psum.tile([P, H], F32, name="h_acc%d" % m) for m in range(B)]
         for m in range(B):
@@ -157,6 +149,8 @@ def tile_moe_dyl_none_kernel(
 
         for m in range(B):
             gather(waq_w[1][:, part(m, H)], wa_w[1][:].bitcast(U32), idx2, m * H, H)
+        wbq_s = sb("wbq_s", [P, B * N], U8)
+        gather(wbq_s[:], wb_s[:], idx3, 0, B * N)
         for pair in range(2):
             gather(wbq_w[:, part(pair, 2 * N)], wb_w[:].bitcast(U32), idx3, pair * 2 * N, 2 * N)
 

@@ -18,6 +18,7 @@ U8 = mybir.dt.uint8
 FP8X4 = mybir.dt.float8_e4m3fn_x4
 MULT = mybir.AluOpType.mult
 ADD = mybir.AluOpType.add
+COPY = mybir.ActivationFunctionType.Copy
 
 X_ROW = (0, 4)
 W_ROW = (0, 4)
@@ -79,11 +80,11 @@ def tile_moe_dyl_none_kernel(
         waq_s = sb("waq_s", [P, B * H], U8)
         ident = sb("ident", [P, P], F32)
 
-        for tile in (x_s[:], w_s[:], wa_s[0:WA_RAW, :], wb_s[:], waq_s[:]):
+        for tile in (x_s[:], w_s[:], wa_s[0:WA_RAW, :], waq_s[:], wb_s[:]):
             nc.vector.memset(tile.bitcast(I32), 0)
 
-        nc.sync.dma_start(idx2[:], offs2)
         nc.sync.dma_start(wa_s[WA_RAW:P, :].bitcast(I32), wa_scales.rearrange("s b c -> (s b) c").bitcast(I32))
+        nc.sync.dma_start(idx2[:], offs2)
         nc.sync.dma_start(idx[:], offs)
         load_scales(nc.scalar, x_s, x_scales, X_ROW[0])
         nc.sync.dma_start(x_both[:], x_words.rearrange("s p n t -> p s (n t)").bitcast(I32))
@@ -94,9 +95,12 @@ def tile_moe_dyl_none_kernel(
             load_words(wa_w[s][:], wa_words[s])
         nc.sync.dma_start(idx3[:], offs3)
         wb_w = sb("wb_w", [P, E * N], I32)
-        gate_sb = sb("gate_sb", [P, SLOTS], F32)
+        gate_rows = sb("gate_rows", [P, 2 * P], F32)
+        gate_col = sb("gate_col", [P, 2], F32)
         load_words(wb_w[:], wb_words[0])
-        nc.sync.dma_start(gate_sb[:], gate)
+        nc.sync.dma_start(gate_rows[:], gate[:, 0 : 2 * P])
+        with nc.allow_non_contiguous_dma(reason="one gate value a partition and block"):
+            nc.sync.dma_start(gate_col[:], gate[0, 2 * P : SLOTS].rearrange("(b p) -> p b", p=P))
         load_scales(nc.gpsimd, wb_s, wb_scales, WB_ROW)
         make_identity(nc, ident[:])
 
@@ -104,7 +108,6 @@ def tile_moe_dyl_none_kernel(
         xq_s = sb("xq_s", [P, SLOTS], U8)
         waq_w = [sb("waq_w%d" % s, [P, B * H], U32) for s in range(2)]
         waq_rows = sb("waq_rows", [P, B * H], U8)
-        wbq_w = sb("wbq_w", [P, B * N], U32)
 
         gather(waq_rows[:], wa_s[:], idx2, 0, B * H)
 
@@ -151,8 +154,8 @@ def tile_moe_dyl_none_kernel(
             gather(waq_w[1][:, part(m, H)], wa_w[1][:].bitcast(U32), idx2, m * H, H)
         wbq_s = sb("wbq_s", [P, B * N], U8)
         gather(wbq_s[:], wb_s[:], idx3, 0, B * N)
-        for pair in range(2):
-            gather(wbq_w[:, part(pair, 2 * N)], wb_w[:].bitcast(U32), idx3, pair * 2 * N, 2 * N)
+        wbq_w = [sb("wbq_w0", [P, 2 * N], U32)]
+        gather(wbq_w[0][:], wb_w[:].bitcast(U32), idx3, 0, 2 * N)
 
         grouped = []
         for pair in range(2):
@@ -169,7 +172,7 @@ def tile_moe_dyl_none_kernel(
             nc.scalar.copy(words[:], turned[:].rearrange("p b u s -> p b s u"))
             grouped.append(words)
 
-        y_acc = []
+        hq = []
         for pair in range(2):
             hq_w = sb("hq_w%d" % pair, [P, 2 * P], U32)
             hq_s = sb("hq_s%d" % pair, [P, 2 * P], U8)
@@ -178,22 +181,39 @@ def tile_moe_dyl_none_kernel(
                 scales=hq_s[:],
                 in_=grouped[pair][:].rearrange("p b s u -> p (b s u)").bitcast(BF16),
             )
-            acc = psum.tile([P, 2, 2 * P], F32, name="y_acc", tag="y", bufs=2)
+            hq.append((hq_w, hq_s))
+            if pair == 0:
+                wbq_w.append(keep.tile([P, 2 * N], U32, name="wbq_w1", tag="grouped0", align_bytes=64))
+                gather(wbq_w[1][:], wb_w[:].bitcast(U32), idx3, 2 * N, 2 * N)
+
+        gated = [sb("gated%d" % pair, [P, 2, 2 * P], F32) for pair in range(2)]
+
+        y_rows = psum.tile([P, 2, 2 * P], F32, name="y_rows", tag="y", bufs=2)
+        for mb in range(2):
+            for j in range(2):
+                mm(y_rows[:, j, part(mb, P)], wbq_w[0], wbq_s, WB_ROW, part(2 * mb + j, P),
+                   hq[0][0], hq[0][1], 0, part(mb, P), True, True)
+        for j in range(2):
+            nc.vector.tensor_tensor(gated[0][:, j, :], y_rows[:, j, :], gate_rows[:], MULT)
+
+        y_slots = psum.tile([P, 2, N], F32, name="y_slots", tag="y", bufs=2)
+        y_gated = sb("y_gated", [P, 2, N], F32)
+        for mb in range(2):
+            mm(y_slots[:, mb, :], hq[1][0], hq[1][1], 0, part(mb, P),
+               wbq_w[1], wbq_s[:, 2 * N : 4 * N], WB_ROW, part(mb, N), True, True)
+        for mb in range(2):
+            nc.scalar.activation(y_gated[:, mb, :], y_slots[:, mb, :], COPY, scale=gate_col[:, mb : mb + 1])
+        back = psum.tile([P, 2, 2, P], F32, name="back", tag="h_acc0")
+        for j in range(2):
             for mb in range(2):
-                for j in range(2):
-                    mm(acc[:, j, part(mb, P)], wbq_w, wbq_s, WB_ROW, part(4 * pair + 2 * mb + j, P),
-                       hq_w, hq_s, 0, part(mb, P), True, True)
-            y_acc.append(acc)
+                nc.tensor.transpose(back[:, j, mb, :], y_gated[:, mb, part(j, P)], ident[:])
+        nc.scalar.copy(gated[1][:], back[:].rearrange("p j b s -> p j (b s)"))
 
         for pair in range(2):
             cols = part(pair, 2 * P)
-            gated = sb("gated%d" % pair, [P, 2, 2 * P], F32)
-            nc.vector.tensor_tensor(
-                gated[:], y_acc[pair][:], gate_sb[:, cols].unsqueeze(1).to_broadcast([P, 2, 2 * P]), MULT
-            )
             for j in range(2):
                 nc.vector.tensor_tensor(
-                    result[j][:].indirect(idx[:, part(pair, 2 * P // 16)]), gated[:, j, :], base_slots[:, j, cols], ADD
+                    result[j][:].indirect(idx[:, part(pair, 2 * P // 16)]), gated[pair][:, j, :], base_slots[:, j, cols], ADD
                 )
                 if pair == 1:
                     nc.sync.dma_start(out[part(j, P), :], result[j][:])

@@ -53,8 +53,8 @@ def tile_moe_dyl_none_kernel(
                     scales[:, 4 * q : 4 * q + 4, :].bitcast(I32),
                 )
 
-        def gather(dst, window, offsets, first, count):
-            nc.vector.tensor_copy(dst, window.indirect(offsets[:, first // 16 : (first + count) // 16]))
+        def gather(dst, window, offsets, entry, count):
+            nc.vector.tensor_copy(dst, window.indirect(offsets[:, entry // 16 : (entry + count) // 16]))
 
         def mm(acc, lhs, lhs_scales, lhs_row, lhs_cols, rhs, rhs_scales, rhs_row, rhs_cols, start, stop):
             nc.tensor.matmul_mx(
@@ -113,10 +113,10 @@ def tile_moe_dyl_none_kernel(
 
         for s in range(2):
             for r in range(4):
-                first = WA_RAW + 16 * s
+                raw = WA_RAW + 16 * s
                 (nc.scalar, nc.gpsimd)[s].dma_start(
                     waq_s[WA_ROW[s] + r : P : 32, :].bitcast(I32),
-                    waq_rows[first + r : first + 16 : 4, :].bitcast(I32),
+                    waq_rows[raw + r : raw + 16 : 4, :].bitcast(I32),
                 )
 
         gather(xq_s[:], x_s[:], idx, 0, SLOTS)
@@ -152,6 +152,7 @@ def tile_moe_dyl_none_kernel(
 
         for m in range(B):
             gather(waq_w[1][:, part(m, H)], wa_w[1][:].bitcast(U32), idx2, m * H, H)
+
         wbq_s = sb("wbq_s", [P, B * N], U8)
         gather(wbq_s[:], wb_s[:], idx3, 0, B * N)
         wbq_w = [sb("wbq_w0", [P, 2 * N], U32)]
@@ -168,21 +169,21 @@ def tile_moe_dyl_none_kernel(
                 h_words = h_bf[:].rearrange("s u p e -> s (u p e)").bitcast(F32)
                 for u in range(2):
                     nc.tensor.transpose(turned[:, mb, u, :], h_words[:, part(u, P)], ident[:])
-            words = sb("grouped%d" % pair, [P, 2, P, 2], F32)
-            nc.scalar.copy(words[:], turned[:].rearrange("p b u s -> p b s u"))
-            grouped.append(words)
+            for mb in range(2):
+                grouped.append(sb("grouped%d" % (2 * pair + mb), [P, P, 2], F32))
+                nc.scalar.copy(grouped[-1][:], turned[:, mb].rearrange("p u s -> p s u"))
 
         hq = []
-        for pair in range(2):
-            hq_w = sb("hq_w%d" % pair, [P, 2 * P], U32)
-            hq_s = sb("hq_s%d" % pair, [P, 2 * P], U8)
+        for m in range(B):
+            hq_w = sb("hq_w%d" % m, [P, P], U32)
+            hq_s = sb("hq_s%d" % m, [P, P], U8)
             nc.vector.quantize_mx(
                 out=hq_w[:].bitcast(FP8X4),
                 scales=hq_s[:],
-                in_=grouped[pair][:].rearrange("p b s u -> p (b s u)").bitcast(BF16),
+                in_=grouped[m][:].rearrange("p s u -> p (s u)").bitcast(BF16),
             )
             hq.append((hq_w, hq_s))
-            if pair == 0:
+            if m == 1:
                 wbq_w.append(keep.tile([P, 2 * N], U32, name="wbq_w1", tag="grouped0", align_bytes=64))
                 gather(wbq_w[1][:], wb_w[:].bitcast(U32), idx3, 2 * N, 2 * N)
 
@@ -192,28 +193,31 @@ def tile_moe_dyl_none_kernel(
         for mb in range(2):
             for j in range(2):
                 mm(y_rows[:, j, part(mb, P)], wbq_w[0], wbq_s, WB_ROW, part(2 * mb + j, P),
-                   hq[0][0], hq[0][1], 0, part(mb, P), True, True)
+                   hq[mb][0], hq[mb][1], 0, slice(0, P), True, True)
         for j in range(2):
             nc.vector.tensor_tensor(gated[0][:, j, :], y_rows[:, j, :], gate_rows[:], MULT)
 
-        y_slots = psum.tile([P, 2, N], F32, name="y_slots", tag="y", bufs=2)
-        y_gated = sb("y_gated", [P, 2, N], F32)
+        y_gated = []
         for mb in range(2):
-            mm(y_slots[:, mb, :], hq[1][0], hq[1][1], 0, part(mb, P),
+            y_slots = psum.tile([P, N], F32, name="y_slots", tag="h_acc%d" % mb)
+            mm(y_slots[:], hq[2 + mb][0], hq[2 + mb][1], 0, slice(0, P),
                wbq_w[1], wbq_s[:, 2 * N : 4 * N], WB_ROW, part(mb, N), True, True)
-        for mb in range(2):
-            nc.scalar.activation(y_gated[:, mb, :], y_slots[:, mb, :], COPY, scale=gate_col[:, mb : mb + 1])
-        back = psum.tile([P, 2, 2, P], F32, name="back", tag="h_acc0")
+            y_gated.append(sb("y_gated%d" % mb, [P, N], F32))
+            nc.scalar.activation(y_gated[mb][:], y_slots[:], COPY, scale=gate_col[:, mb : mb + 1])
         for j in range(2):
+            back = psum.tile([P, 2, P], F32, name="back", tag="h_acc%d" % (2 + j))
             for mb in range(2):
-                nc.tensor.transpose(back[:, j, mb, :], y_gated[:, mb, part(j, P)], ident[:])
-        nc.scalar.copy(gated[1][:], back[:].rearrange("p j b s -> p j (b s)"))
+                nc.tensor.transpose(back[:, mb, :], y_gated[mb][:, part(j, P)], ident[:])
+            nc.scalar.copy(gated[1][:, j, :], back[:].rearrange("p b s -> p (b s)"))
 
         for pair in range(2):
             cols = part(pair, 2 * P)
             for j in range(2):
                 nc.vector.tensor_tensor(
-                    result[j][:].indirect(idx[:, part(pair, 2 * P // 16)]), gated[pair][:, j, :], base_slots[:, j, cols], ADD
+                    result[j][:].indirect(idx[:, part(pair, 2 * P // 16)]),
+                    gated[pair][:, j, :],
+                    base_slots[:, j, cols],
+                    ADD,
                 )
                 if pair == 1:
                     nc.sync.dma_start(out[part(j, P), :], result[j][:])

@@ -77,10 +77,10 @@ def tile_moe_dyl_none_kernel(
         w_s = sb("w_s", [P, N], U8)
         wa_s = sb("wa_s", [P, E * H], U8)
         wb_s = sb("wb_s", [P, E * N], U8)
-        waq_s = sb("waq_s", [P, B * H], U8)
+        waq_s = [sb("waq_s%d" % s, [P, B * H], U8) for s in range(2)]
         ident = sb("ident", [P, P], F32)
 
-        for tile in (x_s[:], w_s[:], wa_s[0:WA_RAW, :], waq_s[:], wb_s[:]):
+        for tile in (x_s[:], w_s[:], wa_s[0:WA_RAW, :], wb_s[:]):
             nc.vector.memset(tile.bitcast(I32), 0)
 
         nc.sync.dma_start(wa_s[WA_RAW:P, :].bitcast(I32), wa_scales.rearrange("s b c -> (s b) c").bitcast(I32))
@@ -91,16 +91,9 @@ def tile_moe_dyl_none_kernel(
         load_scales(nc.scalar, w_s, w_scales, W_ROW[0])
         nc.sync.dma_start(w_w[:], w_words.rearrange("s p n t -> p s (n t)").bitcast(I32))
         wa_w = [sb("wa_w%d" % s, [P, E * H], I32) for s in range(2)]
-        for s in range(2):
-            load_words(wa_w[s][:], wa_words[s])
+        load_words(wa_w[0][:], wa_words[0])
         nc.sync.dma_start(idx3[:], offs3)
-        wb_w = sb("wb_w", [P, E * N], I32)
-        gate_rows = sb("gate_rows", [P, 2 * P], F32)
-        gate_col = sb("gate_col", [P, 2], F32)
-        load_words(wb_w[:], wb_words[0])
-        nc.sync.dma_start(gate_rows[:], gate[:, 0 : 2 * P])
-        with nc.allow_non_contiguous_dma(reason="one gate value a partition and block"):
-            nc.sync.dma_start(gate_col[:], gate[0, 2 * P : SLOTS].rearrange("(b p) -> p b", p=P))
+        load_words(wa_w[1][:], wa_words[1])
         load_scales(nc.gpsimd, wb_s, wb_scales, WB_ROW)
         make_identity(nc, ident[:])
 
@@ -114,15 +107,25 @@ def tile_moe_dyl_none_kernel(
         for s in range(2):
             for r in range(4):
                 raw = WA_RAW + 16 * s
-                (nc.scalar, nc.gpsimd)[s].dma_start(
-                    waq_s[WA_ROW[s] + r : P : 32, :].bitcast(I32),
+                (nc.scalar, nc.sync)[s].dma_start(
+                    waq_s[s][WA_ROW[s] + r : P : 32, :].bitcast(I32),
                     waq_rows[raw + r : raw + 16 : 4, :].bitcast(I32),
                 )
+
+        wb_w = sb("wb_w", [P, E * N], I32)
+        gate_rows = sb("gate_rows", [P, 2 * P], F32)
+        gate_col = sb("gate_col", [P, 2], F32)
+        load_words(wb_w[:], wb_words[0])
+        nc.sync.dma_start(gate_rows[:], gate[:, 0 : 2 * P])
+        with nc.allow_non_contiguous_dma(reason="one gate value a partition and block"):
+            nc.sync.dma_start(gate_col[:], gate[0, 2 * P : SLOTS].rearrange("(b p) -> p b", p=P))
 
         gather(xq_s[:], x_s[:], idx, 0, SLOTS)
         for s in range(2):
             gather(xq_w[s][:], x_w[s].bitcast(U32), idx, 0, SLOTS)
         gather(waq_w[0][:], wa_w[0][:].bitcast(U32), idx2, 0, B * H)
+        wbq_s = [sb("wbq_s0", [P, 2 * N], U8)]
+        gather(wbq_s[0][:], wb_s[:], idx3, 0, 2 * N)
 
         late_banks = ("turn", "y")
         result = [sb("result%d" % j, [P, T], F32) for j in range(2)]
@@ -144,7 +147,7 @@ def tile_moe_dyl_none_kernel(
 
         def h_pass(m, s):
             mm(h_acc[m][:], xq_w[s], xq_s, X_ROW[s], part(m, P),
-               waq_w[s], waq_s, WA_ROW[s], part(m, H), s == 0, s == 1)
+               waq_w[s], waq_s[s], WA_ROW[s], part(m, H), s == 0, s == 1)
 
         h_acc = [psum.tile([P, H], F32, name="h_acc%d" % m) for m in range(B)]
         for m in range(B):
@@ -153,8 +156,8 @@ def tile_moe_dyl_none_kernel(
         for m in range(B):
             gather(waq_w[1][:, part(m, H)], wa_w[1][:].bitcast(U32), idx2, m * H, H)
 
-        wbq_s = sb("wbq_s", [P, B * N], U8)
-        gather(wbq_s[:], wb_s[:], idx3, 0, B * N)
+        wbq_s.append(keep.tile([P, 2 * N], U8, name="wbq_s1", tag="wa_w1", align_bytes=64))
+        gather(wbq_s[1][:], wb_s[:], idx3, 2 * N, 2 * N)
         wbq_w = [sb("wbq_w0", [P, 2 * N], U32)]
         gather(wbq_w[0][:], wb_w[:].bitcast(U32), idx3, 0, 2 * N)
 
@@ -192,7 +195,7 @@ def tile_moe_dyl_none_kernel(
         y_rows = psum.tile([P, 2, 2 * P], F32, name="y_rows", tag="y", bufs=2)
         for mb in range(2):
             for j in range(2):
-                mm(y_rows[:, j, part(mb, P)], wbq_w[0], wbq_s, WB_ROW, part(2 * mb + j, P),
+                mm(y_rows[:, j, part(mb, P)], wbq_w[0], wbq_s[0], WB_ROW, part(2 * mb + j, P),
                    hq[mb][0], hq[mb][1], 0, slice(0, P), True, True)
         for j in range(2):
             nc.vector.tensor_tensor(gated[0][:, j, :], y_rows[:, j, :], gate_rows[:], MULT)
@@ -201,7 +204,7 @@ def tile_moe_dyl_none_kernel(
         for mb in range(2):
             y_slots = psum.tile([P, N], F32, name="y_slots", tag="h_acc%d" % mb)
             mm(y_slots[:], hq[2 + mb][0], hq[2 + mb][1], 0, slice(0, P),
-               wbq_w[1], wbq_s[:, 2 * N : 4 * N], WB_ROW, part(mb, N), True, True)
+               wbq_w[1], wbq_s[1], WB_ROW, part(mb, N), True, True)
             y_gated.append(sb("y_gated%d" % mb, [P, N], F32))
             nc.scalar.activation(y_gated[mb][:], y_slots[:], COPY, scale=gate_col[:, mb : mb + 1])
         for j in range(2):

@@ -34,10 +34,14 @@ def tile_moe_dyl_none_kernel(
     nc = tc.nc
     with ExitStack() as ctx:
         keep = ctx.enter_context(tc.tile_pool(name="keep", bufs=1))
+        shared = ctx.enter_context(tc.tile_pool(name="shared", bufs=1))
         psum = ctx.enter_context(tc.psum_pool(name="psum", bufs=1))
 
         def sb(name, shape, dtype):
             return keep.tile(shape, dtype, name=name, align_bytes=64)
+
+        def placed(name, shape, dtype, offset):
+            return shared.tile(shape, dtype, name=name, offset=offset, align_bytes=64)
 
         def part(index, width):
             return slice(index * width, (index + 1) * width)
@@ -80,104 +84,142 @@ def tile_moe_dyl_none_kernel(
         waq_s = [sb("waq_s%d" % s, [P, B * H], U8) for s in range(2)]
         ident = sb("ident", [P, P], F32)
 
-        for tile in (x_s[:], w_s[:], wa_s[0:WA_RAW, :], wb_s[:]):
+        for tile in (x_s[:], wa_s[0:WA_RAW, :]):
             nc.vector.memset(tile.bitcast(I32), 0)
+        nc.gpsimd.memset(wb_s[:].bitcast(I32), 0)
 
+        wa_w = [sb("wa_w0", [P, E * H], I32), sb("wa_w1", [P, E * H], I32)]
+        wb_w = sb("wb_w", [P, E * N], I32)
         nc.sync.dma_start(wa_s[WA_RAW:P, :].bitcast(I32), wa_scales.rearrange("s b c -> (s b) c").bitcast(I32))
         nc.sync.dma_start(idx2[:], offs2)
+        load_scales(nc.sync, x_s, x_scales, X_ROW[0])
         nc.sync.dma_start(idx[:], offs)
-        load_scales(nc.scalar, x_s, x_scales, X_ROW[0])
         nc.sync.dma_start(x_both[:], x_words.rearrange("s p n t -> p s (n t)").bitcast(I32))
-        load_scales(nc.scalar, w_s, w_scales, W_ROW[0])
         nc.sync.dma_start(w_w[:], w_words.rearrange("s p n t -> p s (n t)").bitcast(I32))
-        wa_w = [sb("wa_w%d" % s, [P, E * H], I32) for s in range(2)]
-        load_words(wa_w[0][:], wa_words[0])
         nc.sync.dma_start(idx3[:], offs3)
-        load_words(wa_w[1][:], wa_words[1])
+        load_scales(nc.sync, w_s, w_scales, W_ROW[0])
+        load_words(wa_w[0][:], wa_words[0])
         load_scales(nc.gpsimd, wb_s, wb_scales, WB_ROW)
         make_identity(nc, ident[:])
 
         xq_w = [sb("xq_w%d" % s, [P, SLOTS], U32) for s in range(2)]
         xq_s = sb("xq_s", [P, SLOTS], U8)
-        waq_w = [sb("waq_w%d" % s, [P, B * H], U32) for s in range(2)]
         waq_rows = sb("waq_rows", [P, B * H], U8)
+
+        def reuse(name, shape, dtype, tag):
+            return keep.tile(shape, dtype, name=name, tag=tag, align_bytes=64)
+
+        def bank(name, shape, tag):
+            return psum.tile(shape, F32, name=name, tag=tag)
 
         gather(waq_rows[:], wa_s[:], idx2, 0, B * H)
 
-        for s in range(2):
-            for r in range(4):
-                raw = WA_RAW + 16 * s
-                (nc.scalar, nc.sync)[s].dma_start(
-                    waq_s[s][WA_ROW[s] + r : P : 32, :].bitcast(I32),
-                    waq_rows[raw + r : raw + 16 : 4, :].bitcast(I32),
-                )
+        def move_rows(s, r):
+            raw = WA_RAW + 16 * s
+            nc.sync.dma_start(
+                waq_s[s][WA_ROW[s] + r : P : 32, :].bitcast(I32),
+                waq_rows[raw + r : raw + 16 : 4, :].bitcast(I32),
+            )
 
-        wb_w = sb("wb_w", [P, E * N], I32)
+        half = E * N // 2
+        for r in range(4):
+            move_rows(0, r)
+        load_words(wa_w[1][:], wa_words[1])
+        load_words(wb_w[:, 0:half], wb_words[0, :, 0:half])
+        for r in range(4):
+            move_rows(1, r)
+        load_words(wb_w[:, half:], wb_words[0, :, half:])
+
         gate_rows = sb("gate_rows", [P, 2 * P], F32)
-        gate_col = sb("gate_col", [P, 2], F32)
-        load_words(wb_w[:], wb_words[0])
-        nc.sync.dma_start(gate_rows[:], gate[:, 0 : 2 * P])
+        gate_col = sb("gate_col", [P, 3], F32)
         with nc.allow_non_contiguous_dma(reason="one gate value a partition and block"):
-            nc.sync.dma_start(gate_col[:], gate[0, 2 * P : SLOTS].rearrange("(b p) -> p b", p=P))
+            nc.sync.dma_start(gate_col[:], gate[0, 0 : 3 * P].rearrange("(b p) -> p b", p=P))
+        nc.sync.dma_start(gate_rows[:], gate[:, 2 * P : SLOTS])
 
         gather(xq_s[:], x_s[:], idx, 0, SLOTS)
         for s in range(2):
             gather(xq_w[s][:], x_w[s].bitcast(U32), idx, 0, SLOTS)
-        gather(waq_w[0][:], wa_w[0][:].bitcast(U32), idx2, 0, B * H)
+
+        waq_w = {}
+
+        def gather_wa(m, s, tile):
+            waq_w[m, s] = tile
+            gather(tile, wa_w[s][:].bitcast(U32), idx2, m * H, H)
+
         wbq_s = [sb("wbq_s0", [P, 2 * N], U8)]
         gather(wbq_s[0][:], wb_s[:], idx3, 0, 2 * N)
+        for m in range(2):
+            gather_wa(m, 0, sb("waq_first%d" % m, [P, H], U32)[:])
 
-        late_banks = ("turn", "y")
         result = [sb("result%d" % j, [P, T], F32) for j in range(2)]
         for j in range(2):
             for half in range(2):
-                acc = psum.tile([P, BANK], F32, name="base_acc", tag=late_banks[half], bufs=2)
+                acc = bank("base_acc", [P, BANK], ("turn0", "turn1", "y0", "y1")[2 * j + half])
                 for s in range(2):
                     mm(acc[:], w_w[:, s, :], w_s, W_ROW[s], part(j, P),
                        x_w[s], x_s, X_ROW[s], part(half, BANK), s == 0, s == 1)
                 nc.scalar.copy(result[j][:, part(half, BANK)], acc[:])
 
-        base_slots = sb("base_slots", [P, 2, SLOTS], F32)
-        for j in range(2):
-            acc = psum.tile([P, SLOTS], F32, name="slot_acc", tag=late_banks[j], bufs=2)
+        base_early = sb("base_early", [P, 2, N], F32)
+        acc = bank("slot_acc", [P, 2, N], "back0")
+        for m in range(2):
             for s in range(2):
-                mm(acc[:], w_w[:, s, :], w_s, W_ROW[s], part(j, P),
-                   xq_w[s], xq_s, X_ROW[s], slice(0, SLOTS), s == 0, s == 1)
-            nc.scalar.copy(base_slots[:, j, :], acc[:])
+                mm(acc[:, m, :], xq_w[s], xq_s, X_ROW[s], part(m, P),
+                   w_w[:, s, :], w_s, W_ROW[s], slice(0, N), s == 0, s == 1)
+        nc.scalar.copy(base_early[:], acc[:])
+        base_late = sb("base_late", [P, 4, P], F32)
+        acc = bank("slot_acc", [P, 4, P], "back1")
+        for s in range(2):
+            mm(acc[:, 0:2, :].rearrange("p b s -> p (b s)"), w_w[:, s, :], w_s, W_ROW[s], part(0, P),
+               xq_w[s], xq_s, X_ROW[s], part(1, 2 * P), s == 0, s == 1)
+        for s in range(2):
+            mm(acc[:, 2, :], w_w[:, s, :], w_s, W_ROW[s], part(1, P),
+               xq_w[s], xq_s, X_ROW[s], part(3, P), s == 0, s == 1)
+        for s in range(2):
+            mm(acc[:, 3, :], xq_w[s], xq_s, X_ROW[s], part(2, P),
+               w_w[:, s, :], w_s, W_ROW[s], part(1, P), s == 0, s == 1)
+        nc.scalar.copy(base_late[:], acc[:])
+
+        h_acc = {}
 
         def h_pass(m, s):
-            mm(h_acc[m][:], xq_w[s], xq_s, X_ROW[s], part(m, P),
-               waq_w[s], waq_s[s], WA_ROW[s], part(m, H), s == 0, s == 1)
+            nc.tensor.matmul_mx(
+                out=h_acc[m][:],
+                lhsT=xq_w[s][:, part(m, P)].bitcast(FP8X4),
+                lhsT_scale=xq_s[X_ROW[s] : P, part(m, P)],
+                rhs=waq_w[m, s].bitcast(FP8X4),
+                rhs_scale=waq_s[s][WA_ROW[s] : P, part(m, H)],
+                start=s == 0,
+                stop=s == 1,
+            )
 
-        h_acc = [psum.tile([P, H], F32, name="h_acc%d" % m) for m in range(B)]
-        for m in range(B):
+        for m in range(2):
+            h_acc[m] = bank("h_acc%d" % m, [P, H], "h%d" % m)
             h_pass(m, 0)
 
-        for m in range(B):
-            gather(waq_w[1][:, part(m, H)], wa_w[1][:].bitcast(U32), idx2, m * H, H)
-
-        wbq_s.append(keep.tile([P, 2 * N], U8, name="wbq_s1", tag="wa_w1", align_bytes=64))
-        gather(wbq_s[1][:], wb_s[:], idx3, 2 * N, 2 * N)
+        for m in range(2):
+            gather_wa(m, 1, sb("waq_second%d" % m, [P, H], U32)[:])
+        gather_wa(2, 0, reuse("waq_first2", [P, H], U32, "waq_second0")[:])
         wbq_w = [sb("wbq_w0", [P, 2 * N], U32)]
         gather(wbq_w[0][:], wb_w[:].bitcast(U32), idx3, 0, 2 * N)
 
-        grouped = []
-        for pair in range(2):
-            turned = psum.tile([P, 2, 2, P], F32, name="turned", tag="turn", bufs=2)
-            for mb in range(2):
-                m = 2 * pair + mb
-                h_pass(m, 1)
-                h_bf = sb("h_bf%d" % m, [P, 2, P, 2], BF16)
-                nc.scalar.copy(h_bf[:], h_acc[m][:].rearrange("s (p u e) -> s u p e", u=2, e=2))
-                h_words = h_bf[:].rearrange("s u p e -> s (u p e)").bitcast(F32)
-                for u in range(2):
-                    nc.tensor.transpose(turned[:, mb, u, :], h_words[:, part(u, P)], ident[:])
-            for mb in range(2):
-                grouped.append(sb("grouped%d" % (2 * pair + mb), [P, P, 2], F32))
-                nc.scalar.copy(grouped[-1][:], turned[:, mb].rearrange("p u s -> p s u"))
+        grouped = {}
 
-        hq = []
-        for m in range(B):
+        def round_h(m):
+            h_bf = sb("h_bf%d" % m, [P, 2, P, 2], BF16)
+            nc.scalar.copy(h_bf[:], h_acc[m][:].rearrange("s (p u e) -> s u p e", u=2, e=2))
+            return h_bf[:].rearrange("s u p e -> s (u p e)").bitcast(F32)
+
+        def turn_h(m, h_words):
+            turned = bank("turned", [P, 2, P], "turn%d" % (m % 2))
+            for u in range(2):
+                nc.tensor.transpose(turned[:, u, :], h_words[:, part(u, P)], ident[:])
+            grouped[m] = sb("grouped%d" % m, [P, P, 2], F32)
+            nc.scalar.copy(grouped[m][:], turned[:].rearrange("p u s -> p s u"))
+
+        hq = {}
+
+        def quantise(m):
             hq_w = sb("hq_w%d" % m, [P, P], U32)
             hq_s = sb("hq_s%d" % m, [P, P], U8)
             nc.vector.quantize_mx(
@@ -185,42 +227,93 @@ def tile_moe_dyl_none_kernel(
                 scales=hq_s[:],
                 in_=grouped[m][:].rearrange("p s u -> p (s u)").bitcast(BF16),
             )
-            hq.append((hq_w, hq_s))
-            if m == 1:
-                wbq_w.append(keep.tile([P, 2 * N], U32, name="wbq_w1", tag="grouped0", align_bytes=64))
-                gather(wbq_w[1][:], wb_w[:].bitcast(U32), idx3, 2 * N, 2 * N)
+            hq[m] = (hq_w, hq_s)
 
-        gated = [sb("gated%d" % pair, [P, 2, 2 * P], F32) for pair in range(2)]
+        def gate_slots(m, cols, width, tag):
+            y_slots = bank("y_slots", [P, width], tag)
+            mm(y_slots[:], hq[m][0], hq[m][1], 0, slice(0, P),
+               wbq_w[m // 2], wbq_s[m // 2], WB_ROW, cols, True, True)
+            y_gated = sb("y_gated%d" % m, [P, width], F32)
+            nc.scalar.activation(y_gated[:], y_slots[:], COPY, scale=gate_col[:, m : m + 1])
+            return y_gated
 
-        y_rows = psum.tile([P, 2, 2 * P], F32, name="y_rows", tag="y", bufs=2)
-        for mb in range(2):
-            for j in range(2):
-                mm(y_rows[:, j, part(mb, P)], wbq_w[0], wbq_s[0], WB_ROW, part(2 * mb + j, P),
-                   hq[mb][0], hq[mb][1], 0, slice(0, P), True, True)
+        def turn_sum(acc, first, second):
+            nc.tensor.matmul(acc, first, ident[:], start=True, stop=False, is_transpose=True)
+            nc.tensor.matmul(acc, second, ident[:], start=False, stop=True, is_transpose=True)
+
+        def scatter(j, entry, count, values):
+            nc.scalar.activation(result[j][:].indirect(idx[:, entry // 16 : (entry + count) // 16]), values, COPY)
+
+        for m in range(2):
+            h_pass(m, 1)
+            turn_h(m, round_h(m))
+
+        gather_wa(2, 1, reuse("waq_second2", [P, H], U32, "h_bf0")[:])
+        quantise(0)
+        gather_wa(3, 0, reuse("waq_first3", [P, H], U32, "h_bf1")[:])
+        quantise(1)
+        gather_wa(3, 1, reuse("waq_second3", [P, H], U32, "grouped0")[:])
+        wbq_s.append(reuse("wbq_s1", [P, 2 * N], U8, "grouped1"))
+        gather(wbq_s[1][:], wb_s[:], idx3, 2 * N, 2 * N)
+        wbq_w.append(reuse("wbq_w1", [P, 2 * N], U32, "wa_w0"))
+        gather(wbq_w[1][:, 0:N], wb_w[:].bitcast(U32), idx3, 2 * N, N)
+
+        def sum_back(pieces, tag):
+            back = bank("back", [P, len(pieces), P], tag)
+            for place, (base, y) in enumerate(pieces):
+                turn_sum(back[:, place, :], base, y)
+            return back[:].rearrange("p b s -> p (b s)")
+
+        def copy_scatter(j, entry, back, summed):
+            nc.scalar.copy(summed[:], back)
+            scatter(j, entry, summed.shape[1], summed[:])
+
+        def early(m, j):
+            return base_early[:, m, part(j, P)], y_gated[m][:, part(j, P)]
+
+        y_gated = [gate_slots(0, part(0, N), N, "y0")]
+        copy_scatter(0, 0, sum_back([early(0, 0)], "back0"), sb("summed0", [P, P], F32))
+        y_gated.append(gate_slots(1, part(1, N), N, "y1"))
+        back_second = sum_back([early(1, 0)], "back0")
+        back_rows = sum_back([early(0, 1), early(1, 1)], "back1")
+
+        words = {}
+        for m in range(2, B):
+            h_acc[m] = bank("h_acc%d" % m, [P, H], "h%d" % (m - 2))
+            for s in range(2):
+                h_pass(m, s)
+            words[m] = round_h(m)
+            if m == 2:
+                turn_h(m, words[m])
+        copy_scatter(0, P, back_second, reuse("summed1", [P, P], F32, "grouped0"))
+        turn_h(3, words[3])
+
+        quantise(2)
+        gather(wbq_w[1][:, N : 2 * N], wb_w[:].bitcast(U32), idx3, 3 * N, N)
+        gated = sb("gated", [P, 3, P], F32)
+        y_third = bank("y_third", [P, P], "h0")
+        mm(y_third[:], wbq_w[1], wbq_s[1], WB_ROW, part(0, P), hq[2][0], hq[2][1], 0, slice(0, P), True, True)
+        nc.vector.tensor_tensor(gated[:, 0, :], y_third[:], gate_rows[:, 0:P], MULT)
+        quantise(3)
+
+        third = gate_slots(2, part(1, P), P, "y0")
+        back_third = sum_back([(base_late[:, 3, :], third[:])], "y1")
+        copy_scatter(1, 0, back_rows, reuse("summed2", [P, 2 * P], F32, "h_bf3"))
+        copy_scatter(1, 2 * P, back_third, sb("summed3", [P, P], F32))
+
+        y_last = bank("y_last", [P, 2, P], "h1")
         for j in range(2):
-            nc.vector.tensor_tensor(gated[0][:, j, :], y_rows[:, j, :], gate_rows[:], MULT)
+            mm(y_last[:, j, :], wbq_w[1], wbq_s[1], WB_ROW, part(2 + j, P),
+               hq[3][0], hq[3][1], 0, slice(0, P), True, True)
 
-        y_gated = []
-        for mb in range(2):
-            y_slots = psum.tile([P, N], F32, name="y_slots", tag="h_acc%d" % mb)
-            mm(y_slots[:], hq[2 + mb][0], hq[2 + mb][1], 0, slice(0, P),
-               wbq_w[1], wbq_s[1], WB_ROW, part(mb, N), True, True)
-            y_gated.append(sb("y_gated%d" % mb, [P, N], F32))
-            nc.scalar.activation(y_gated[mb][:], y_slots[:], COPY, scale=gate_col[:, mb : mb + 1])
+        def add_scatter(j, m, place):
+            nc.vector.tensor_tensor(
+                result[j][:].indirect(idx[:, part(m, P // 16)]), gated[:, place, :], base_late[:, place, :], ADD
+            )
+
+        add_scatter(0, 2, 0)
         for j in range(2):
-            back = psum.tile([P, 2, P], F32, name="back", tag="h_acc%d" % (2 + j))
-            for mb in range(2):
-                nc.tensor.transpose(back[:, mb, :], y_gated[mb][:, part(j, P)], ident[:])
-            nc.scalar.copy(gated[1][:, j, :], back[:].rearrange("p b s -> p (b s)"))
-
-        for pair in range(2):
-            cols = part(pair, 2 * P)
-            for j in range(2):
-                nc.vector.tensor_tensor(
-                    result[j][:].indirect(idx[:, part(pair, 2 * P // 16)]),
-                    gated[pair][:, j, :],
-                    base_slots[:, j, cols],
-                    ADD,
-                )
-                if pair == 1:
-                    nc.sync.dma_start(out[part(j, P), :], result[j][:])
+            nc.vector.tensor_tensor(gated[:, 1 + j, :], y_last[:, j, :], gate_rows[:, P : 2 * P], MULT)
+        for j in range(2):
+            add_scatter(j, 3, 1 + j)
+            nc.sync.dma_start(out[part(j, P), :], result[j][:])

@@ -34,14 +34,10 @@ def tile_moe_dyl_none_kernel(
     nc = tc.nc
     with ExitStack() as ctx:
         keep = ctx.enter_context(tc.tile_pool(name="keep", bufs=1))
-        shared = ctx.enter_context(tc.tile_pool(name="shared", bufs=1))
         psum = ctx.enter_context(tc.psum_pool(name="psum", bufs=1))
 
         def sb(name, shape, dtype):
             return keep.tile(shape, dtype, name=name, align_bytes=64)
-
-        def placed(name, shape, dtype, offset):
-            return shared.tile(shape, dtype, name=name, offset=offset, align_bytes=64)
 
         def part(index, width):
             return slice(index * width, (index + 1) * width)
@@ -84,9 +80,8 @@ def tile_moe_dyl_none_kernel(
         waq_s = [sb("waq_s%d" % s, [P, B * H], U8) for s in range(2)]
         ident = sb("ident", [P, P], F32)
 
-        for tile in (x_s[:], wa_s[0:WA_RAW, :]):
+        for tile in (x_s[:], wa_s[0:WA_RAW, :], wb_s[:]):
             nc.vector.memset(tile.bitcast(I32), 0)
-        nc.gpsimd.memset(wb_s[:].bitcast(I32), 0)
 
         wa_w = [sb("wa_w0", [P, E * H], I32), sb("wa_w1", [P, E * H], I32)]
         wb_w = sb("wb_w", [P, E * N], I32)
@@ -99,7 +94,7 @@ def tile_moe_dyl_none_kernel(
         nc.sync.dma_start(idx3[:], offs3)
         load_scales(nc.sync, w_s, w_scales, W_ROW[0])
         load_words(wa_w[0][:], wa_words[0])
-        load_scales(nc.gpsimd, wb_s, wb_scales, WB_ROW)
+        load_scales(nc.sync, wb_s, wb_scales, WB_ROW)
         make_identity(nc, ident[:])
 
         xq_w = [sb("xq_w%d" % s, [P, SLOTS], U32) for s in range(2)]
@@ -122,18 +117,20 @@ def tile_moe_dyl_none_kernel(
             )
 
         half = E * N // 2
-        for r in range(4):
+        for r in range(2):
             move_rows(0, r)
         load_words(wa_w[1][:], wa_words[1])
+        for r in range(2, 4):
+            move_rows(0, r)
         load_words(wb_w[:, 0:half], wb_words[0, :, 0:half])
         for r in range(4):
             move_rows(1, r)
         load_words(wb_w[:, half:], wb_words[0, :, half:])
 
         gate_rows = sb("gate_rows", [P, 2 * P], F32)
-        gate_col = sb("gate_col", [P, 3], F32)
+        gate_col = sb("gate_col", [P, 2], F32)
         with nc.allow_non_contiguous_dma(reason="one gate value a partition and block"):
-            nc.sync.dma_start(gate_col[:], gate[0, 0 : 3 * P].rearrange("(b p) -> p b", p=P))
+            nc.sync.dma_start(gate_col[:], gate[0, 0 : 2 * P].rearrange("(b p) -> p b", p=P))
         nc.sync.dma_start(gate_rows[:], gate[:, 2 * P : SLOTS])
 
         gather(xq_s[:], x_s[:], idx, 0, SLOTS)
@@ -146,10 +143,10 @@ def tile_moe_dyl_none_kernel(
             waq_w[m, s] = tile
             gather(tile, wa_w[s][:].bitcast(U32), idx2, m * H, H)
 
+        for m in range(3):
+            gather_wa(m, 0, sb("waq_first%d" % m, [P, H], U32)[:])
         wbq_s = [sb("wbq_s0", [P, 2 * N], U8)]
         gather(wbq_s[0][:], wb_s[:], idx3, 0, 2 * N)
-        for m in range(2):
-            gather_wa(m, 0, sb("waq_first%d" % m, [P, H], U32)[:])
 
         result = [sb("result%d" % j, [P, T], F32) for j in range(2)]
         for j in range(2):
@@ -167,17 +164,12 @@ def tile_moe_dyl_none_kernel(
                 mm(acc[:, m, :], xq_w[s], xq_s, X_ROW[s], part(m, P),
                    w_w[:, s, :], w_s, W_ROW[s], slice(0, N), s == 0, s == 1)
         nc.scalar.copy(base_early[:], acc[:])
-        base_late = sb("base_late", [P, 4, P], F32)
-        acc = bank("slot_acc", [P, 4, P], "back1")
-        for s in range(2):
-            mm(acc[:, 0:2, :].rearrange("p b s -> p (b s)"), w_w[:, s, :], w_s, W_ROW[s], part(0, P),
-               xq_w[s], xq_s, X_ROW[s], part(1, 2 * P), s == 0, s == 1)
-        for s in range(2):
-            mm(acc[:, 2, :], w_w[:, s, :], w_s, W_ROW[s], part(1, P),
-               xq_w[s], xq_s, X_ROW[s], part(3, P), s == 0, s == 1)
-        for s in range(2):
-            mm(acc[:, 3, :], xq_w[s], xq_s, X_ROW[s], part(2, P),
-               w_w[:, s, :], w_s, W_ROW[s], part(1, P), s == 0, s == 1)
+        base_late = sb("base_late", [P, 2, 2 * P], F32)
+        acc = bank("slot_acc", [P, 2, 2 * P], "back1")
+        for j in range(2):
+            for s in range(2):
+                mm(acc[:, j, :], w_w[:, s, :], w_s, W_ROW[s], part(j, P),
+                   xq_w[s], xq_s, X_ROW[s], part(1, 2 * P), s == 0, s == 1)
         nc.scalar.copy(base_late[:], acc[:])
 
         h_acc = {}
@@ -199,7 +191,6 @@ def tile_moe_dyl_none_kernel(
 
         for m in range(2):
             gather_wa(m, 1, sb("waq_second%d" % m, [P, H], U32)[:])
-        gather_wa(2, 0, reuse("waq_first2", [P, H], U32, "waq_second0")[:])
         wbq_w = [sb("wbq_w0", [P, 2 * N], U32)]
         gather(wbq_w[0][:], wb_w[:].bitcast(U32), idx3, 0, 2 * N)
 
@@ -290,30 +281,32 @@ def tile_moe_dyl_none_kernel(
 
         quantise(2)
         gather(wbq_w[1][:, N : 2 * N], wb_w[:].bitcast(U32), idx3, 3 * N, N)
-        gated = sb("gated", [P, 3, P], F32)
-        y_third = bank("y_third", [P, P], "h0")
-        mm(y_third[:], wbq_w[1], wbq_s[1], WB_ROW, part(0, P), hq[2][0], hq[2][1], 0, slice(0, P), True, True)
-        nc.vector.tensor_tensor(gated[:, 0, :], y_third[:], gate_rows[:, 0:P], MULT)
-        quantise(3)
+        gated = sb("gated", [P, 2, 2 * P], F32)
 
-        third = gate_slots(2, part(1, P), P, "y0")
-        back_third = sum_back([(base_late[:, 3, :], third[:])], "y1")
-        copy_scatter(1, 0, back_rows, reuse("summed2", [P, 2 * P], F32, "h_bf3"))
-        copy_scatter(1, 2 * P, back_third, sb("summed3", [P, P], F32))
+        def y_rows(mb):
+            acc = bank("y_rows", [P, 2, P], "h%d" % mb)
+            for j in range(2):
+                mm(acc[:, j, :], wbq_w[1], wbq_s[1], WB_ROW, part(2 * mb + j, P),
+                   hq[2 + mb][0], hq[2 + mb][1], 0, slice(0, P), True, True)
+            return acc
 
-        y_last = bank("y_last", [P, 2, P], "h1")
-        for j in range(2):
-            mm(y_last[:, j, :], wbq_w[1], wbq_s[1], WB_ROW, part(2 + j, P),
-               hq[3][0], hq[3][1], 0, slice(0, P), True, True)
-
-        def add_scatter(j, m, place):
+        def add_scatter(j, cols):
             nc.vector.tensor_tensor(
-                result[j][:].indirect(idx[:, part(m, P // 16)]), gated[:, place, :], base_late[:, place, :], ADD
+                result[j][:].indirect(idx[:, (2 * P + cols.start) // 16 : (2 * P + cols.stop) // 16]),
+                gated[:, j, cols],
+                base_late[:, j, cols],
+                ADD,
             )
 
-        add_scatter(0, 2, 0)
+        third_gate = gate_rows[:, part(0, P)].unsqueeze(1).to_broadcast([P, 2, P])
+        nc.vector.tensor_tensor(gated[:, :, part(0, P)], y_rows(0)[:], third_gate, MULT)
+        quantise(3)
+        copy_scatter(1, 0, back_rows, reuse("summed2", [P, 2 * P], F32, "h_bf3"))
+        add_scatter(0, part(0, P))
+        y_last = y_rows(1)
         for j in range(2):
-            nc.vector.tensor_tensor(gated[:, 1 + j, :], y_last[:, j, :], gate_rows[:, P : 2 * P], MULT)
-        for j in range(2):
-            add_scatter(j, 3, 1 + j)
-            nc.sync.dma_start(out[part(j, P), :], result[j][:])
+            nc.vector.tensor_tensor(gated[:, j, part(1, P)], y_last[:, j, :], gate_rows[:, part(1, P)], MULT)
+        add_scatter(0, part(1, P))
+        nc.sync.dma_start(out[part(0, P), :], result[0][:])
+        add_scatter(1, slice(0, 2 * P))
+        nc.sync.dma_start(out[part(1, P), :], result[1][:])

@@ -45,9 +45,9 @@ def tile_moe_dyl_none_kernel(
         def load_words(tile, words):
             nc.sync.dma_start(tile, words.rearrange("p n t -> p (n t)").bitcast(I32))
 
-        def load_scales(queue, tile, scales, first_row):
+        def load_scales(queue, tile, scales, first_row, sets=range(4)):
             rows = 4 * scales.shape[0]
-            for q in range(4):
+            for q in sets:
                 queue.dma_start(
                     tile[32 * q + first_row : 32 * q + first_row + rows, :].bitcast(I32),
                     scales[:, 4 * q : 4 * q + 4, :].bitcast(I32),
@@ -92,9 +92,11 @@ def tile_moe_dyl_none_kernel(
         nc.sync.dma_start(x_both[:], x_words.rearrange("s p n t -> p s (n t)").bitcast(I32))
         nc.sync.dma_start(w_w[:], w_words.rearrange("s p n t -> p s (n t)").bitcast(I32))
         nc.sync.dma_start(idx3[:], offs3)
-        load_scales(nc.sync, w_s, w_scales, W_ROW[0])
+        load_scales(nc.gpsimd, w_s, w_scales, W_ROW[0], range(1))
+        load_scales(nc.sync, w_s, w_scales, W_ROW[0], range(1, 4))
+        load_scales(nc.sync, wb_s, wb_scales, WB_ROW, range(1))
         load_words(wa_w[0][:], wa_words[0])
-        load_scales(nc.sync, wb_s, wb_scales, WB_ROW)
+        load_scales(nc.sync, wb_s, wb_scales, WB_ROW, range(1, 4))
         make_identity(nc, ident[:])
 
         xq_w = [sb("xq_w%d" % s, [P, SLOTS], U32) for s in range(2)]
@@ -116,12 +118,11 @@ def tile_moe_dyl_none_kernel(
                 waq_rows[raw + r : raw + 16 : 4, :].bitcast(I32),
             )
 
-        half = E * N // 2
-        for r in range(2):
+        half = E * N // 4
+        for r in range(3):
             move_rows(0, r)
         load_words(wa_w[1][:], wa_words[1])
-        for r in range(2, 4):
-            move_rows(0, r)
+        move_rows(0, 3)
         load_words(wb_w[:, 0:half], wb_words[0, :, 0:half])
         for r in range(4):
             move_rows(1, r)
@@ -151,21 +152,21 @@ def tile_moe_dyl_none_kernel(
         result = [sb("result%d" % j, [P, T], F32) for j in range(2)]
         for j in range(2):
             for half in range(2):
-                acc = bank("base_acc", [P, BANK], ("turn0", "turn1", "y0", "y1")[2 * j + half])
+                acc = bank("base_acc", [P, BANK], ("turn0", "turn1", "back0", "back1")[2 * j + half])
                 for s in range(2):
                     mm(acc[:], w_w[:, s, :], w_s, W_ROW[s], part(j, P),
                        x_w[s], x_s, X_ROW[s], part(half, BANK), s == 0, s == 1)
                 nc.scalar.copy(result[j][:, part(half, BANK)], acc[:])
 
         base_early = sb("base_early", [P, 2, N], F32)
-        acc = bank("slot_acc", [P, 2, N], "back0")
+        acc = bank("slot_acc", [P, 2, N], "turn0")
         for m in range(2):
             for s in range(2):
                 mm(acc[:, m, :], xq_w[s], xq_s, X_ROW[s], part(m, P),
                    w_w[:, s, :], w_s, W_ROW[s], slice(0, N), s == 0, s == 1)
         nc.scalar.copy(base_early[:], acc[:])
         base_late = sb("base_late", [P, 2, 2 * P], F32)
-        acc = bank("slot_acc", [P, 2, 2 * P], "back1")
+        acc = bank("slot_acc", [P, 2, 2 * P], "turn1")
         for j in range(2):
             for s in range(2):
                 mm(acc[:, j, :], w_w[:, s, :], w_s, W_ROW[s], part(j, P),
@@ -185,11 +186,12 @@ def tile_moe_dyl_none_kernel(
                 stop=s == 1,
             )
 
-        for m in range(2):
+        for m in range(B):
             h_acc[m] = bank("h_acc%d" % m, [P, H], "h%d" % m)
+        for m in range(3):
             h_pass(m, 0)
 
-        for m in range(2):
+        for m in range(3):
             gather_wa(m, 1, sb("waq_second%d" % m, [P, H], U32)[:])
         wbq_w = [sb("wbq_w0", [P, 2 * N], U32)]
         gather(wbq_w[0][:], wb_w[:].bitcast(U32), idx3, 0, 2 * N)
@@ -197,7 +199,7 @@ def tile_moe_dyl_none_kernel(
         grouped = {}
 
         def round_h(m):
-            h_bf = sb("h_bf%d" % m, [P, 2, P, 2], BF16)
+            h_bf = reuse("h_bf%d" % m, [P, 2, P, 2], BF16, ("h_bf0", "h_bf1", "h_bf0", "h_bf3")[m])
             nc.scalar.copy(h_bf[:], h_acc[m][:].rearrange("s (p u e) -> s u p e", u=2, e=2))
             return h_bf[:].rearrange("s u p e -> s (u p e)").bitcast(F32)
 
@@ -235,78 +237,69 @@ def tile_moe_dyl_none_kernel(
         def scatter(j, entry, count, values):
             nc.scalar.activation(result[j][:].indirect(idx[:, entry // 16 : (entry + count) // 16]), values, COPY)
 
-        for m in range(2):
+        for m in range(3):
             h_pass(m, 1)
             turn_h(m, round_h(m))
 
-        gather_wa(2, 1, reuse("waq_second2", [P, H], U32, "h_bf0")[:])
         quantise(0)
-        gather_wa(3, 0, reuse("waq_first3", [P, H], U32, "h_bf1")[:])
+        last = reuse("waq_last", [P, 2, H], U32, "grouped0")
+        for s in range(2):
+            gather_wa(3, s, last[:, s, :])
         quantise(1)
-        gather_wa(3, 1, reuse("waq_second3", [P, H], U32, "grouped0")[:])
-        wbq_s.append(reuse("wbq_s1", [P, 2 * N], U8, "grouped1"))
+        wbq_s.append(reuse("wbq_s1", [P, 2 * N], U8, "hq_w0"))
         gather(wbq_s[1][:], wb_s[:], idx3, 2 * N, 2 * N)
-        wbq_w.append(reuse("wbq_w1", [P, 2 * N], U32, "wa_w0"))
-        gather(wbq_w[1][:, 0:N], wb_w[:].bitcast(U32), idx3, 2 * N, N)
-
-        def sum_back(pieces, tag):
-            back = bank("back", [P, len(pieces), P], tag)
-            for place, (base, y) in enumerate(pieces):
-                turn_sum(back[:, place, :], base, y)
-            return back[:].rearrange("p b s -> p (b s)")
-
-        def copy_scatter(j, entry, back, summed):
-            nc.scalar.copy(summed[:], back)
-            scatter(j, entry, summed.shape[1], summed[:])
-
-        def early(m, j):
-            return base_early[:, m, part(j, P)], y_gated[m][:, part(j, P)]
-
-        y_gated = [gate_slots(0, part(0, N), N, "y0")]
-        copy_scatter(0, 0, sum_back([early(0, 0)], "back0"), sb("summed0", [P, P], F32))
-        y_gated.append(gate_slots(1, part(1, N), N, "y1"))
-        back_second = sum_back([early(1, 0)], "back0")
-        back_rows = sum_back([early(0, 1), early(1, 1)], "back1")
-
-        words = {}
-        for m in range(2, B):
-            h_acc[m] = bank("h_acc%d" % m, [P, H], "h%d" % (m - 2))
-            for s in range(2):
-                h_pass(m, s)
-            words[m] = round_h(m)
-            if m == 2:
-                turn_h(m, words[m])
-        copy_scatter(0, P, back_second, reuse("summed1", [P, P], F32, "grouped0"))
-        turn_h(3, words[3])
-
         quantise(2)
-        gather(wbq_w[1][:, N : 2 * N], wb_w[:].bitcast(U32), idx3, 3 * N, N)
+        wbq_w.append(reuse("wbq_w1", [P, 2 * N], U32, "hq_w1"))
+        for m in range(2, B):
+            gather(wbq_w[1][:, part(m - 2, N)], wb_w[:].bitcast(U32), idx3, m * N, N)
+
+        def sum_back(m):
+            y_gated = gate_slots(m, part(m, N), N, "h%d" % m)
+            back = bank("back", [P, 2, P], "back%d" % m)
+            for j in range(2):
+                turn_sum(back[:, j, :], base_early[:, m, part(j, P)], y_gated[:, part(j, P)])
+            return back
+
+        back_first = sum_back(0)
+        first = sb("summed0", [P, 2, P], F32)
+        nc.scalar.copy(first[:], back_first[:])
+        for j in range(2):
+            scatter(j, 0, P, first[:, j, :])
+        for s in range(2):
+            h_pass(3, s)
+        turn_h(3, round_h(3))
+        back_second = sum_back(1)
+
         gated = sb("gated", [P, 2, 2 * P], F32)
 
         def y_rows(mb):
-            acc = bank("y_rows", [P, 2, P], "h%d" % mb)
+            acc = bank("y_rows", [P, 2, P], "h%d" % (3 - mb))
             for j in range(2):
                 mm(acc[:, j, :], wbq_w[1], wbq_s[1], WB_ROW, part(2 * mb + j, P),
                    hq[2 + mb][0], hq[2 + mb][1], 0, slice(0, P), True, True)
             return acc
 
-        def add_scatter(j, cols):
+        def add_scatter(j, mb):
             nc.vector.tensor_tensor(
-                result[j][:].indirect(idx[:, (2 * P + cols.start) // 16 : (2 * P + cols.stop) // 16]),
-                gated[:, j, cols],
-                base_late[:, j, cols],
+                result[j][:].indirect(idx[:, part(2 + mb, P // 16)]),
+                gated[:, j, part(mb, P)],
+                base_late[:, j, part(mb, P)],
                 ADD,
             )
 
-        third_gate = gate_rows[:, part(0, P)].unsqueeze(1).to_broadcast([P, 2, P])
-        nc.vector.tensor_tensor(gated[:, :, part(0, P)], y_rows(0)[:], third_gate, MULT)
+        y_third = y_rows(0)
+        for j in range(2):
+            nc.vector.tensor_tensor(gated[:, j, part(0, P)], y_third[:, j, :], gate_rows[:, part(0, P)], MULT)
+        add_scatter(0, 0)
         quantise(3)
-        copy_scatter(1, 0, back_rows, reuse("summed2", [P, 2 * P], F32, "h_bf3"))
-        add_scatter(0, part(0, P))
+        add_scatter(1, 0)
+        held = reuse("summed1", [P, 2, P], F32, "h_bf3")
+        nc.scalar.copy(held[:], back_second[:])
+        for j in range(2):
+            scatter(j, P, P, held[:, j, :])
         y_last = y_rows(1)
         for j in range(2):
             nc.vector.tensor_tensor(gated[:, j, part(1, P)], y_last[:, j, :], gate_rows[:, part(1, P)], MULT)
-        add_scatter(0, part(1, P))
-        nc.sync.dma_start(out[part(0, P), :], result[0][:])
-        add_scatter(1, slice(0, 2 * P))
-        nc.sync.dma_start(out[part(1, P), :], result[1][:])
+        for j in range(2):
+            add_scatter(j, 1)
+            nc.sync.dma_start(out[part(j, P), :], result[j][:])

@@ -45,9 +45,9 @@ def tile_moe_dyl_none_kernel(
         def load_words(tile, words):
             nc.sync.dma_start(tile, words.rearrange("p n t -> p (n t)").bitcast(I32))
 
-        def load_scales(queue, tile, scales, first_row, sets=range(4)):
+        def load_scales(queue, tile, scales, first_row):
             rows = 4 * scales.shape[0]
-            for q in sets:
+            for q in range(4):
                 queue.dma_start(
                     tile[32 * q + first_row : 32 * q + first_row + rows, :].bitcast(I32),
                     scales[:, 4 * q : 4 * q + 4, :].bitcast(I32),
@@ -80,24 +80,22 @@ def tile_moe_dyl_none_kernel(
         waq_s = [sb("waq_s%d" % s, [P, B * H], U8) for s in range(2)]
         ident = sb("ident", [P, P], F32)
 
-        for tile in (x_s[:], wa_s[0:WA_RAW, :], wb_s[:]):
+        make_identity(nc, ident[:])
+        for tile in (x_s[:], wb_s[:], w_s[:], wa_s[0:WA_RAW, :]):
             nc.vector.memset(tile.bitcast(I32), 0)
 
-        wa_w = [sb("wa_w0", [P, E * H], I32), sb("wa_w1", [P, E * H], I32)]
-        wb_w = sb("wb_w", [P, E * N], I32)
         nc.sync.dma_start(wa_s[WA_RAW:P, :].bitcast(I32), wa_scales.rearrange("s b c -> (s b) c").bitcast(I32))
         nc.sync.dma_start(idx2[:], offs2)
-        load_scales(nc.sync, x_s, x_scales, X_ROW[0])
         nc.sync.dma_start(idx[:], offs)
+        load_scales(nc.scalar, x_s, x_scales, X_ROW[0])
         nc.sync.dma_start(x_both[:], x_words.rearrange("s p n t -> p s (n t)").bitcast(I32))
+        load_scales(nc.scalar, w_s, w_scales, W_ROW[0])
         nc.sync.dma_start(w_w[:], w_words.rearrange("s p n t -> p s (n t)").bitcast(I32))
+        wa_w = [sb("wa_w%d" % s, [P, E * H], I32) for s in range(2)]
+        for s in range(2):
+            load_words(wa_w[s][:], wa_words[s])
         nc.sync.dma_start(idx3[:], offs3)
-        load_scales(nc.gpsimd, w_s, w_scales, W_ROW[0], range(1))
-        load_scales(nc.sync, w_s, w_scales, W_ROW[0], range(1, 4))
-        load_scales(nc.sync, wb_s, wb_scales, WB_ROW, range(1))
-        load_words(wa_w[0][:], wa_words[0])
-        load_scales(nc.sync, wb_s, wb_scales, WB_ROW, range(1, 4))
-        make_identity(nc, ident[:])
+        load_scales(nc.gpsimd, wb_s, wb_scales, WB_ROW)
 
         xq_w = [sb("xq_w%d" % s, [P, SLOTS], U32) for s in range(2)]
         xq_s = sb("xq_s", [P, SLOTS], U8)
@@ -111,22 +109,13 @@ def tile_moe_dyl_none_kernel(
 
         gather(waq_rows[:], wa_s[:], idx2, 0, B * H)
 
-        def move_rows(s, r):
-            raw = WA_RAW + 16 * s
-            nc.sync.dma_start(
-                waq_s[s][WA_ROW[s] + r : P : 32, :].bitcast(I32),
-                waq_rows[raw + r : raw + 16 : 4, :].bitcast(I32),
-            )
-
-        half = E * N // 4
-        for r in range(3):
-            move_rows(0, r)
-        load_words(wa_w[1][:], wa_words[1])
-        move_rows(0, 3)
-        load_words(wb_w[:, 0:half], wb_words[0, :, 0:half])
-        for r in range(4):
-            move_rows(1, r)
-        load_words(wb_w[:, half:], wb_words[0, :, half:])
+        for s in range(2):
+            for r in range(4):
+                raw = WA_RAW + 16 * s
+                (nc.scalar, nc.sync)[s].dma_start(
+                    waq_s[s][WA_ROW[s] + r : P : 32, :].bitcast(I32),
+                    waq_rows[raw + r : raw + 16 : 4, :].bitcast(I32),
+                )
 
         gate_rows = sb("gate_rows", [P, 2 * P], F32)
         gate_col = sb("gate_col", [P, 2], F32)
@@ -144,10 +133,10 @@ def tile_moe_dyl_none_kernel(
             waq_w[m, s] = tile
             gather(tile, wa_w[s][:].bitcast(U32), idx2, m * H, H)
 
-        for m in range(3):
-            gather_wa(m, 0, sb("waq_first%d" % m, [P, H], U32)[:])
-        wbq_s = [sb("wbq_s0", [P, 2 * N], U8)]
-        gather(wbq_s[0][:], wb_s[:], idx3, 0, 2 * N)
+        waq_first = sb("waq_first", [P, B * H], U32)
+        gather(waq_first[:], wa_w[0][:].bitcast(U32), idx2, 0, B * H)
+        for m in range(B):
+            waq_w[m, 0] = waq_first[:, part(m, H)]
 
         result = [sb("result%d" % j, [P, T], F32) for j in range(2)]
         for j in range(2):
@@ -188,18 +177,22 @@ def tile_moe_dyl_none_kernel(
 
         for m in range(B):
             h_acc[m] = bank("h_acc%d" % m, [P, H], "h%d" % m)
-        for m in range(3):
             h_pass(m, 0)
 
-        for m in range(3):
+        wb_w = reuse("wb_w", [P, E * N], I32, "wa_w0")
+        nc.scalar.dma_start(wb_w[:], wb_words[0].rearrange("p n t -> p (n t)").bitcast(I32))
+
+        for m in range(B):
             gather_wa(m, 1, sb("waq_second%d" % m, [P, H], U32)[:])
+        wbq_s = [sb("wbq_s0", [P, 2 * N], U8)]
+        gather(wbq_s[0][:], wb_s[:], idx3, 0, 2 * N)
         wbq_w = [sb("wbq_w0", [P, 2 * N], U32)]
         gather(wbq_w[0][:], wb_w[:].bitcast(U32), idx3, 0, 2 * N)
 
         grouped = {}
 
         def round_h(m):
-            h_bf = reuse("h_bf%d" % m, [P, 2, P, 2], BF16, ("h_bf0", "h_bf1", "h_bf0", "h_bf3")[m])
+            h_bf = reuse("h_bf%d" % m, [P, 2, P, 2], BF16, "h_bf%d" % (m % 2))
             nc.scalar.copy(h_bf[:], h_acc[m][:].rearrange("s (p u e) -> s u p e", u=2, e=2))
             return h_bf[:].rearrange("s u p e -> s (u p e)").bitcast(F32)
 
@@ -237,69 +230,54 @@ def tile_moe_dyl_none_kernel(
         def scatter(j, entry, count, values):
             nc.scalar.activation(result[j][:].indirect(idx[:, entry // 16 : (entry + count) // 16]), values, COPY)
 
-        for m in range(3):
+        for m in range(B):
             h_pass(m, 1)
             turn_h(m, round_h(m))
 
-        quantise(0)
-        last = reuse("waq_last", [P, 2, H], U32, "grouped0")
-        for s in range(2):
-            gather_wa(3, s, last[:, s, :])
-        quantise(1)
-        wbq_s.append(reuse("wbq_s1", [P, 2 * N], U8, "hq_w0"))
+        for m in range(2):
+            quantise(m)
+        wbq_s.append(reuse("wbq_s1", [P, 2 * N], U8, "grouped1"))
         gather(wbq_s[1][:], wb_s[:], idx3, 2 * N, 2 * N)
-        quantise(2)
-        wbq_w.append(reuse("wbq_w1", [P, 2 * N], U32, "hq_w1"))
+        for m in range(2, B):
+            quantise(m)
+        wbq_w.append(reuse("wbq_w1", [P, 2 * N], U32, "grouped2"))
         for m in range(2, B):
             gather(wbq_w[1][:, part(m - 2, N)], wb_w[:].bitcast(U32), idx3, m * N, N)
 
-        def sum_back(m):
+        summed = []
+        for m in range(2):
             y_gated = gate_slots(m, part(m, N), N, "h%d" % m)
             back = bank("back", [P, 2, P], "back%d" % m)
             for j in range(2):
                 turn_sum(back[:, j, :], base_early[:, m, part(j, P)], y_gated[:, part(j, P)])
-            return back
-
-        back_first = sum_back(0)
-        first = sb("summed0", [P, 2, P], F32)
-        nc.scalar.copy(first[:], back_first[:])
-        for j in range(2):
-            scatter(j, 0, P, first[:, j, :])
-        for s in range(2):
-            h_pass(3, s)
-        turn_h(3, round_h(3))
-        back_second = sum_back(1)
+            summed.append(sb("summed%d" % m, [P, 2, P], F32))
+            nc.scalar.copy(summed[m][:], back[:])
+            scatter(0, m * P, P, summed[m][:, 0, :])
 
         gated = sb("gated", [P, 2, 2 * P], F32)
 
-        def y_rows(mb):
-            acc = bank("y_rows", [P, 2, P], "h%d" % (3 - mb))
+        def gate_rows_of(mb):
+            acc = bank("y_rows", [P, 2, P], "h%d" % (2 + mb))
             for j in range(2):
                 mm(acc[:, j, :], wbq_w[1], wbq_s[1], WB_ROW, part(2 * mb + j, P),
                    hq[2 + mb][0], hq[2 + mb][1], 0, slice(0, P), True, True)
-            return acc
+            for j in (1, 0):
+                nc.vector.tensor_tensor(gated[:, j, part(mb, P)], acc[:, j, :], gate_rows[:, part(mb, P)], MULT)
 
-        def add_scatter(j, mb):
+        def add_scatter(j, first, count):
             nc.vector.tensor_tensor(
-                result[j][:].indirect(idx[:, part(2 + mb, P // 16)]),
-                gated[:, j, part(mb, P)],
-                base_late[:, j, part(mb, P)],
+                result[j][:].indirect(idx[:, (2 + first) * P // 16 : (2 + first + count) * P // 16]),
+                gated[:, j, first * P : (first + count) * P],
+                base_late[:, j, first * P : (first + count) * P],
                 ADD,
             )
 
-        y_third = y_rows(0)
-        for j in range(2):
-            nc.vector.tensor_tensor(gated[:, j, part(0, P)], y_third[:, j, :], gate_rows[:, part(0, P)], MULT)
-        add_scatter(0, 0)
-        quantise(3)
-        add_scatter(1, 0)
-        held = reuse("summed1", [P, 2, P], F32, "h_bf3")
-        nc.scalar.copy(held[:], back_second[:])
-        for j in range(2):
-            scatter(j, P, P, held[:, j, :])
-        y_last = y_rows(1)
-        for j in range(2):
-            nc.vector.tensor_tensor(gated[:, j, part(1, P)], y_last[:, j, :], gate_rows[:, part(1, P)], MULT)
-        for j in range(2):
-            add_scatter(j, 1)
-            nc.sync.dma_start(out[part(j, P), :], result[j][:])
+        gate_rows_of(0)
+        add_scatter(1, 0, 1)
+        for m in range(2):
+            scatter(1, m * P, P, summed[m][:, 1, :])
+        gate_rows_of(1)
+        add_scatter(0, 0, 2)
+        nc.sync.dma_start(out[part(0, P), :], result[0][:])
+        add_scatter(1, 1, 1)
+        nc.sync.dma_start(out[part(1, P), :], result[1][:])

@@ -1,7 +1,6 @@
 from contextlib import ExitStack
 
 import concourse.mybir as mybir
-from concourse.masks import make_identity
 
 K, T, E, B, H, N = 1024, 1024, 8, 4, 512, 256
 P = 128
@@ -19,6 +18,8 @@ FP8X4 = mybir.dt.float8_e4m3fn_x4
 MULT = mybir.AluOpType.mult
 ADD = mybir.AluOpType.add
 COPY = mybir.ActivationFunctionType.Copy
+
+BANKS = ("h0", "h1", "h2", "h3", "turn0", "turn1", "back0", "back1")
 
 X_ROW = (0, 4)
 W_ROW = (0, 4)
@@ -45,9 +46,9 @@ def tile_moe_dyl_none_kernel(
         def load_words(tile, words):
             nc.sync.dma_start(tile, words.rearrange("p n t -> p (n t)").bitcast(I32))
 
-        def load_scales(queue, tile, scales, first_row):
+        def load_scales(queue, tile, scales, first_row, sets=range(4)):
             rows = 4 * scales.shape[0]
-            for q in range(4):
+            for q in sets:
                 queue.dma_start(
                     tile[32 * q + first_row : 32 * q + first_row + rows, :].bitcast(I32),
                     scales[:, 4 * q : 4 * q + 4, :].bitcast(I32),
@@ -80,20 +81,23 @@ def tile_moe_dyl_none_kernel(
         waq_s = [sb("waq_s%d" % s, [P, B * H], U8) for s in range(2)]
         ident = sb("ident", [P, P], F32)
 
-        make_identity(nc, ident[:])
-        for tile in (x_s[:], wb_s[:], w_s[:], wa_s[0:WA_RAW, :]):
+        offset = sb("offset", [P, P], I32)
+        nc.gpsimd.iota(offset[:], [[1, P]], base=0, channel_multiplier=-1)
+        for tile in (x_s[:], wa_s[0:WA_RAW, :], wb_s[:]):
             nc.vector.memset(tile.bitcast(I32), 0)
+        nc.vector.tensor_scalar(ident[:], offset[:], 0, None, mybir.AluOpType.is_equal)
 
         nc.sync.dma_start(wa_s[WA_RAW:P, :].bitcast(I32), wa_scales.rearrange("s b c -> (s b) c").bitcast(I32))
         nc.sync.dma_start(idx2[:], offs2)
-        nc.sync.dma_start(idx[:], offs)
+        load_scales(nc.gpsimd, w_s, w_scales, W_ROW[0], range(3))
+        load_scales(nc.scalar, w_s, w_scales, W_ROW[0], range(3, 4))
         load_scales(nc.scalar, x_s, x_scales, X_ROW[0])
         nc.sync.dma_start(x_both[:], x_words.rearrange("s p n t -> p s (n t)").bitcast(I32))
-        load_scales(nc.scalar, w_s, w_scales, W_ROW[0])
-        nc.sync.dma_start(w_w[:], w_words.rearrange("s p n t -> p s (n t)").bitcast(I32))
+        nc.sync.dma_start(idx[:], offs)
         wa_w = [sb("wa_w%d" % s, [P, E * H], I32) for s in range(2)]
-        for s in range(2):
-            load_words(wa_w[s][:], wa_words[s])
+        load_words(wa_w[0][:], wa_words[0])
+        nc.sync.dma_start(w_w[:], w_words.rearrange("s p n t -> p s (n t)").bitcast(I32))
+        load_words(wa_w[1][:], wa_words[1])
         nc.sync.dma_start(idx3[:], offs3)
         load_scales(nc.gpsimd, wb_s, wb_scales, WB_ROW)
 
@@ -105,7 +109,7 @@ def tile_moe_dyl_none_kernel(
             return keep.tile(shape, dtype, name=name, tag=tag, align_bytes=64)
 
         def bank(name, shape, tag):
-            return psum.tile(shape, F32, name=name, tag=tag)
+            return psum.tile(shape, F32, name=name + "_" + tag, offset=4 * BANK * BANKS.index(tag))
 
         gather(waq_rows[:], wa_s[:], idx2, 0, B * H)
 
@@ -116,6 +120,9 @@ def tile_moe_dyl_none_kernel(
                     waq_s[s][WA_ROW[s] + r : P : 32, :].bitcast(I32),
                     waq_rows[raw + r : raw + 16 : 4, :].bitcast(I32),
                 )
+
+        wb_w = sb("wb_w", [P, E * N], I32)
+        load_words(wb_w[:], wb_words[0])
 
         gate_rows = sb("gate_rows", [P, 2 * P], F32)
         gate_col = sb("gate_col", [P, 2], F32)
@@ -141,7 +148,7 @@ def tile_moe_dyl_none_kernel(
         result = [sb("result%d" % j, [P, T], F32) for j in range(2)]
         for j in range(2):
             for half in range(2):
-                acc = bank("base_acc", [P, BANK], ("turn0", "turn1", "back0", "back1")[2 * j + half])
+                acc = bank("base_acc", [P, BANK], "h%d" % (2 * j + half))
                 for s in range(2):
                     mm(acc[:], w_w[:, s, :], w_s, W_ROW[s], part(j, P),
                        x_w[s], x_s, X_ROW[s], part(half, BANK), s == 0, s == 1)
@@ -178,9 +185,6 @@ def tile_moe_dyl_none_kernel(
         for m in range(B):
             h_acc[m] = bank("h_acc%d" % m, [P, H], "h%d" % m)
             h_pass(m, 0)
-
-        wb_w = reuse("wb_w", [P, E * N], I32, "wa_w0")
-        nc.scalar.dma_start(wb_w[:], wb_words[0].rearrange("p n t -> p (n t)").bitcast(I32))
 
         for m in range(B):
             gather_wa(m, 1, sb("waq_second%d" % m, [P, H], U32)[:])

@@ -82,6 +82,7 @@ def tile_moe_dyl_none_kernel(
         ident = sb("ident", [P, P], F32)
 
         offset = sb("offset", [P, P], I32)
+        load_scales(nc.gpsimd, w_s, w_scales, W_ROW[0], range(3))
         nc.gpsimd.iota(offset[:], [[1, P]], base=0, channel_multiplier=-1)
         for tile in (x_s[:], wa_s[0:WA_RAW, :], wb_s[:]):
             nc.vector.memset(tile.bitcast(I32), 0)
@@ -89,7 +90,6 @@ def tile_moe_dyl_none_kernel(
 
         nc.sync.dma_start(wa_s[WA_RAW:P, :].bitcast(I32), wa_scales.rearrange("s b c -> (s b) c").bitcast(I32))
         nc.sync.dma_start(idx2[:], offs2)
-        load_scales(nc.gpsimd, w_s, w_scales, W_ROW[0], range(3))
         load_scales(nc.scalar, w_s, w_scales, W_ROW[0], range(3, 4))
         load_scales(nc.scalar, x_s, x_scales, X_ROW[0])
         nc.sync.dma_start(x_both[:], x_words.rearrange("s p n t -> p s (n t)").bitcast(I32))
@@ -124,11 +124,11 @@ def tile_moe_dyl_none_kernel(
         wb_w = sb("wb_w", [P, E * N], I32)
         load_words(wb_w[:], wb_words[0])
 
-        gate_rows = sb("gate_rows", [P, 2 * P], F32)
+        gate_rows = sb("gate_rows", [P, 3 * P], F32)
         gate_col = sb("gate_col", [P, 2], F32)
         with nc.allow_non_contiguous_dma(reason="one gate value a partition and block"):
             nc.sync.dma_start(gate_col[:], gate[0, 0 : 2 * P].rearrange("(b p) -> p b", p=P))
-        nc.sync.dma_start(gate_rows[:], gate[:, 2 * P : SLOTS])
+        nc.sync.dma_start(gate_rows[:], gate[:, P:SLOTS])
 
         gather(xq_s[:], x_s[:], idx, 0, SLOTS)
         for s in range(2):
@@ -154,12 +154,17 @@ def tile_moe_dyl_none_kernel(
                        x_w[s], x_s, X_ROW[s], part(half, BANK), s == 0, s == 1)
                 nc.scalar.copy(result[j][:, part(half, BANK)], acc[:])
 
-        base_early = sb("base_early", [P, 2, N], F32)
-        acc = bank("slot_acc", [P, 2, N], "turn0")
-        for m in range(2):
-            for s in range(2):
-                mm(acc[:, m, :], xq_w[s], xq_s, X_ROW[s], part(m, P),
-                   w_w[:, s, :], w_s, W_ROW[s], slice(0, N), s == 0, s == 1)
+        base_early = sb("base_early", [P, 4, P], F32)
+        acc = bank("slot_acc", [P, 4, P], "turn0")
+        for s in range(2):
+            mm(acc[:, 0:2, :].rearrange("p j n -> p (j n)"), xq_w[s], xq_s, X_ROW[s], part(0, P),
+               w_w[:, s, :], w_s, W_ROW[s], slice(0, N), s == 0, s == 1)
+        for s in range(2):
+            mm(acc[:, 2, :], xq_w[s], xq_s, X_ROW[s], part(1, P),
+               w_w[:, s, :], w_s, W_ROW[s], part(0, P), s == 0, s == 1)
+        for s in range(2):
+            mm(acc[:, 3, :], w_w[:, s, :], w_s, W_ROW[s], part(1, P),
+               xq_w[s], xq_s, X_ROW[s], part(1, P), s == 0, s == 1)
         nc.scalar.copy(base_early[:], acc[:])
         base_late = sb("base_late", [P, 2, 2 * P], F32)
         acc = bank("slot_acc", [P, 2, 2 * P], "turn1")
@@ -204,7 +209,7 @@ def tile_moe_dyl_none_kernel(
             turned = bank("turned", [P, 2, P], "turn%d" % (m % 2))
             for u in range(2):
                 nc.tensor.transpose(turned[:, u, :], h_words[:, part(u, P)], ident[:])
-            grouped[m] = sb("grouped%d" % m, [P, P, 2], F32)
+            grouped[m] = reuse("grouped%d" % m, [P, P, 2], F32, "hq_s0" if m == 3 else "grouped%d" % m)
             nc.scalar.copy(grouped[m][:], turned[:].rearrange("p u s -> p s u"))
 
         hq = {}
@@ -227,19 +232,30 @@ def tile_moe_dyl_none_kernel(
             nc.scalar.activation(y_gated[:], y_slots[:], COPY, scale=gate_col[:, m : m + 1])
             return y_gated
 
-        def turn_sum(acc, first, second):
-            nc.tensor.matmul(acc, first, ident[:], start=True, stop=False, is_transpose=True)
-            nc.tensor.matmul(acc, second, ident[:], start=False, stop=True, is_transpose=True)
-
         def scatter(j, entry, count, values):
             nc.scalar.activation(result[j][:].indirect(idx[:, entry // 16 : (entry + count) // 16]), values, COPY)
 
         for m in range(B):
             h_pass(m, 1)
-            turn_h(m, round_h(m))
+            words = round_h(m)
+            if m < 3:
+                turn_h(m, words)
 
-        for m in range(2):
-            quantise(m)
+        def sum_back(m, base, y_gated):
+            tiles = y_gated.shape[1] // P
+            back = bank("back", [P, tiles, P], "back%d" % m)
+            for step, source in enumerate((base, y_gated[:])):
+                for j in range(tiles):
+                    nc.tensor.matmul(back[:, j, :], source[:, part(j, P)], ident[:], is_transpose=True,
+                                     start=step == 0 and j == 0, stop=step == 1 and j == tiles - 1)
+            return back
+
+        quantise(0)
+        first_gated = gate_slots(0, slice(0, N), N, "h0")
+        turn_h(3, words)
+        back_first = sum_back(0, base_early[:, 0:2, :].rearrange("p j n -> p (j n)"), first_gated)
+        quantise(1)
+        back_second = sum_back(1, base_early[:, 2, :], gate_slots(1, slice(N, N + P), P, "h0"))
         wbq_s.append(reuse("wbq_s1", [P, 2 * N], U8, "grouped1"))
         gather(wbq_s[1][:], wb_s[:], idx3, 2 * N, 2 * N)
         for m in range(2, B):
@@ -248,40 +264,37 @@ def tile_moe_dyl_none_kernel(
         for m in range(2, B):
             gather(wbq_w[1][:, part(m - 2, N)], wb_w[:].bitcast(U32), idx3, m * N, N)
 
-        summed = []
-        for m in range(2):
-            y_gated = gate_slots(m, part(m, N), N, "h%d" % m)
-            back = bank("back", [P, 2, P], "back%d" % m)
-            for j in range(2):
-                turn_sum(back[:, j, :], base_early[:, m, part(j, P)], y_gated[:, part(j, P)])
-            summed.append(sb("summed%d" % m, [P, 2, P], F32))
-            nc.scalar.copy(summed[m][:], back[:])
-            scatter(0, m * P, P, summed[m][:, 0, :])
+        first = sb("summed0", [P, 2, P], F32)
+        nc.scalar.copy(first[:], back_first[:])
+        scatter(0, 0, P, first[:, 0, :])
+        second = sb("summed1", [P, P], F32)
+        nc.scalar.copy(second[:], back_second[:, 0, :])
+        scatter(0, P, P, second[:])
 
-        gated = sb("gated", [P, 2, 2 * P], F32)
+        def gate_rows_of(m, tiles, tag):
+            acc = bank("y_rows", [P, 2, P], tag)
+            for j in tiles:
+                mm(acc[:, j, :], wbq_w[m // 2], wbq_s[m // 2], WB_ROW, part(2 * (m % 2) + j, P),
+                   hq[m][0], hq[m][1], 0, slice(0, P), True, True)
+            for j in tiles:
+                nc.vector.tensor_tensor(gated[:, j, part(m - 1, P)], acc[:, j, :], gate_rows[:, part(m - 1, P)], MULT)
 
-        def gate_rows_of(mb):
-            acc = bank("y_rows", [P, 2, P], "h%d" % (2 + mb))
-            for j in range(2):
-                mm(acc[:, j, :], wbq_w[1], wbq_s[1], WB_ROW, part(2 * mb + j, P),
-                   hq[2 + mb][0], hq[2 + mb][1], 0, slice(0, P), True, True)
-            for j in (1, 0):
-                nc.vector.tensor_tensor(gated[:, j, part(mb, P)], acc[:, j, :], gate_rows[:, part(mb, P)], MULT)
-
-        def add_scatter(j, first, count):
+        def add_scatter(j, first, count, base):
             nc.vector.tensor_tensor(
-                result[j][:].indirect(idx[:, (2 + first) * P // 16 : (2 + first + count) * P // 16]),
-                gated[:, j, first * P : (first + count) * P],
-                base_late[:, j, first * P : (first + count) * P],
+                result[j][:].indirect(idx[:, first * P // 16 : (first + count) * P // 16]),
+                gated[:, j, (first - 1) * P : (first - 1 + count) * P],
+                base,
                 ADD,
             )
 
-        gate_rows_of(0)
-        add_scatter(1, 0, 1)
-        for m in range(2):
-            scatter(1, m * P, P, summed[m][:, 1, :])
-        gate_rows_of(1)
-        add_scatter(0, 0, 2)
+        gated = reuse("gated", [P, 2, 3 * P], F32, "wb_w")
+        gate_rows_of(1, [1], "h1")
+        gate_rows_of(2, [1, 0], "h0")
+        add_scatter(1, 1, 1, base_early[:, 3, :])
+        add_scatter(1, 2, 1, base_late[:, 1, part(0, P)])
+        scatter(1, 0, P, first[:, 1, :])
+        gate_rows_of(3, [0, 1], "back0")
+        add_scatter(0, 2, 2, base_late[:, 0, :])
         nc.sync.dma_start(out[part(0, P), :], result[0][:])
-        add_scatter(1, 1, 1)
+        add_scatter(1, 3, 1, base_late[:, 1, part(1, P)])
         nc.sync.dma_start(out[part(1, P), :], result[1][:])

@@ -99,6 +99,9 @@ def tile_moe_dyl_none_kernel(
         nc.sync.dma_start(w_w[:], w_words.rearrange("s p n t -> p s (n t)").bitcast(I32))
         load_words(wa_w[1][:], wa_words[1])
         nc.sync.dma_start(idx3[:], offs3)
+        wb_w = sb("wb_w", [P, E * N], I32)
+        ahead = 3 * E * N // 4
+        load_words(wb_w[:, 0:ahead], wb_words[0, :, 0:ahead])
         load_scales(nc.gpsimd, wb_s, wb_scales, WB_ROW)
 
         xq_w = [sb("xq_w%d" % s, [P, SLOTS], U32) for s in range(2)]
@@ -121,14 +124,13 @@ def tile_moe_dyl_none_kernel(
                     waq_rows[raw + r : raw + 16 : 4, :].bitcast(I32),
                 )
 
-        wb_w = sb("wb_w", [P, E * N], I32)
-        load_words(wb_w[:], wb_words[0])
+        load_words(wb_w[:, ahead:], wb_words[0, :, ahead:])
 
-        gate_rows = sb("gate_rows", [P, 3 * P], F32)
+        gate_rows = sb("gate_rows", [P, 2 * P], F32)
         gate_col = sb("gate_col", [P, 2], F32)
         with nc.allow_non_contiguous_dma(reason="one gate value a partition and block"):
             nc.sync.dma_start(gate_col[:], gate[0, 0 : 2 * P].rearrange("(b p) -> p b", p=P))
-        nc.sync.dma_start(gate_rows[:], gate[:, P:SLOTS])
+        nc.sync.dma_start(gate_rows[:], gate[:, 2 * P : SLOTS])
 
         gather(xq_s[:], x_s[:], idx, 0, SLOTS)
         for s in range(2):
@@ -154,17 +156,12 @@ def tile_moe_dyl_none_kernel(
                        x_w[s], x_s, X_ROW[s], part(half, BANK), s == 0, s == 1)
                 nc.scalar.copy(result[j][:, part(half, BANK)], acc[:])
 
-        base_early = sb("base_early", [P, 4, P], F32)
-        acc = bank("slot_acc", [P, 4, P], "turn0")
-        for s in range(2):
-            mm(acc[:, 0:2, :].rearrange("p j n -> p (j n)"), xq_w[s], xq_s, X_ROW[s], part(0, P),
-               w_w[:, s, :], w_s, W_ROW[s], slice(0, N), s == 0, s == 1)
-        for s in range(2):
-            mm(acc[:, 2, :], xq_w[s], xq_s, X_ROW[s], part(1, P),
-               w_w[:, s, :], w_s, W_ROW[s], part(0, P), s == 0, s == 1)
-        for s in range(2):
-            mm(acc[:, 3, :], w_w[:, s, :], w_s, W_ROW[s], part(1, P),
-               xq_w[s], xq_s, X_ROW[s], part(1, P), s == 0, s == 1)
+        base_early = sb("base_early", [P, 2, N], F32)
+        acc = bank("slot_acc", [P, 2, N], "turn0")
+        for m in range(2):
+            for s in range(2):
+                mm(acc[:, m, :], xq_w[s], xq_s, X_ROW[s], part(m, P),
+                   w_w[:, s, :], w_s, W_ROW[s], slice(0, N), s == 0, s == 1)
         nc.scalar.copy(base_early[:], acc[:])
         base_late = sb("base_late", [P, 2, 2 * P], F32)
         acc = bank("slot_acc", [P, 2, 2 * P], "turn1")
@@ -253,9 +250,9 @@ def tile_moe_dyl_none_kernel(
         quantise(0)
         first_gated = gate_slots(0, slice(0, N), N, "h0")
         turn_h(3, words)
-        back_first = sum_back(0, base_early[:, 0:2, :].rearrange("p j n -> p (j n)"), first_gated)
+        back_first = sum_back(0, base_early[:, 0, :], first_gated)
         quantise(1)
-        back_second = sum_back(1, base_early[:, 2, :], gate_slots(1, slice(N, N + P), P, "h0"))
+        back_second = sum_back(1, base_early[:, 1, :], gate_slots(1, part(1, N), N, "h1"))
         wbq_s.append(reuse("wbq_s1", [P, 2 * N], U8, "grouped1"))
         gather(wbq_s[1][:], wb_s[:], idx3, 2 * N, 2 * N)
         for m in range(2, B):
@@ -264,37 +261,35 @@ def tile_moe_dyl_none_kernel(
         for m in range(2, B):
             gather(wbq_w[1][:, part(m - 2, N)], wb_w[:].bitcast(U32), idx3, m * N, N)
 
-        first = sb("summed0", [P, 2, P], F32)
-        nc.scalar.copy(first[:], back_first[:])
-        scatter(0, 0, P, first[:, 0, :])
-        second = sb("summed1", [P, P], F32)
-        nc.scalar.copy(second[:], back_second[:, 0, :])
-        scatter(0, P, P, second[:])
+        summed = sb("summed", [P, 2, 2 * P], F32)
+        for m, back in enumerate((back_first, back_second)):
+            nc.scalar.copy(summed[:, :, part(m, P)], back[:])
+            scatter(0, m * P, P, summed[:, 0, part(m, P)])
 
-        def gate_rows_of(m, tiles, tag):
+        gated = sb("gated", [P, 2, 2 * P], F32)
+
+        def gate_rows_of(mb, tiles, tag):
             acc = bank("y_rows", [P, 2, P], tag)
             for j in tiles:
-                mm(acc[:, j, :], wbq_w[m // 2], wbq_s[m // 2], WB_ROW, part(2 * (m % 2) + j, P),
-                   hq[m][0], hq[m][1], 0, slice(0, P), True, True)
+                mm(acc[:, j, :], wbq_w[1], wbq_s[1], WB_ROW, part(2 * mb + j, P),
+                   hq[2 + mb][0], hq[2 + mb][1], 0, slice(0, P), True, True)
             for j in tiles:
-                nc.vector.tensor_tensor(gated[:, j, part(m - 1, P)], acc[:, j, :], gate_rows[:, part(m - 1, P)], MULT)
+                nc.vector.tensor_tensor(gated[:, j, part(mb, P)], acc[:, j, :], gate_rows[:, part(mb, P)], MULT)
 
-        def add_scatter(j, first, count, base):
+        def add_scatter(j, first, count):
+            cols = slice(first * P, (first + count) * P)
             nc.vector.tensor_tensor(
-                result[j][:].indirect(idx[:, first * P // 16 : (first + count) * P // 16]),
-                gated[:, j, (first - 1) * P : (first - 1 + count) * P],
-                base,
+                result[j][:].indirect(idx[:, (2 + first) * P // 16 : (2 + first + count) * P // 16]),
+                gated[:, j, cols],
+                base_late[:, j, cols],
                 ADD,
             )
 
-        gated = reuse("gated", [P, 2, 3 * P], F32, "wb_w")
-        gate_rows_of(1, [1], "h1")
-        gate_rows_of(2, [1, 0], "h0")
-        add_scatter(1, 1, 1, base_early[:, 3, :])
-        add_scatter(1, 2, 1, base_late[:, 1, part(0, P)])
-        scatter(1, 0, P, first[:, 1, :])
-        gate_rows_of(3, [0, 1], "back0")
-        add_scatter(0, 2, 2, base_late[:, 0, :])
+        gate_rows_of(0, [1, 0], "h1")
+        add_scatter(1, 0, 1)
+        scatter(1, 0, 2 * P, summed[:, 1, :])
+        gate_rows_of(1, [0, 1], "back0")
+        add_scatter(0, 0, 2)
         nc.sync.dma_start(out[part(0, P), :], result[0][:])
-        add_scatter(1, 3, 1, base_late[:, 1, part(1, P)])
+        add_scatter(1, 1, 1)
         nc.sync.dma_start(out[part(1, P), :], result[1][:])

@@ -100,7 +100,7 @@ def tile_moe_dyl_none_kernel(
         load_words(wa_w[1][:], wa_words[1])
         nc.sync.dma_start(idx3[:], offs3)
         wb_w = sb("wb_w", [P, E * N], I32)
-        ahead = 3 * E * N // 4
+        ahead = E * N // 4
         load_words(wb_w[:, 0:ahead], wb_words[0, :, 0:ahead])
         load_scales(nc.gpsimd, wb_s, wb_scales, WB_ROW)
 
@@ -264,7 +264,7 @@ def tile_moe_dyl_none_kernel(
         summed = sb("summed", [P, 2, 2 * P], F32)
         for m, back in enumerate((back_first, back_second)):
             nc.scalar.copy(summed[:, :, part(m, P)], back[:])
-            scatter(0, m * P, P, summed[:, 0, part(m, P)])
+        scatter(0, 0, 2 * P, summed[:, 0, :])
 
         gated = sb("gated", [P, 2, 2 * P], F32)
 

@@ -28,6 +28,8 @@ WB_ROW = 8
 
 WA_RAW = 96
 
+WB_AHEAD = E * N // 4
+
 
 def tile_moe_dyl_none_kernel(
     tc, x_words, x_scales, w_words, w_scales, wa_words, wa_scales, wb_words, wb_scales, gate, offs, offs2, offs3, out
@@ -39,6 +41,12 @@ def tile_moe_dyl_none_kernel(
 
         def sb(name, shape, dtype):
             return keep.tile(shape, dtype, name=name, align_bytes=64)
+
+        def reuse(name, shape, dtype, tag):
+            return keep.tile(shape, dtype, name=name, tag=tag, align_bytes=64)
+
+        def bank(name, shape, tag):
+            return psum.tile(shape, F32, name=name + "_" + tag, offset=4 * BANK * BANKS.index(tag))
 
         def part(index, width):
             return slice(index * width, (index + 1) * width)
@@ -81,12 +89,12 @@ def tile_moe_dyl_none_kernel(
         waq_s = [sb("waq_s%d" % s, [P, B * H], U8) for s in range(2)]
         ident = sb("ident", [P, P], F32)
 
-        offset = sb("offset", [P, P], I32)
+        diagonal = sb("offset", [P, P], I32)
+        nc.gpsimd.iota(diagonal[:], [[1, P]], base=0, channel_multiplier=-1)
         load_scales(nc.gpsimd, w_s, w_scales, W_ROW[0], range(3))
-        nc.gpsimd.iota(offset[:], [[1, P]], base=0, channel_multiplier=-1)
         for tile in (x_s[:], wa_s[0:WA_RAW, :], wb_s[:]):
             nc.vector.memset(tile.bitcast(I32), 0)
-        nc.vector.tensor_scalar(ident[:], offset[:], 0, None, mybir.AluOpType.is_equal)
+        nc.vector.tensor_scalar(ident[:], diagonal[:], 0, None, mybir.AluOpType.is_equal)
 
         nc.sync.dma_start(wa_s[WA_RAW:P, :].bitcast(I32), wa_scales.rearrange("s b c -> (s b) c").bitcast(I32))
         nc.sync.dma_start(idx2[:], offs2)
@@ -100,19 +108,12 @@ def tile_moe_dyl_none_kernel(
         load_words(wa_w[1][:], wa_words[1])
         nc.sync.dma_start(idx3[:], offs3)
         wb_w = sb("wb_w", [P, E * N], I32)
-        ahead = E * N // 4
-        load_words(wb_w[:, 0:ahead], wb_words[0, :, 0:ahead])
+        load_words(wb_w[:, 0:WB_AHEAD], wb_words[0, :, 0:WB_AHEAD])
         load_scales(nc.gpsimd, wb_s, wb_scales, WB_ROW)
 
         xq_w = [sb("xq_w%d" % s, [P, SLOTS], U32) for s in range(2)]
         xq_s = sb("xq_s", [P, SLOTS], U8)
         waq_rows = sb("waq_rows", [P, B * H], U8)
-
-        def reuse(name, shape, dtype, tag):
-            return keep.tile(shape, dtype, name=name, tag=tag, align_bytes=64)
-
-        def bank(name, shape, tag):
-            return psum.tile(shape, F32, name=name + "_" + tag, offset=4 * BANK * BANKS.index(tag))
 
         gather(waq_rows[:], wa_s[:], idx2, 0, B * H)
 
@@ -124,7 +125,7 @@ def tile_moe_dyl_none_kernel(
                     waq_rows[raw + r : raw + 16 : 4, :].bitcast(I32),
                 )
 
-        load_words(wb_w[:, ahead:], wb_words[0, :, ahead:])
+        load_words(wb_w[:, WB_AHEAD:], wb_words[0, :, WB_AHEAD:])
 
         gate_rows = sb("gate_rows", [P, 2 * P], F32)
         gate_col = sb("gate_col", [P, 2], F32)
@@ -135,17 +136,8 @@ def tile_moe_dyl_none_kernel(
         gather(xq_s[:], x_s[:], idx, 0, SLOTS)
         for s in range(2):
             gather(xq_w[s][:], x_w[s].bitcast(U32), idx, 0, SLOTS)
-
-        waq_w = {}
-
-        def gather_wa(m, s, tile):
-            waq_w[m, s] = tile
-            gather(tile, wa_w[s][:].bitcast(U32), idx2, m * H, H)
-
         waq_first = sb("waq_first", [P, B * H], U32)
         gather(waq_first[:], wa_w[0][:].bitcast(U32), idx2, 0, B * H)
-        for m in range(B):
-            waq_w[m, 0] = waq_first[:, part(m, H)]
 
         result = [sb("result%d" % j, [P, T], F32) for j in range(2)]
         for j in range(2):
@@ -156,60 +148,61 @@ def tile_moe_dyl_none_kernel(
                        x_w[s], x_s, X_ROW[s], part(half, BANK), s == 0, s == 1)
                 nc.scalar.copy(result[j][:, part(half, BANK)], acc[:])
 
-        base_early = sb("base_early", [P, 2, N], F32)
+        base_first = sb("base_early", [P, 2, N], F32)
         acc = bank("slot_acc", [P, 2, N], "turn0")
         for m in range(2):
             for s in range(2):
                 mm(acc[:, m, :], xq_w[s], xq_s, X_ROW[s], part(m, P),
                    w_w[:, s, :], w_s, W_ROW[s], slice(0, N), s == 0, s == 1)
-        nc.scalar.copy(base_early[:], acc[:])
-        base_late = sb("base_late", [P, 2, 2 * P], F32)
+        nc.scalar.copy(base_first[:], acc[:])
+        base_second = sb("base_late", [P, 2, 2 * P], F32)
         acc = bank("slot_acc", [P, 2, 2 * P], "turn1")
         for j in range(2):
             for s in range(2):
                 mm(acc[:, j, :], w_w[:, s, :], w_s, W_ROW[s], part(j, P),
                    xq_w[s], xq_s, X_ROW[s], part(1, 2 * P), s == 0, s == 1)
-        nc.scalar.copy(base_late[:], acc[:])
+        nc.scalar.copy(base_second[:], acc[:])
 
-        h_acc = {}
-
-        def h_pass(m, s):
+        def h_pass(m, s, words):
             nc.tensor.matmul_mx(
                 out=h_acc[m][:],
                 lhsT=xq_w[s][:, part(m, P)].bitcast(FP8X4),
                 lhsT_scale=xq_s[X_ROW[s] : P, part(m, P)],
-                rhs=waq_w[m, s].bitcast(FP8X4),
+                rhs=words.bitcast(FP8X4),
                 rhs_scale=waq_s[s][WA_ROW[s] : P, part(m, H)],
                 start=s == 0,
                 stop=s == 1,
             )
 
+        h_acc = []
         for m in range(B):
-            h_acc[m] = bank("h_acc%d" % m, [P, H], "h%d" % m)
-            h_pass(m, 0)
+            h_acc.append(bank("h_acc%d" % m, [P, H], "h%d" % m))
+            h_pass(m, 0, waq_first[:, part(m, H)])
 
+        waq_second = []
         for m in range(B):
-            gather_wa(m, 1, sb("waq_second%d" % m, [P, H], U32)[:])
+            waq_second.append(sb("waq_second%d" % m, [P, H], U32))
+            gather(waq_second[m][:], wa_w[1][:].bitcast(U32), idx2, m * H, H)
         wbq_s = [sb("wbq_s0", [P, 2 * N], U8)]
         gather(wbq_s[0][:], wb_s[:], idx3, 0, 2 * N)
         wbq_w = [sb("wbq_w0", [P, 2 * N], U32)]
         gather(wbq_w[0][:], wb_w[:].bitcast(U32), idx3, 0, 2 * N)
-
-        grouped = {}
 
         def round_h(m):
             h_bf = reuse("h_bf%d" % m, [P, 2, P, 2], BF16, "h_bf%d" % (m % 2))
             nc.scalar.copy(h_bf[:], h_acc[m][:].rearrange("s (p u e) -> s u p e", u=2, e=2))
             return h_bf[:].rearrange("s u p e -> s (u p e)").bitcast(F32)
 
+        grouped = []
+
         def turn_h(m, h_words):
             turned = bank("turned", [P, 2, P], "turn%d" % (m % 2))
             for u in range(2):
                 nc.tensor.transpose(turned[:, u, :], h_words[:, part(u, P)], ident[:])
-            grouped[m] = reuse("grouped%d" % m, [P, P, 2], F32, "hq_s0" if m == 3 else "grouped%d" % m)
+            grouped.append(sb("grouped%d" % m, [P, P, 2], F32))
             nc.scalar.copy(grouped[m][:], turned[:].rearrange("p u s -> p s u"))
 
-        hq = {}
+        hq = []
 
         def quantise(m):
             hq_w = sb("hq_w%d" % m, [P, P], U32)
@@ -219,40 +212,32 @@ def tile_moe_dyl_none_kernel(
                 scales=hq_s[:],
                 in_=grouped[m][:].rearrange("p s u -> p (s u)").bitcast(BF16),
             )
-            hq[m] = (hq_w, hq_s)
+            hq.append((hq_w, hq_s))
 
-        def gate_slots(m, cols, width, tag):
-            y_slots = bank("y_slots", [P, width], tag)
-            mm(y_slots[:], hq[m][0], hq[m][1], 0, slice(0, P),
-               wbq_w[m // 2], wbq_s[m // 2], WB_ROW, cols, True, True)
-            y_gated = sb("y_gated%d" % m, [P, width], F32)
+        def gate_slots(m):
+            y_slots = bank("y_slots", [P, N], "h%d" % m)
+            mm(y_slots[:], hq[m][0], hq[m][1], 0, slice(0, P), wbq_w[0], wbq_s[0], WB_ROW, part(m, N), True, True)
+            y_gated = sb("y_gated%d" % m, [P, N], F32)
             nc.scalar.activation(y_gated[:], y_slots[:], COPY, scale=gate_col[:, m : m + 1])
             return y_gated
 
-        def scatter(j, entry, count, values):
-            nc.scalar.activation(result[j][:].indirect(idx[:, entry // 16 : (entry + count) // 16]), values, COPY)
-
-        for m in range(B):
-            h_pass(m, 1)
-            words = round_h(m)
-            if m < 3:
-                turn_h(m, words)
-
-        def sum_back(m, base, y_gated):
-            tiles = y_gated.shape[1] // P
-            back = bank("back", [P, tiles, P], "back%d" % m)
-            for step, source in enumerate((base, y_gated[:])):
-                for j in range(tiles):
+        def sum_back(m, y_gated):
+            back = bank("back", [P, 2, P], "back%d" % m)
+            for step, source in enumerate((base_first[:, m, :], y_gated[:])):
+                for j in range(2):
                     nc.tensor.matmul(back[:, j, :], source[:, part(j, P)], ident[:], is_transpose=True,
-                                     start=step == 0 and j == 0, stop=step == 1 and j == tiles - 1)
+                                     start=step == 0 and j == 0, stop=step == 1 and j == 1)
             return back
 
-        quantise(0)
-        first_gated = gate_slots(0, slice(0, N), N, "h0")
-        turn_h(3, words)
-        back_first = sum_back(0, base_early[:, 0, :], first_gated)
-        quantise(1)
-        back_second = sum_back(1, base_early[:, 1, :], gate_slots(1, part(1, N), N, "h1"))
+        for m in range(B):
+            h_pass(m, 1, waq_second[m][:])
+            turn_h(m, round_h(m))
+
+        backs = []
+        for m in range(2):
+            quantise(m)
+            backs.append(sum_back(m, gate_slots(m)))
+
         wbq_s.append(reuse("wbq_s1", [P, 2 * N], U8, "grouped1"))
         gather(wbq_s[1][:], wb_s[:], idx3, 2 * N, 2 * N)
         for m in range(2, B):
@@ -262,13 +247,17 @@ def tile_moe_dyl_none_kernel(
             gather(wbq_w[1][:, part(m - 2, N)], wb_w[:].bitcast(U32), idx3, m * N, N)
 
         summed = sb("summed", [P, 2, 2 * P], F32)
-        for m, back in enumerate((back_first, back_second)):
-            nc.scalar.copy(summed[:, :, part(m, P)], back[:])
-        scatter(0, 0, 2 * P, summed[:, 0, :])
+        for m in range(2):
+            nc.scalar.copy(summed[:, :, part(m, P)], backs[m][:])
+
+        def scatter_first_pair(j):
+            nc.scalar.activation(result[j][:].indirect(idx[:, 0 : 2 * P // 16]), summed[:, j, :], COPY)
+
+        scatter_first_pair(0)
 
         gated = sb("gated", [P, 2, 2 * P], F32)
 
-        def gate_rows_of(mb, tiles, tag):
+        def gate_block(mb, tiles, tag):
             acc = bank("y_rows", [P, 2, P], tag)
             for j in tiles:
                 mm(acc[:, j, :], wbq_w[1], wbq_s[1], WB_ROW, part(2 * mb + j, P),
@@ -276,19 +265,19 @@ def tile_moe_dyl_none_kernel(
             for j in tiles:
                 nc.vector.tensor_tensor(gated[:, j, part(mb, P)], acc[:, j, :], gate_rows[:, part(mb, P)], MULT)
 
-        def add_scatter(j, first, count):
-            cols = slice(first * P, (first + count) * P)
+        def add_scatter(j, mb, blocks):
+            cols = slice(mb * P, (mb + blocks) * P)
             nc.vector.tensor_tensor(
-                result[j][:].indirect(idx[:, (2 + first) * P // 16 : (2 + first + count) * P // 16]),
+                result[j][:].indirect(idx[:, (2 + mb) * P // 16 : (2 + mb + blocks) * P // 16]),
                 gated[:, j, cols],
-                base_late[:, j, cols],
+                base_second[:, j, cols],
                 ADD,
             )
 
-        gate_rows_of(0, [1, 0], "h1")
+        gate_block(0, [1, 0], "h1")
         add_scatter(1, 0, 1)
-        scatter(1, 0, 2 * P, summed[:, 1, :])
-        gate_rows_of(1, [0, 1], "back0")
+        scatter_first_pair(1)
+        gate_block(1, [0, 1], "back0")
         add_scatter(0, 0, 2)
         nc.sync.dma_start(out[part(0, P), :], result[0][:])
         add_scatter(1, 1, 1)

@@ -113,16 +113,17 @@ def tile_moe_dyl_none_kernel(
 
         xq_w = [sb("xq_w%d" % s, [P, SLOTS], U32) for s in range(2)]
         xq_s = sb("xq_s", [P, SLOTS], U8)
-        waq_rows = sb("waq_rows", [P, B * H], U8)
+        waq_rows = [sb("waq_rows%d" % s, [P, B * H], U8) for s in range(2)]
 
-        gather(waq_rows[:], wa_s[:], idx2, 0, B * H)
+        for s in range(2):
+            gather(waq_rows[s][:], wa_s[:], idx2, 0, B * H)
 
         for s in range(2):
             for r in range(4):
                 raw = WA_RAW + 16 * s
                 (nc.scalar, nc.sync)[s].dma_start(
                     waq_s[s][WA_ROW[s] + r : P : 32, :].bitcast(I32),
-                    waq_rows[raw + r : raw + 16 : 4, :].bitcast(I32),
+                    waq_rows[s][raw + r : raw + 16 : 4, :].bitcast(I32),
                 )
 
         load_words(wb_w[:, WB_AHEAD:], wb_words[0, :, WB_AHEAD:])

@@ -19,16 +19,10 @@ MULT = mybir.AluOpType.mult
 ADD = mybir.AluOpType.add
 COPY = mybir.ActivationFunctionType.Copy
 
-BANKS = ("h0", "h1", "h2", "h3", "turn0", "turn1", "back0", "back1")
-
-X_ROW = (0, 4)
-W_ROW = (0, 4)
-WA_ROW = (8, 12)
+X_ROW = (8, 12)
+W_ROW = (8, 12)
+WA_ROW = (0, 4)
 WB_ROW = 8
-
-WA_RAW = 96
-
-WB_AHEAD = E * N // 4
 
 
 def tile_moe_dyl_none_kernel(
@@ -45,8 +39,8 @@ def tile_moe_dyl_none_kernel(
         def reuse(name, shape, dtype, tag):
             return keep.tile(shape, dtype, name=name, tag=tag, align_bytes=64)
 
-        def bank(name, shape, tag):
-            return psum.tile(shape, F32, name=name + "_" + tag, offset=4 * BANK * BANKS.index(tag))
+        def bank(name, shape, number):
+            return psum.tile(shape, F32, name="%s_%d" % (name, number), offset=4 * BANK * number)
 
         def part(index, width):
             return slice(index * width, (index + 1) * width)
@@ -54,9 +48,9 @@ def tile_moe_dyl_none_kernel(
         def load_words(tile, words):
             nc.sync.dma_start(tile, words.rearrange("p n t -> p (n t)").bitcast(I32))
 
-        def load_scales(queue, tile, scales, first_row, sets=range(4)):
+        def load_scales(queue, tile, scales, first_row):
             rows = 4 * scales.shape[0]
-            for q in sets:
+            for q in range(4):
                 queue.dma_start(
                     tile[32 * q + first_row : 32 * q + first_row + rows, :].bitcast(I32),
                     scales[:, 4 * q : 4 * q + 4, :].bitcast(I32),
@@ -65,13 +59,13 @@ def tile_moe_dyl_none_kernel(
         def gather(dst, window, offsets, entry, count):
             nc.vector.tensor_copy(dst, window.indirect(offsets[:, entry // 16 : (entry + count) // 16]))
 
-        def mm(acc, lhs, lhs_scales, lhs_row, lhs_cols, rhs, rhs_scales, rhs_row, rhs_cols, start, stop):
+        def mm(acc, lhs, lhs_scales, rhs, rhs_scales, start, stop):
             nc.tensor.matmul_mx(
                 out=acc,
-                lhsT=lhs[:, lhs_cols].bitcast(FP8X4),
-                lhsT_scale=lhs_scales[lhs_row:P, lhs_cols],
-                rhs=rhs[:, rhs_cols].bitcast(FP8X4),
-                rhs_scale=rhs_scales[rhs_row:P, rhs_cols],
+                lhsT=lhs.bitcast(FP8X4),
+                lhsT_scale=lhs_scales,
+                rhs=rhs.bitcast(FP8X4),
+                rhs_scale=rhs_scales,
                 start=start,
                 stop=stop,
             )
@@ -79,129 +73,99 @@ def tile_moe_dyl_none_kernel(
         idx = sb("idx", [P, SLOTS // 16], U16)
         idx2 = sb("idx2", [P, B * H // 16], U16)
         idx3 = sb("idx3", [P, B * N // 16], U16)
-        x_both = sb("x_w", [P, 2, T], I32)
-        x_w = [x_both[:, s, :] for s in range(2)]
+        x_w = sb("x_w", [P, 2, T], I32)
         w_w = sb("w_w", [P, 2, N], I32)
+        wa_w = [sb("wa_w%d" % s, [P, E * H], I32) for s in range(2)]
+        wb_w = sb("wb_w", [P, E * N], I32)
         x_s = sb("x_s", [P, T], U8)
         w_s = sb("w_s", [P, N], U8)
         wa_s = sb("wa_s", [P, E * H], U8)
         wb_s = sb("wb_s", [P, E * N], U8)
-        waq_s = [sb("waq_s%d" % s, [P, B * H], U8) for s in range(2)]
+        gate_rows = sb("gate_rows", [P, SLOTS], F32)
+        gate_col = sb("gate_col", [P, B], F32)
         ident = sb("ident", [P, P], F32)
+        diagonal = sb("diagonal", [P, P], I32)
 
-        diagonal = sb("offset", [P, P], I32)
         nc.gpsimd.iota(diagonal[:], [[1, P]], base=0, channel_multiplier=-1)
-        load_scales(nc.gpsimd, w_s, w_scales, W_ROW[0], range(3))
-        for tile in (x_s[:], wa_s[0:WA_RAW, :], wb_s[:]):
-            nc.vector.memset(tile.bitcast(I32), 0)
+        for tile in (x_s, wa_s, wb_s):
+            nc.vector.memset(tile[:].bitcast(I32), 0)
         nc.vector.tensor_scalar(ident[:], diagonal[:], 0, None, mybir.AluOpType.is_equal)
 
-        nc.sync.dma_start(wa_s[WA_RAW:P, :].bitcast(I32), wa_scales.rearrange("s b c -> (s b) c").bitcast(I32))
-        nc.sync.dma_start(idx2[:], offs2)
-        load_scales(nc.scalar, w_s, w_scales, W_ROW[0], range(3, 4))
         load_scales(nc.scalar, x_s, x_scales, X_ROW[0])
-        nc.sync.dma_start(x_both[:], x_words.rearrange("s p n t -> p s (n t)").bitcast(I32))
-        nc.sync.dma_start(idx[:], offs)
-        wa_w = [sb("wa_w%d" % s, [P, E * H], I32) for s in range(2)]
-        load_words(wa_w[0][:], wa_words[0])
-        nc.sync.dma_start(w_w[:], w_words.rearrange("s p n t -> p s (n t)").bitcast(I32))
-        load_words(wa_w[1][:], wa_words[1])
-        nc.sync.dma_start(idx3[:], offs3)
-        wb_w = sb("wb_w", [P, E * N], I32)
-        load_words(wb_w[:, 0:WB_AHEAD], wb_words[0, :, 0:WB_AHEAD])
+        load_scales(nc.gpsimd, wa_s, wa_scales, WA_ROW[0])
         load_scales(nc.gpsimd, wb_s, wb_scales, WB_ROW)
-
-        xq_w = [sb("xq_w%d" % s, [P, SLOTS], U32) for s in range(2)]
-        xq_s = sb("xq_s", [P, SLOTS], U8)
-        waq_rows = [sb("waq_rows%d" % s, [P, B * H], U8) for s in range(2)]
-
-        for s in range(2):
-            gather(waq_rows[s][:], wa_s[:], idx2, 0, B * H)
-
-        for s in range(2):
-            for r in range(4):
-                raw = WA_RAW + 16 * s
-                (nc.scalar, nc.sync)[s].dma_start(
-                    waq_s[s][WA_ROW[s] + r : P : 32, :].bitcast(I32),
-                    waq_rows[s][raw + r : raw + 16 : 4, :].bitcast(I32),
-                )
-
-        load_words(wb_w[:, WB_AHEAD:], wb_words[0, :, WB_AHEAD:])
-
-        gate_rows = sb("gate_rows", [P, 2 * P], F32)
-        gate_col = sb("gate_col", [P, 2], F32)
+        nc.sync.dma_start(idx[:], offs)
+        nc.sync.dma_start(x_w[:], x_words.rearrange("s p n t -> p s (n t)").bitcast(I32))
+        nc.sync.dma_start(idx2[:], offs2)
+        nc.sync.dma_start(idx3[:], offs3)
+        nc.sync.dma_start(w_w[:], w_words.rearrange("s p n t -> p s (n t)").bitcast(I32))
+        load_words(wa_w[0][:], wa_words[0])
+        load_scales(nc.sync, w_s, w_scales, W_ROW[0])
+        load_words(wa_w[1][:], wa_words[1])
+        load_words(wb_w[:], wb_words[0])
+        nc.sync.dma_start(gate_rows[:], gate)
         with nc.allow_non_contiguous_dma(reason="one gate value a partition and block"):
-            nc.sync.dma_start(gate_col[:], gate[0, 0 : 2 * P].rearrange("(b p) -> p b", p=P))
-        nc.sync.dma_start(gate_rows[:], gate[:, 2 * P : SLOTS])
+            nc.sync.dma_start(gate_col[:], gate[0, :].rearrange("(b p) -> p b", p=P))
 
+        xq_s = sb("xq_s", [P, SLOTS], U8)
         gather(xq_s[:], x_s[:], idx, 0, SLOTS)
+        xq_w = [sb("xq_w%d" % s, [P, SLOTS], U32) for s in range(2)]
         for s in range(2):
-            gather(xq_w[s][:], x_w[s].bitcast(U32), idx, 0, SLOTS)
-        waq_first = sb("waq_first", [P, B * H], U32)
-        gather(waq_first[:], wa_w[0][:].bitcast(U32), idx2, 0, B * H)
+            gather(xq_w[s][:], x_w[:, s, :].bitcast(U32), idx, 0, SLOTS)
+
+        waq_listed = sb("waq_listed", [P, B * H], U8)
+        gather(waq_listed[:], wa_s[:], idx2, 0, B * H)
+        waq_s = sb("waq_s", [P, B * H], U8)
+        nc.vector.tensor_copy(
+            waq_s[:].rearrange("p (m t q) -> p m t q", m=B, t=4),
+            waq_listed[:].rearrange("p (m q t) -> p m t q", m=B, t=4),
+        )
+        waq_first = sb("waq_first", [P, B, 4, P], U32)
+        gather(waq_first[:].rearrange("p m t q -> p m q t"), wa_w[0][:].bitcast(U32), idx2, 0, B * H)
+        wbq_s = reuse("wbq_s", [P, B * N], U8, "wa_w0")
+        gather(wbq_s[:], wb_s[:], idx3, 0, B * N)
 
         result = [sb("result%d" % j, [P, T], F32) for j in range(2)]
         for j in range(2):
             for half in range(2):
-                acc = bank("base_acc", [P, BANK], "h%d" % (2 * j + half))
+                acc = bank("base_acc", [P, BANK], 2 * j + half)
                 for s in range(2):
-                    mm(acc[:], w_w[:, s, :], w_s, W_ROW[s], part(j, P),
-                       x_w[s], x_s, X_ROW[s], part(half, BANK), s == 0, s == 1)
+                    mm(acc[:], w_w[:, s, part(j, P)], w_s[W_ROW[s] : P, part(j, P)],
+                       x_w[:, s, part(half, BANK)], x_s[X_ROW[s] : P, part(half, BANK)], s == 0, s == 1)
                 nc.scalar.copy(result[j][:, part(half, BANK)], acc[:])
 
-        base_first = sb("base_early", [P, 2, N], F32)
-        acc = bank("slot_acc", [P, 2, N], "turn0")
-        for m in range(2):
+        base_slots = sb("base_slots", [P, B, P], F32)
+        acc = bank("slot_acc", [P, B, P], 4)
+        for m in range(B):
             for s in range(2):
-                mm(acc[:, m, :], xq_w[s], xq_s, X_ROW[s], part(m, P),
-                   w_w[:, s, :], w_s, W_ROW[s], slice(0, N), s == 0, s == 1)
-        nc.scalar.copy(base_first[:], acc[:])
-        base_second = sb("base_late", [P, 2, 2 * P], F32)
-        acc = bank("slot_acc", [P, 2, 2 * P], "turn1")
-        for j in range(2):
-            for s in range(2):
-                mm(acc[:, j, :], w_w[:, s, :], w_s, W_ROW[s], part(j, P),
-                   xq_w[s], xq_s, X_ROW[s], part(1, 2 * P), s == 0, s == 1)
-        nc.scalar.copy(base_second[:], acc[:])
+                mm(acc[:, m, :], xq_w[s][:, part(m, P)], xq_s[X_ROW[s] : P, part(m, P)],
+                   w_w[:, s, part(0, P)], w_s[W_ROW[s] : P, part(0, P)], s == 0, s == 1)
+        nc.scalar.copy(base_slots[:], acc[:])
+        base_rows = sb("base_rows", [P, SLOTS], F32)
+        acc = bank("slot_acc", [P, SLOTS], 5)
+        for s in range(2):
+            mm(acc[:], w_w[:, s, part(1, P)], w_s[W_ROW[s] : P, part(1, P)],
+               xq_w[s][:], xq_s[X_ROW[s] : P, :], s == 0, s == 1)
+        nc.scalar.copy(base_rows[:], acc[:])
 
         def h_pass(m, s, words):
-            nc.tensor.matmul_mx(
-                out=h_acc[m][:],
-                lhsT=xq_w[s][:, part(m, P)].bitcast(FP8X4),
-                lhsT_scale=xq_s[X_ROW[s] : P, part(m, P)],
-                rhs=words.bitcast(FP8X4),
-                rhs_scale=waq_s[s][WA_ROW[s] : P, part(m, H)],
-                start=s == 0,
-                stop=s == 1,
-            )
+            for t in range(4):
+                mm(h_acc[m][:, t, :], words[:, t, :], waq_s[WA_ROW[s] : P, part(4 * m + t, P)],
+                   xq_w[s][:, part(m, P)], xq_s[X_ROW[s] : P, part(m, P)],
+                   s == 0 and t == 0, s == 1 and t == 3)
 
         h_acc = []
         for m in range(B):
-            h_acc.append(bank("h_acc%d" % m, [P, H], "h%d" % m))
-            h_pass(m, 0, waq_first[:, part(m, H)])
-
-        waq_second = []
-        for m in range(B):
-            waq_second.append(sb("waq_second%d" % m, [P, H], U32))
-            gather(waq_second[m][:], wa_w[1][:].bitcast(U32), idx2, m * H, H)
-        wbq_s = [sb("wbq_s0", [P, 2 * N], U8)]
-        gather(wbq_s[0][:], wb_s[:], idx3, 0, 2 * N)
-        wbq_w = [sb("wbq_w0", [P, 2 * N], U32)]
-        gather(wbq_w[0][:], wb_w[:].bitcast(U32), idx3, 0, 2 * N)
-
-        def round_h(m):
-            h_bf = reuse("h_bf%d" % m, [P, 2, P, 2], BF16, "h_bf%d" % (m % 2))
-            nc.scalar.copy(h_bf[:], h_acc[m][:].rearrange("s (p u e) -> s u p e", u=2, e=2))
-            return h_bf[:].rearrange("s u p e -> s (u p e)").bitcast(F32)
+            h_acc.append(bank("h_acc", [P, 4, P], m))
+            h_pass(m, 0, waq_first[:, m])
 
         grouped = []
-
-        def turn_h(m, h_words):
-            turned = bank("turned", [P, 2, P], "turn%d" % (m % 2))
-            for u in range(2):
-                nc.tensor.transpose(turned[:, u, :], h_words[:, part(u, P)], ident[:])
-            grouped.append(sb("grouped%d" % m, [P, P, 2], F32))
-            nc.scalar.copy(grouped[m][:], turned[:].rearrange("p u s -> p s u"))
+        for m in range(B):
+            waq_second = sb("waq_second%d" % m, [P, 4, P], U32)
+            gather(waq_second[:].rearrange("p t q -> p q t"), wa_w[1][:].bitcast(U32), idx2, m * H, H)
+            h_pass(m, 1, waq_second)
+            grouped.append(sb("grouped%d" % m, [P, P, 4], BF16))
+            nc.scalar.copy(grouped[m][:], h_acc[m][:].rearrange("p t u -> p u t"))
 
         hq = []
 
@@ -209,77 +173,49 @@ def tile_moe_dyl_none_kernel(
             hq_w = sb("hq_w%d" % m, [P, P], U32)
             hq_s = sb("hq_s%d" % m, [P, P], U8)
             nc.vector.quantize_mx(
-                out=hq_w[:].bitcast(FP8X4),
-                scales=hq_s[:],
-                in_=grouped[m][:].rearrange("p s u -> p (s u)").bitcast(BF16),
+                out=hq_w[:].bitcast(FP8X4), scales=hq_s[:], in_=grouped[m][:].rearrange("p u t -> p (u t)")
             )
             hq.append((hq_w, hq_s))
 
-        def gate_slots(m):
-            y_slots = bank("y_slots", [P, N], "h%d" % m)
-            mm(y_slots[:], hq[m][0], hq[m][1], 0, slice(0, P), wbq_w[0], wbq_s[0], WB_ROW, part(m, N), True, True)
-            y_gated = sb("y_gated%d" % m, [P, N], F32)
-            nc.scalar.activation(y_gated[:], y_slots[:], COPY, scale=gate_col[:, m : m + 1])
-            return y_gated
+        y_slots, y_rows = [], []
+        for pair in range(2):
+            wbq_w = sb("wbq_w%d" % pair, [P, 2 * N], U32)
+            gather(wbq_w[:], wb_w[:].bitcast(U32), idx3, pair * 2 * N, 2 * N)
+            y_slots.append(bank("y_slots", [P, 2, P], 4 + pair))
+            y_rows.append(bank("y_rows", [P, 2, P], 6 + pair))
+            for b in range(2):
+                quantise(2 * pair + b)
+            for b in range(2):
+                m = 2 * pair + b
+                mm(y_slots[pair][:, b, :], hq[m][0][:], hq[m][1][:],
+                   wbq_w[:, part(2 * b, P)], wbq_s[WB_ROW:P, part(2 * m, P)], True, True)
+            for b in range(2):
+                m = 2 * pair + b
+                mm(y_rows[pair][:, b, :], wbq_w[:, part(2 * b + 1, P)], wbq_s[WB_ROW:P, part(2 * m + 1, P)],
+                   hq[m][0][:], hq[m][1][:], True, True)
 
-        def sum_back(m, y_gated):
-            back = bank("back", [P, 2, P], "back%d" % m)
-            for step, source in enumerate((base_first[:, m, :], y_gated[:])):
-                for j in range(2):
-                    nc.tensor.matmul(back[:, j, :], source[:, part(j, P)], ident[:], is_transpose=True,
-                                     start=step == 0 and j == 0, stop=step == 1 and j == 1)
-            return back
-
-        for m in range(B):
-            h_pass(m, 1, waq_second[m][:])
-            turn_h(m, round_h(m))
-
+        y_gated = sb("y_gated", [P, B, P], F32)
         backs = []
-        for m in range(2):
-            quantise(m)
-            backs.append(sum_back(m, gate_slots(m)))
+        for pair in range(2):
+            for b in range(2):
+                m = 2 * pair + b
+                nc.scalar.activation(y_gated[:, m, :], y_slots[pair][:, b, :], COPY, scale=gate_col[:, m : m + 1])
+            back = bank("back", [P, 2, P], pair)
+            for step, source in enumerate((base_slots, y_gated)):
+                for b in range(2):
+                    nc.tensor.matmul(back[:, b, :], source[:, 2 * pair + b, :], ident[:], is_transpose=True,
+                                     start=step == 0 and b == 0, stop=step == 1 and b == 1)
+            backs.append(back)
 
-        wbq_s.append(reuse("wbq_s1", [P, 2 * N], U8, "grouped1"))
-        gather(wbq_s[1][:], wb_s[:], idx3, 2 * N, 2 * N)
-        for m in range(2, B):
-            quantise(m)
-        wbq_w.append(reuse("wbq_w1", [P, 2 * N], U32, "grouped2"))
-        for m in range(2, B):
-            gather(wbq_w[1][:, part(m - 2, N)], wb_w[:].bitcast(U32), idx3, m * N, N)
+        for pair in range(2):
+            cols = part(pair, 2 * P)
+            offsets = idx[:, part(pair, 2 * P // 16)]
+            summed = sb("summed%d" % pair, [P, 2 * P], F32)
+            nc.scalar.copy(summed[:], backs[pair][:].rearrange("p b u -> p (b u)"))
+            nc.scalar.activation(result[0][:].indirect(offsets), summed[:], COPY)
+            gated = sb("gated%d" % pair, [P, 2 * P], F32)
+            nc.vector.tensor_tensor(gated[:], y_rows[pair][:].rearrange("p b u -> p (b u)"), gate_rows[:, cols], MULT)
+            nc.vector.tensor_tensor(result[1][:].indirect(offsets), gated[:], base_rows[:, cols], ADD)
 
-        summed = sb("summed", [P, 2, 2 * P], F32)
-        for m in range(2):
-            nc.scalar.copy(summed[:, :, part(m, P)], backs[m][:])
-
-        def scatter_first_pair(j):
-            nc.scalar.activation(result[j][:].indirect(idx[:, 0 : 2 * P // 16]), summed[:, j, :], COPY)
-
-        scatter_first_pair(0)
-
-        gated = sb("gated", [P, 2, 2 * P], F32)
-
-        def gate_block(mb, tiles, tag):
-            acc = bank("y_rows", [P, 2, P], tag)
-            for j in tiles:
-                mm(acc[:, j, :], wbq_w[1], wbq_s[1], WB_ROW, part(2 * mb + j, P),
-                   hq[2 + mb][0], hq[2 + mb][1], 0, slice(0, P), True, True)
-            for j in tiles:
-                nc.vector.tensor_tensor(gated[:, j, part(mb, P)], acc[:, j, :], gate_rows[:, part(mb, P)], MULT)
-
-        def add_scatter(j, mb, blocks):
-            cols = slice(mb * P, (mb + blocks) * P)
-            nc.vector.tensor_tensor(
-                result[j][:].indirect(idx[:, (2 + mb) * P // 16 : (2 + mb + blocks) * P // 16]),
-                gated[:, j, cols],
-                base_second[:, j, cols],
-                ADD,
-            )
-
-        gate_block(0, [1, 0], "h1")
-        add_scatter(1, 0, 1)
-        scatter_first_pair(1)
-        gate_block(1, [0, 1], "back0")
-        add_scatter(0, 0, 2)
-        nc.sync.dma_start(out[part(0, P), :], result[0][:])
-        add_scatter(1, 1, 1)
-        nc.sync.dma_start(out[part(1, P), :], result[1][:])
+        for j in (1, 0):
+            nc.sync.dma_start(out[part(j, P), :], result[j][:])

@@ -19,10 +19,11 @@ MULT = mybir.AluOpType.mult
 ADD = mybir.AluOpType.add
 COPY = mybir.ActivationFunctionType.Copy
 
-X_ROW = (8, 12)
-W_ROW = (8, 12)
-WA_ROW = (0, 4)
+X_ROW = (0, 4)
+W_ROW = (0, 4)
+WA_ROW = (12, 8)
 WB_ROW = 8
+WA_RAW = 96
 
 
 def tile_moe_dyl_none_kernel(
@@ -81,31 +82,49 @@ def tile_moe_dyl_none_kernel(
         w_s = sb("w_s", [P, N], U8)
         wa_s = sb("wa_s", [P, E * H], U8)
         wb_s = sb("wb_s", [P, E * N], U8)
-        gate_rows = sb("gate_rows", [P, SLOTS], F32)
-        gate_col = sb("gate_col", [P, B], F32)
+        gate_rows = sb("gate_rows", [P, 2 * P], F32)
+        gate_col = sb("gate_col", [P, 2], F32)
         ident = sb("ident", [P, P], F32)
         diagonal = sb("diagonal", [P, P], I32)
 
         nc.gpsimd.iota(diagonal[:], [[1, P]], base=0, channel_multiplier=-1)
-        for tile in (x_s, wa_s, wb_s):
-            nc.vector.memset(tile[:].bitcast(I32), 0)
+        for tile in (wb_s[:], x_s[:], wa_s[0:WA_RAW, :]):
+            nc.vector.memset(tile.bitcast(I32), 0)
         nc.vector.tensor_scalar(ident[:], diagonal[:], 0, None, mybir.AluOpType.is_equal)
 
-        load_scales(nc.scalar, x_s, x_scales, X_ROW[0])
-        load_scales(nc.gpsimd, wa_s, wa_scales, WA_ROW[0])
         load_scales(nc.gpsimd, wb_s, wb_scales, WB_ROW)
-        nc.sync.dma_start(idx[:], offs)
-        nc.sync.dma_start(x_w[:], x_words.rearrange("s p n t -> p s (n t)").bitcast(I32))
+        load_scales(nc.scalar, w_s, w_scales, W_ROW[0])
+        load_scales(nc.scalar, x_s, x_scales, X_ROW[0])
+        nc.sync.dma_start(wa_s[WA_RAW:P, :].bitcast(I32), wa_scales.rearrange("s b c -> (s b) c").bitcast(I32))
         nc.sync.dma_start(idx2[:], offs2)
-        nc.sync.dma_start(idx3[:], offs3)
+        nc.sync.dma_start(x_w[:], x_words.rearrange("s p n t -> p s (n t)").bitcast(I32))
+        nc.sync.dma_start(idx[:], offs)
         nc.sync.dma_start(w_w[:], w_words.rearrange("s p n t -> p s (n t)").bitcast(I32))
         load_words(wa_w[0][:], wa_words[0])
-        load_scales(nc.sync, w_s, w_scales, W_ROW[0])
+        nc.sync.dma_start(idx3[:], offs3)
         load_words(wa_w[1][:], wa_words[1])
         load_words(wb_w[:], wb_words[0])
-        nc.sync.dma_start(gate_rows[:], gate)
         with nc.allow_non_contiguous_dma(reason="one gate value a partition and block"):
-            nc.sync.dma_start(gate_col[:], gate[0, :].rearrange("(b p) -> p b", p=P))
+            nc.sync.dma_start(gate_col[:], gate[0, 0 : 2 * P].rearrange("(b p) -> p b", p=P))
+        nc.sync.dma_start(gate_rows[:], gate[:, 2 * P : SLOTS])
+
+        waq_listed = sb("waq_listed", [P, B * H], U8)
+        gather(waq_listed[:], wa_s[:], idx2, 0, B * H)
+        waq_rows = sb("waq_rows", [P, B * H], U8)
+        nc.vector.tensor_copy(
+            waq_rows[:].rearrange("p (m t q) -> p m t q", m=B, t=4),
+            waq_listed[:].rearrange("p (m q t) -> p m t q", m=B, t=4),
+        )
+
+        def move_rows(s, tile):
+            for r in range(4):
+                raw = WA_RAW + 16 * s
+                nc.scalar.dma_start(
+                    tile[WA_ROW[s] + r : P : 32, :].bitcast(I32), waq_rows[raw + r : raw + 16 : 4, :].bitcast(I32)
+                )
+
+        waq_s = [sb("waq_s0", [P, B * H], U8)]
+        move_rows(0, waq_s[0])
 
         xq_s = sb("xq_s", [P, SLOTS], U8)
         gather(xq_s[:], x_s[:], idx, 0, SLOTS)
@@ -113,13 +132,6 @@ def tile_moe_dyl_none_kernel(
         for s in range(2):
             gather(xq_w[s][:], x_w[:, s, :].bitcast(U32), idx, 0, SLOTS)
 
-        waq_listed = sb("waq_listed", [P, B * H], U8)
-        gather(waq_listed[:], wa_s[:], idx2, 0, B * H)
-        waq_s = sb("waq_s", [P, B * H], U8)
-        nc.vector.tensor_copy(
-            waq_s[:].rearrange("p (m t q) -> p m t q", m=B, t=4),
-            waq_listed[:].rearrange("p (m q t) -> p m t q", m=B, t=4),
-        )
         waq_first = sb("waq_first", [P, B, 4, P], U32)
         gather(waq_first[:].rearrange("p m t q -> p m q t"), wa_w[0][:].bitcast(U32), idx2, 0, B * H)
         wbq_s = reuse("wbq_s", [P, B * N], U8, "wa_w0")
@@ -134,23 +146,26 @@ def tile_moe_dyl_none_kernel(
                        x_w[:, s, part(half, BANK)], x_s[X_ROW[s] : P, part(half, BANK)], s == 0, s == 1)
                 nc.scalar.copy(result[j][:, part(half, BANK)], acc[:])
 
-        base_slots = sb("base_slots", [P, B, P], F32)
-        acc = bank("slot_acc", [P, B, P], 4)
-        for m in range(B):
+        base_first = sb("base_first", [P, 2, N], F32)
+        acc = bank("slot_acc", [P, 2, N], 4)
+        for m in range(2):
             for s in range(2):
                 mm(acc[:, m, :], xq_w[s][:, part(m, P)], xq_s[X_ROW[s] : P, part(m, P)],
-                   w_w[:, s, part(0, P)], w_s[W_ROW[s] : P, part(0, P)], s == 0, s == 1)
-        nc.scalar.copy(base_slots[:], acc[:])
-        base_rows = sb("base_rows", [P, SLOTS], F32)
-        acc = bank("slot_acc", [P, SLOTS], 5)
-        for s in range(2):
-            mm(acc[:], w_w[:, s, part(1, P)], w_s[W_ROW[s] : P, part(1, P)],
-               xq_w[s][:], xq_s[X_ROW[s] : P, :], s == 0, s == 1)
-        nc.scalar.copy(base_rows[:], acc[:])
+                   w_w[:, s, :], w_s[W_ROW[s] : P, :], s == 0, s == 1)
+        nc.scalar.copy(base_first[:], acc[:])
+        base_second = sb("base_second", [P, 2, 2 * P], F32)
+        acc = bank("slot_acc", [P, 2, 2 * P], 5)
+        for j in range(2):
+            for s in range(2):
+                mm(acc[:, j, :], w_w[:, s, part(j, P)], w_s[W_ROW[s] : P, part(j, P)],
+                   xq_w[s][:, part(1, 2 * P)], xq_s[X_ROW[s] : P, part(1, 2 * P)], s == 0, s == 1)
+        waq_s.append(reuse("waq_s1", [P, B * H], U8, "w_s"))
+        move_rows(1, waq_s[1])
+        nc.scalar.copy(base_second[:], acc[:])
 
         def h_pass(m, s, words):
             for t in range(4):
-                mm(h_acc[m][:, t, :], words[:, t, :], waq_s[WA_ROW[s] : P, part(4 * m + t, P)],
+                mm(h_acc[m][:, t, :], words[:, t, :], waq_s[s][WA_ROW[s] : P, part(4 * m + t, P)],
                    xq_w[s][:, part(m, P)], xq_s[X_ROW[s] : P, part(m, P)],
                    s == 0 and t == 0, s == 1 and t == 3)
 
@@ -177,45 +192,62 @@ def tile_moe_dyl_none_kernel(
             )
             hq.append((hq_w, hq_s))
 
-        y_slots, y_rows = [], []
-        for pair in range(2):
-            wbq_w = sb("wbq_w%d" % pair, [P, 2 * N], U32)
-            gather(wbq_w[:], wb_w[:].bitcast(U32), idx3, pair * 2 * N, 2 * N)
-            y_slots.append(bank("y_slots", [P, 2, P], 4 + pair))
-            y_rows.append(bank("y_rows", [P, 2, P], 6 + pair))
-            for b in range(2):
-                quantise(2 * pair + b)
-            for b in range(2):
-                m = 2 * pair + b
-                mm(y_slots[pair][:, b, :], hq[m][0][:], hq[m][1][:],
-                   wbq_w[:, part(2 * b, P)], wbq_s[WB_ROW:P, part(2 * m, P)], True, True)
-            for b in range(2):
-                m = 2 * pair + b
-                mm(y_rows[pair][:, b, :], wbq_w[:, part(2 * b + 1, P)], wbq_s[WB_ROW:P, part(2 * m + 1, P)],
-                   hq[m][0][:], hq[m][1][:], True, True)
+        wbq_w = [sb("wbq_w0", [P, 2 * N], U32)]
+        gather(wbq_w[0][:], wb_w[:].bitcast(U32), idx3, 0, 2 * N)
 
-        y_gated = sb("y_gated", [P, B, P], F32)
         backs = []
-        for pair in range(2):
-            for b in range(2):
-                m = 2 * pair + b
-                nc.scalar.activation(y_gated[:, m, :], y_slots[pair][:, b, :], COPY, scale=gate_col[:, m : m + 1])
-            back = bank("back", [P, 2, P], pair)
-            for step, source in enumerate((base_slots, y_gated)):
-                for b in range(2):
-                    nc.tensor.matmul(back[:, b, :], source[:, 2 * pair + b, :], ident[:], is_transpose=True,
-                                     start=step == 0 and b == 0, stop=step == 1 and b == 1)
+        for m in range(2):
+            quantise(m)
+            y_slots = bank("y_slots", [P, N], 4 + m)
+            mm(y_slots[:], hq[m][0][:], hq[m][1][:], wbq_w[0][:, part(m, N)], wbq_s[WB_ROW:P, part(m, N)], True, True)
+            y_gated = sb("y_gated%d" % m, [P, N], F32)
+            nc.scalar.activation(y_gated[:], y_slots[:], COPY, scale=gate_col[:, m : m + 1])
+            back = bank("back", [P, 2, P], 6 + m)
+            for step, source in enumerate((base_first[:, m, :], y_gated[:])):
+                for j in range(2):
+                    nc.tensor.matmul(back[:, j, :], source[:, part(j, P)], ident[:], is_transpose=True,
+                                     start=step == 0 and j == 0, stop=step == 1 and j == 1)
             backs.append(back)
 
-        for pair in range(2):
-            cols = part(pair, 2 * P)
-            offsets = idx[:, part(pair, 2 * P // 16)]
-            summed = sb("summed%d" % pair, [P, 2 * P], F32)
-            nc.scalar.copy(summed[:], backs[pair][:].rearrange("p b u -> p (b u)"))
-            nc.scalar.activation(result[0][:].indirect(offsets), summed[:], COPY)
-            gated = sb("gated%d" % pair, [P, 2 * P], F32)
-            nc.vector.tensor_tensor(gated[:], y_rows[pair][:].rearrange("p b u -> p (b u)"), gate_rows[:, cols], MULT)
-            nc.vector.tensor_tensor(result[1][:].indirect(offsets), gated[:], base_rows[:, cols], ADD)
+        for m in range(2, B):
+            quantise(m)
+        wbq_w.append(reuse("wbq_w1", [P, 2 * N], U32, "grouped1"))
+        for m in range(2, B):
+            gather(wbq_w[1][:, part(m - 2, N)], wb_w[:].bitcast(U32), idx3, m * N, N)
 
-        for j in (1, 0):
-            nc.sync.dma_start(out[part(j, P), :], result[j][:])
+        summed = sb("summed", [P, 2, 2 * P], F32)
+        for m in range(2):
+            nc.scalar.copy(summed[:, :, part(m, P)], backs[m][:])
+
+        def scatter_first_pair(j):
+            nc.scalar.activation(result[j][:].indirect(idx[:, 0 : 2 * P // 16]), summed[:, j, :], COPY)
+
+        scatter_first_pair(0)
+
+        gated = sb("gated", [P, 2, 2 * P], F32)
+
+        def gate_block(mb, tiles, number):
+            acc = bank("y_rows", [P, 2, P], number)
+            for j in tiles:
+                mm(acc[:, j, :], wbq_w[1][:, part(2 * mb + j, P)], wbq_s[WB_ROW:P, part(4 + 2 * mb + j, P)],
+                   hq[2 + mb][0][:], hq[2 + mb][1][:], True, True)
+            for j in tiles:
+                nc.vector.tensor_tensor(gated[:, j, part(mb, P)], acc[:, j, :], gate_rows[:, part(mb, P)], MULT)
+
+        def add_scatter(j, mb, blocks):
+            cols = slice(mb * P, (mb + blocks) * P)
+            nc.vector.tensor_tensor(
+                result[j][:].indirect(idx[:, (2 + mb) * P // 16 : (2 + mb + blocks) * P // 16]),
+                gated[:, j, cols],
+                base_second[:, j, cols],
+                ADD,
+            )
+
+        gate_block(0, [1, 0], 5)
+        add_scatter(1, 0, 1)
+        scatter_first_pair(1)
+        gate_block(1, [0, 1], 6)
+        add_scatter(0, 0, 2)
+        nc.sync.dma_start(out[part(0, P), :], result[0][:])
+        add_scatter(1, 1, 1)
+        nc.sync.dma_start(out[part(1, P), :], result[1][:])

@@ -21,7 +21,7 @@ COPY = mybir.ActivationFunctionType.Copy
 
 X_ROW = (0, 4)
 W_ROW = (0, 4)
-WA_ROW = (12, 8)
+WA_ROW = (8, 12)
 WB_ROW = 8
 WA_RAW = 96
 
@@ -108,13 +108,8 @@ def tile_moe_dyl_none_kernel(
             nc.sync.dma_start(gate_col[:], gate[0, 0 : 2 * P].rearrange("(b p) -> p b", p=P))
         nc.sync.dma_start(gate_rows[:], gate[:, 2 * P : SLOTS])
 
-        waq_listed = sb("waq_listed", [P, B * H], U8)
-        gather(waq_listed[:], wa_s[:], idx2, 0, B * H)
         waq_rows = sb("waq_rows", [P, B * H], U8)
-        nc.vector.tensor_copy(
-            waq_rows[:].rearrange("p (m t q) -> p m t q", m=B, t=4),
-            waq_listed[:].rearrange("p (m q t) -> p m t q", m=B, t=4),
-        )
+        gather(waq_rows[:], wa_s[:], idx2, 0, B * H)
 
         def move_rows(s, tile):
             for r in range(4):
@@ -132,8 +127,9 @@ def tile_moe_dyl_none_kernel(
         for s in range(2):
             gather(xq_w[s][:], x_w[:, s, :].bitcast(U32), idx, 0, SLOTS)
 
-        waq_first = sb("waq_first", [P, B, 4, P], U32)
-        gather(waq_first[:].rearrange("p m t q -> p m q t"), wa_w[0][:].bitcast(U32), idx2, 0, B * H)
+        waq_first = sb("waq_first", [P, B * H], U32)
+        for pair in range(2):
+            gather(waq_first[:, part(pair, 2 * H)], wa_w[0][:].bitcast(U32), idx2, pair * 2 * H, 2 * H)
         wbq_s = reuse("wbq_s", [P, B * N], U8, "wa_w0")
         gather(wbq_s[:], wb_s[:], idx3, 0, B * N)
 
@@ -164,23 +160,27 @@ def tile_moe_dyl_none_kernel(
         nc.scalar.copy(base_second[:], acc[:])
 
         def h_pass(m, s, words):
-            for t in range(4):
-                mm(h_acc[m][:, t, :], words[:, t, :], waq_s[s][WA_ROW[s] : P, part(4 * m + t, P)],
-                   xq_w[s][:, part(m, P)], xq_s[X_ROW[s] : P, part(m, P)],
-                   s == 0 and t == 0, s == 1 and t == 3)
+            mm(h_acc[m][:], xq_w[s][:, part(m, P)], xq_s[X_ROW[s] : P, part(m, P)],
+               words, waq_s[s][WA_ROW[s] : P, part(m, H)], s == 0, s == 1)
 
         h_acc = []
         for m in range(B):
-            h_acc.append(bank("h_acc", [P, 4, P], m))
-            h_pass(m, 0, waq_first[:, m])
+            h_acc.append(bank("h_acc", [P, H], m))
+            h_pass(m, 0, waq_first[:, part(m, H)])
 
         grouped = []
         for m in range(B):
-            waq_second = sb("waq_second%d" % m, [P, 4, P], U32)
-            gather(waq_second[:].rearrange("p t q -> p q t"), wa_w[1][:].bitcast(U32), idx2, m * H, H)
-            h_pass(m, 1, waq_second)
-            grouped.append(sb("grouped%d" % m, [P, P, 4], BF16))
-            nc.scalar.copy(grouped[m][:], h_acc[m][:].rearrange("p t u -> p u t"))
+            waq_second = sb("waq_second%d" % m, [P, H], U32)
+            gather(waq_second[:], wa_w[1][:].bitcast(U32), idx2, m * H, H)
+            h_pass(m, 1, waq_second[:])
+            h_bf = reuse("h_bf%d" % m, [P, 2, P, 2], BF16, "h_bf%d" % (m % 2))
+            nc.scalar.copy(h_bf[:], h_acc[m][:].rearrange("s (p u e) -> s u p e", u=2, e=2))
+            h_words = h_bf[:].rearrange("s u p e -> s (u p e)").bitcast(F32)
+            turned = bank("turned%d" % m, [P, 2, P], 4 + m % 2)
+            for u in range(2):
+                nc.tensor.transpose(turned[:, u, :], h_words[:, part(u, P)], ident[:])
+            grouped.append(sb("grouped%d" % m, [P, P, 2], F32))
+            nc.scalar.copy(grouped[m][:], turned[:].rearrange("p u s -> p s u"))
 
         hq = []
 
@@ -188,7 +188,7 @@ def tile_moe_dyl_none_kernel(
             hq_w = sb("hq_w%d" % m, [P, P], U32)
             hq_s = sb("hq_s%d" % m, [P, P], U8)
             nc.vector.quantize_mx(
-                out=hq_w[:].bitcast(FP8X4), scales=hq_s[:], in_=grouped[m][:].rearrange("p u t -> p (u t)")
+                out=hq_w[:].bitcast(FP8X4), scales=hq_s[:], in_=grouped[m][:].rearrange("p s u -> p (s u)").bitcast(BF16)
             )
             hq.append((hq_w, hq_s))
 
@@ -198,7 +198,7 @@ def tile_moe_dyl_none_kernel(
         backs = []
         for m in range(2):
             quantise(m)
-            y_slots = bank("y_slots", [P, N], 4 + m)
+            y_slots = bank("y_slots", [P, N], m)
             mm(y_slots[:], hq[m][0][:], hq[m][1][:], wbq_w[0][:, part(m, N)], wbq_s[WB_ROW:P, part(m, N)], True, True)
             y_gated = sb("y_gated%d" % m, [P, N], F32)
             nc.scalar.activation(y_gated[:], y_slots[:], COPY, scale=gate_col[:, m : m + 1])
@@ -243,7 +243,7 @@ def tile_moe_dyl_none_kernel(
                 ADD,
             )
 
-        gate_block(0, [1, 0], 5)
+        gate_block(0, [1, 0], 1)
         add_scatter(1, 0, 1)
         scatter_first_pair(1)
         gate_block(1, [0, 1], 6)

@@ -21,7 +21,7 @@ COPY = mybir.ActivationFunctionType.Copy
 
 X_ROW = (0, 4)
 W_ROW = (0, 4)
-WA_ROW = (8, 12)
+WA_ROW = (12, 8)
 WB_ROW = 8
 WA_RAW = 96
 
@@ -88,19 +88,38 @@ def tile_moe_dyl_none_kernel(
         diagonal = sb("diagonal", [P, P], I32)
 
         nc.gpsimd.iota(diagonal[:], [[1, P]], base=0, channel_multiplier=-1)
-        for tile in (wb_s[:], x_s[:], wa_s[0:WA_RAW, :]):
+        load_scales(nc.gpsimd, w_s, w_scales, W_ROW[0])
+        for tile in (wa_s[0:WA_RAW, :], x_s[:], wb_s[:]):
             nc.vector.memset(tile.bitcast(I32), 0)
         nc.vector.tensor_scalar(ident[:], diagonal[:], 0, None, mybir.AluOpType.is_equal)
-
         load_scales(nc.gpsimd, wb_s, wb_scales, WB_ROW)
-        load_scales(nc.scalar, w_s, w_scales, W_ROW[0])
-        load_scales(nc.scalar, x_s, x_scales, X_ROW[0])
-        nc.sync.dma_start(wa_s[WA_RAW:P, :].bitcast(I32), wa_scales.rearrange("s b c -> (s b) c").bitcast(I32))
+
         nc.sync.dma_start(idx2[:], offs2)
-        nc.sync.dma_start(x_w[:], x_words.rearrange("s p n t -> p s (n t)").bitcast(I32))
         nc.sync.dma_start(idx[:], offs)
+        nc.sync.dma_start(wa_s[WA_RAW:P, :].bitcast(I32), wa_scales.rearrange("s b c -> (s b) c").bitcast(I32))
+        load_scales(nc.scalar, x_s, x_scales, X_ROW[0])
+        nc.sync.dma_start(x_w[:], x_words.rearrange("s p n t -> p s (n t)").bitcast(I32))
         nc.sync.dma_start(w_w[:], w_words.rearrange("s p n t -> p s (n t)").bitcast(I32))
         load_words(wa_w[0][:], wa_words[0])
+
+        waq_listed = sb("waq_listed", [P, B * H], U8)
+        gather(waq_listed[:], wa_s[:], idx2, 0, B * H)
+        waq_rows = sb("waq_rows", [P, B * H], U8)
+        nc.vector.tensor_copy(
+            waq_rows[:].rearrange("p (m t q) -> p m t q", m=B, t=4),
+            waq_listed[:].rearrange("p (m q t) -> p m t q", m=B, t=4),
+        )
+
+        def move_rows(queue, s, tile):
+            for r in range(4):
+                raw = WA_RAW + 16 * s
+                queue.dma_start(
+                    tile[WA_ROW[s] + r : P : 32, :].bitcast(I32), waq_rows[raw + r : raw + 16 : 4, :].bitcast(I32)
+                )
+
+        waq_s = [sb("waq_s0", [P, B * H], U8)]
+        move_rows(nc.sync, 0, waq_s[0])
+
         nc.sync.dma_start(idx3[:], offs3)
         load_words(wa_w[1][:], wa_words[1])
         load_words(wb_w[:], wb_words[0])
@@ -108,30 +127,18 @@ def tile_moe_dyl_none_kernel(
             nc.sync.dma_start(gate_col[:], gate[0, 0 : 2 * P].rearrange("(b p) -> p b", p=P))
         nc.sync.dma_start(gate_rows[:], gate[:, 2 * P : SLOTS])
 
-        waq_rows = sb("waq_rows", [P, B * H], U8)
-        gather(waq_rows[:], wa_s[:], idx2, 0, B * H)
-
-        def move_rows(s, tile):
-            for r in range(4):
-                raw = WA_RAW + 16 * s
-                nc.scalar.dma_start(
-                    tile[WA_ROW[s] + r : P : 32, :].bitcast(I32), waq_rows[raw + r : raw + 16 : 4, :].bitcast(I32)
-                )
-
-        waq_s = [sb("waq_s0", [P, B * H], U8)]
-        move_rows(0, waq_s[0])
-
         xq_s = sb("xq_s", [P, SLOTS], U8)
         gather(xq_s[:], x_s[:], idx, 0, SLOTS)
         xq_w = [sb("xq_w%d" % s, [P, SLOTS], U32) for s in range(2)]
         for s in range(2):
             gather(xq_w[s][:], x_w[:, s, :].bitcast(U32), idx, 0, SLOTS)
 
-        waq_first = sb("waq_first", [P, B * H], U32)
-        for pair in range(2):
-            gather(waq_first[:, part(pair, 2 * H)], wa_w[0][:].bitcast(U32), idx2, pair * 2 * H, 2 * H)
-        wbq_s = reuse("wbq_s", [P, B * N], U8, "wa_w0")
-        gather(wbq_s[:], wb_s[:], idx3, 0, B * N)
+        waq_first = []
+        for m in range(B):
+            waq_first.append(sb("waq_first%d" % m, [P, 4, P], U32))
+            gather(waq_first[m][:].rearrange("p t q -> p q t"), wa_w[0][:].bitcast(U32), idx2, m * H, H)
+        wbq_s = [reuse("wbq_s0", [P, 2 * N], U8, "wa_w0")]
+        gather(wbq_s[0][:], wb_s[:], idx3, 0, 2 * N)
 
         result = [sb("result%d" % j, [P, T], F32) for j in range(2)]
         for j in range(2):
@@ -155,32 +162,28 @@ def tile_moe_dyl_none_kernel(
             for s in range(2):
                 mm(acc[:, j, :], w_w[:, s, part(j, P)], w_s[W_ROW[s] : P, part(j, P)],
                    xq_w[s][:, part(1, 2 * P)], xq_s[X_ROW[s] : P, part(1, 2 * P)], s == 0, s == 1)
-        waq_s.append(reuse("waq_s1", [P, B * H], U8, "w_s"))
-        move_rows(1, waq_s[1])
         nc.scalar.copy(base_second[:], acc[:])
 
         def h_pass(m, s, words):
-            mm(h_acc[m][:], xq_w[s][:, part(m, P)], xq_s[X_ROW[s] : P, part(m, P)],
-               words, waq_s[s][WA_ROW[s] : P, part(m, H)], s == 0, s == 1)
+            for t in range(4):
+                mm(h_acc[m][:, t, :], words[:, t, :], waq_s[s][WA_ROW[s] : P, part(4 * m + t, P)],
+                   xq_w[s][:, part(m, P)], xq_s[X_ROW[s] : P, part(m, P)],
+                   s == 0 and t == 0, s == 1 and t == 3)
 
         h_acc = []
         for m in range(B):
-            h_acc.append(bank("h_acc", [P, H], m))
-            h_pass(m, 0, waq_first[:, part(m, H)])
+            h_acc.append(bank("h_acc", [P, 4, P], m))
+            h_pass(m, 0, waq_first[m])
+        waq_s.append(reuse("waq_s1", [P, B * H], U8, "waq_first0"))
+        move_rows(nc.scalar, 1, waq_s[1])
 
         grouped = []
         for m in range(B):
-            waq_second = sb("waq_second%d" % m, [P, H], U32)
-            gather(waq_second[:], wa_w[1][:].bitcast(U32), idx2, m * H, H)
-            h_pass(m, 1, waq_second[:])
-            h_bf = reuse("h_bf%d" % m, [P, 2, P, 2], BF16, "h_bf%d" % (m % 2))
-            nc.scalar.copy(h_bf[:], h_acc[m][:].rearrange("s (p u e) -> s u p e", u=2, e=2))
-            h_words = h_bf[:].rearrange("s u p e -> s (u p e)").bitcast(F32)
-            turned = bank("turned%d" % m, [P, 2, P], 4 + m % 2)
-            for u in range(2):
-                nc.tensor.transpose(turned[:, u, :], h_words[:, part(u, P)], ident[:])
-            grouped.append(sb("grouped%d" % m, [P, P, 2], F32))
-            nc.scalar.copy(grouped[m][:], turned[:].rearrange("p u s -> p s u"))
+            waq_second = sb("waq_second%d" % m, [P, 4, P], U32)
+            gather(waq_second[:].rearrange("p t q -> p q t"), wa_w[1][:].bitcast(U32), idx2, m * H, H)
+            h_pass(m, 1, waq_second)
+            grouped.append(sb("grouped%d" % m, [P, P, 4], BF16))
+            nc.scalar.copy(grouped[m][:], h_acc[m][:].rearrange("p t u -> p u t"))
 
         hq = []
 
@@ -188,18 +191,21 @@ def tile_moe_dyl_none_kernel(
             hq_w = sb("hq_w%d" % m, [P, P], U32)
             hq_s = sb("hq_s%d" % m, [P, P], U8)
             nc.vector.quantize_mx(
-                out=hq_w[:].bitcast(FP8X4), scales=hq_s[:], in_=grouped[m][:].rearrange("p s u -> p (s u)").bitcast(BF16)
+                out=hq_w[:].bitcast(FP8X4), scales=hq_s[:], in_=grouped[m][:].rearrange("p u t -> p (u t)")
             )
             hq.append((hq_w, hq_s))
 
-        wbq_w = [sb("wbq_w0", [P, 2 * N], U32)]
-        gather(wbq_w[0][:], wb_w[:].bitcast(U32), idx3, 0, 2 * N)
+        wbq_w = []
 
-        backs = []
-        for m in range(2):
-            quantise(m)
+        def gather_wb(m):
+            name = "wbq_w%d" % m
+            behind = (name, "grouped0", "hq_w0", "grouped2")[m]
+            wbq_w.append(reuse(name, [P, N], U32, behind))
+            gather(wbq_w[m][:], wb_w[:].bitcast(U32), idx3, m * N, N)
+
+        def gate_slots(m):
             y_slots = bank("y_slots", [P, N], m)
-            mm(y_slots[:], hq[m][0][:], hq[m][1][:], wbq_w[0][:, part(m, N)], wbq_s[WB_ROW:P, part(m, N)], True, True)
+            mm(y_slots[:], hq[m][0][:], hq[m][1][:], wbq_w[m][:], wbq_s[0][WB_ROW:P, part(m, N)], True, True)
             y_gated = sb("y_gated%d" % m, [P, N], F32)
             nc.scalar.activation(y_gated[:], y_slots[:], COPY, scale=gate_col[:, m : m + 1])
             back = bank("back", [P, 2, P], 6 + m)
@@ -207,29 +213,38 @@ def tile_moe_dyl_none_kernel(
                 for j in range(2):
                     nc.tensor.matmul(back[:, j, :], source[:, part(j, P)], ident[:], is_transpose=True,
                                      start=step == 0 and j == 0, stop=step == 1 and j == 1)
-            backs.append(back)
+            return back
 
-        for m in range(2, B):
+        backs = []
+        for m in range(2):
+            gather_wb(m)
             quantise(m)
-        wbq_w.append(reuse("wbq_w1", [P, 2 * N], U32, "grouped1"))
+            backs.append(gate_slots(m))
+        wbq_s.append(reuse("wbq_s1", [P, 2 * N], U8, "grouped1"))
+        gather(wbq_s[1][:], wb_s[:], idx3, 2 * N, 2 * N)
         for m in range(2, B):
-            gather(wbq_w[1][:, part(m - 2, N)], wb_w[:].bitcast(U32), idx3, m * N, N)
+            gather_wb(m)
+            quantise(m)
 
         summed = sb("summed", [P, 2, 2 * P], F32)
+
+        def scatter(j, m, blocks):
+            nc.scalar.activation(
+                result[j][:].indirect(idx[:, m * P // 16 : (m + blocks) * P // 16]),
+                summed[:, j, m * P : (m + blocks) * P],
+                COPY,
+            )
+
         for m in range(2):
             nc.scalar.copy(summed[:, :, part(m, P)], backs[m][:])
-
-        def scatter_first_pair(j):
-            nc.scalar.activation(result[j][:].indirect(idx[:, 0 : 2 * P // 16]), summed[:, j, :], COPY)
-
-        scatter_first_pair(0)
+            scatter(0, m, 1)
 
         gated = sb("gated", [P, 2, 2 * P], F32)
 
         def gate_block(mb, tiles, number):
             acc = bank("y_rows", [P, 2, P], number)
             for j in tiles:
-                mm(acc[:, j, :], wbq_w[1][:, part(2 * mb + j, P)], wbq_s[WB_ROW:P, part(4 + 2 * mb + j, P)],
+                mm(acc[:, j, :], wbq_w[2 + mb][:, part(j, P)], wbq_s[1][WB_ROW:P, part(2 * mb + j, P)],
                    hq[2 + mb][0][:], hq[2 + mb][1][:], True, True)
             for j in tiles:
                 nc.vector.tensor_tensor(gated[:, j, part(mb, P)], acc[:, j, :], gate_rows[:, part(mb, P)], MULT)
@@ -245,7 +260,7 @@ def tile_moe_dyl_none_kernel(
 
         gate_block(0, [1, 0], 1)
         add_scatter(1, 0, 1)
-        scatter_first_pair(1)
+        scatter(1, 0, 2)
         gate_block(1, [0, 1], 6)
         add_scatter(0, 0, 2)
         nc.sync.dma_start(out[part(0, P), :], result[0][:])

@@ -110,18 +110,20 @@ def tile_moe_dyl_none_kernel(
             waq_listed[:].rearrange("p (m q t) -> p m t q", m=B, t=4),
         )
 
-        def move_rows(queue, s, tile):
+        def move_rows(s, tile):
             for r in range(4):
                 raw = WA_RAW + 16 * s
-                queue.dma_start(
+                nc.sync.dma_start(
                     tile[WA_ROW[s] + r : P : 32, :].bitcast(I32), waq_rows[raw + r : raw + 16 : 4, :].bitcast(I32)
                 )
 
         waq_s = [sb("waq_s0", [P, B * H], U8)]
-        move_rows(nc.sync, 0, waq_s[0])
+        move_rows(0, waq_s[0])
 
-        nc.sync.dma_start(idx3[:], offs3)
         load_words(wa_w[1][:], wa_words[1])
+        nc.sync.dma_start(idx3[:], offs3)
+        waq_s.append(sb("waq_s1", [P, B * H], U8))
+        move_rows(1, waq_s[1])
         load_words(wb_w[:], wb_words[0])
         with nc.allow_non_contiguous_dma(reason="one gate value a partition and block"):
             nc.sync.dma_start(gate_col[:], gate[0, 0 : 2 * P].rearrange("(b p) -> p b", p=P))
@@ -137,8 +139,6 @@ def tile_moe_dyl_none_kernel(
         for m in range(B):
             waq_first.append(sb("waq_first%d" % m, [P, 4, P], U32))
             gather(waq_first[m][:].rearrange("p t q -> p q t"), wa_w[0][:].bitcast(U32), idx2, m * H, H)
-        wbq_s = [reuse("wbq_s0", [P, 2 * N], U8, "wa_w0")]
-        gather(wbq_s[0][:], wb_s[:], idx3, 0, 2 * N)
 
         result = [sb("result%d" % j, [P, T], F32) for j in range(2)]
         for j in range(2):
@@ -174,8 +174,6 @@ def tile_moe_dyl_none_kernel(
         for m in range(B):
             h_acc.append(bank("h_acc", [P, 4, P], m))
             h_pass(m, 0, waq_first[m])
-        waq_s.append(reuse("waq_s1", [P, B * H], U8, "waq_first0"))
-        move_rows(nc.scalar, 1, waq_s[1])
 
         grouped = []
         for m in range(B):
@@ -185,10 +183,14 @@ def tile_moe_dyl_none_kernel(
             grouped.append(sb("grouped%d" % m, [P, P, 4], BF16))
             nc.scalar.copy(grouped[m][:], h_acc[m][:].rearrange("p t u -> p u t"))
 
+        wbq_s = [sb("wbq_s0", [P, 2 * N], U8)]
+        gather(wbq_s[0][:], wb_s[:], idx3, 0, 2 * N)
+
         hq = []
 
         def quantise(m):
-            hq_w = sb("hq_w%d" % m, [P, P], U32)
+            name = "hq_w%d" % m
+            hq_w = reuse(name, [P, P], U32, (name, name, "hq_s0", "hq_w1")[m])
             hq_s = sb("hq_s%d" % m, [P, P], U8)
             nc.vector.quantize_mx(
                 out=hq_w[:].bitcast(FP8X4), scales=hq_s[:], in_=grouped[m][:].rearrange("p u t -> p (u t)")
@@ -199,7 +201,7 @@ def tile_moe_dyl_none_kernel(
 
         def gather_wb(m):
             name = "wbq_w%d" % m
-            behind = (name, "grouped0", "hq_w0", "grouped2")[m]
+            behind = (name, name, "grouped1", "grouped2")[m]
             wbq_w.append(reuse(name, [P, N], U32, behind))
             gather(wbq_w[m][:], wb_w[:].bitcast(U32), idx3, m * N, N)
 
@@ -220,7 +222,7 @@ def tile_moe_dyl_none_kernel(
             gather_wb(m)
             quantise(m)
             backs.append(gate_slots(m))
-        wbq_s.append(reuse("wbq_s1", [P, 2 * N], U8, "grouped1"))
+        wbq_s.append(reuse("wbq_s1", [P, 2 * N], U8, "hq_w0"))
         gather(wbq_s[1][:], wb_s[:], idx3, 2 * N, 2 * N)
         for m in range(2, B):
             gather_wb(m)

@@ -95,8 +95,8 @@ def tile_moe_dyl_none_kernel(
         load_scales(nc.gpsimd, wb_s, wb_scales, WB_ROW)
 
         nc.sync.dma_start(idx2[:], offs2)
-        nc.sync.dma_start(idx[:], offs)
         nc.sync.dma_start(wa_s[WA_RAW:P, :].bitcast(I32), wa_scales.rearrange("s b c -> (s b) c").bitcast(I32))
+        nc.sync.dma_start(idx[:], offs)
         load_scales(nc.scalar, x_s, x_scales, X_ROW[0])
         nc.sync.dma_start(x_w[:], x_words.rearrange("s p n t -> p s (n t)").bitcast(I32))
         nc.sync.dma_start(w_w[:], w_words.rearrange("s p n t -> p s (n t)").bitcast(I32))
@@ -176,12 +176,19 @@ def tile_moe_dyl_none_kernel(
             h_pass(m, 0, waq_first[m])
 
         grouped = []
-        for m in range(B):
-            waq_second = sb("waq_second%d" % m, [P, 4, P], U32)
+
+        def close_h(m, tag):
+            waq_second = reuse("waq_second%d" % m, [P, 4, P], U32, tag)
             gather(waq_second[:].rearrange("p t q -> p q t"), wa_w[1][:].bitcast(U32), idx2, m * H, H)
             h_pass(m, 1, waq_second)
-            grouped.append(sb("grouped%d" % m, [P, P, 4], BF16))
+
+        def round_h(m, tag):
+            grouped.append(reuse("grouped%d" % m, [P, P, 4], BF16, tag))
             nc.scalar.copy(grouped[m][:], h_acc[m][:].rearrange("p t u -> p u t"))
+
+        for m in range(B - 1):
+            close_h(m, "waq_second%d" % m)
+            round_h(m, "grouped%d" % m)
 
         wbq_s = [sb("wbq_s0", [P, 2 * N], U8)]
         gather(wbq_s[0][:], wb_s[:], idx3, 0, 2 * N)
@@ -190,7 +197,7 @@ def tile_moe_dyl_none_kernel(
 
         def quantise(m):
             name = "hq_w%d" % m
-            hq_w = reuse(name, [P, P], U32, (name, name, "hq_s0", "hq_w1")[m])
+            hq_w = reuse(name, [P, P], U32, (name, "hq_s0", "wbq_w1", name)[m])
             hq_s = sb("hq_s%d" % m, [P, P], U8)
             nc.vector.quantize_mx(
                 out=hq_w[:].bitcast(FP8X4), scales=hq_s[:], in_=grouped[m][:].rearrange("p u t -> p (u t)")
@@ -201,7 +208,7 @@ def tile_moe_dyl_none_kernel(
 
         def gather_wb(m):
             name = "wbq_w%d" % m
-            behind = (name, name, "grouped1", "grouped2")[m]
+            behind = (name, name, "hq_s0", "grouped2")[m]
             wbq_w.append(reuse(name, [P, N], U32, behind))
             gather(wbq_w[m][:], wb_w[:].bitcast(U32), idx3, m * N, N)
 
@@ -222,11 +229,12 @@ def tile_moe_dyl_none_kernel(
             gather_wb(m)
             quantise(m)
             backs.append(gate_slots(m))
-        wbq_s.append(reuse("wbq_s1", [P, 2 * N], U8, "hq_w0"))
+        close_h(B - 1, "wbq_w0")
+        wbq_s.append(reuse("wbq_s1", [P, 2 * N], U8, "hq_s1"))
         gather(wbq_s[1][:], wb_s[:], idx3, 2 * N, 2 * N)
+        quantise(2)
         for m in range(2, B):
             gather_wb(m)
-            quantise(m)
 
         summed = sb("summed", [P, 2, 2 * P], F32)
 
@@ -237,9 +245,12 @@ def tile_moe_dyl_none_kernel(
                 COPY,
             )
 
-        for m in range(2):
-            nc.scalar.copy(summed[:, :, part(m, P)], backs[m][:])
-            scatter(0, m, 1)
+        nc.scalar.copy(summed[:, :, part(0, P)], backs[0][:])
+        scatter(0, 0, 1)
+        round_h(B - 1, "y_gated0")
+        quantise(B - 1)
+        nc.scalar.copy(summed[:, :, part(1, P)], backs[1][:])
+        scatter(0, 1, 1)
 
         gated = sb("gated", [P, 2, 2 * P], F32)
 

@@ -49,9 +49,9 @@ def tile_moe_dyl_none_kernel(
         def load_words(tile, words):
             nc.sync.dma_start(tile, words.rearrange("p n t -> p (n t)").bitcast(I32))
 
-        def load_scales(queue, tile, scales, first_row):
+        def load_scales(queue, tile, scales, first_row, sets=range(4)):
             rows = 4 * scales.shape[0]
-            for q in range(4):
+            for q in sets:
                 queue.dma_start(
                     tile[32 * q + first_row : 32 * q + first_row + rows, :].bitcast(I32),
                     scales[:, 4 * q : 4 * q + 4, :].bitcast(I32),
@@ -92,7 +92,7 @@ def tile_moe_dyl_none_kernel(
         for tile in (wa_s[0:WA_RAW, :], x_s[:], wb_s[:]):
             nc.vector.memset(tile.bitcast(I32), 0)
         nc.vector.tensor_scalar(ident[:], diagonal[:], 0, None, mybir.AluOpType.is_equal)
-        load_scales(nc.gpsimd, wb_s, wb_scales, WB_ROW)
+        load_scales(nc.gpsimd, wb_s, wb_scales, WB_ROW, range(1))
 
         nc.sync.dma_start(idx2[:], offs2)
         nc.sync.dma_start(wa_s[WA_RAW:P, :].bitcast(I32), wa_scales.rearrange("s b c -> (s b) c").bitcast(I32))
@@ -110,20 +110,22 @@ def tile_moe_dyl_none_kernel(
             waq_listed[:].rearrange("p (m q t) -> p m t q", m=B, t=4),
         )
 
-        def move_rows(s, tile):
-            for r in range(4):
-                raw = WA_RAW + 16 * s
-                nc.sync.dma_start(
-                    tile[WA_ROW[s] + r : P : 32, :].bitcast(I32), waq_rows[raw + r : raw + 16 : 4, :].bitcast(I32)
-                )
+        waq_s = [sb("waq_s%d" % s, [P, B * H], U8) for s in range(2)]
 
-        waq_s = [sb("waq_s0", [P, B * H], U8)]
-        move_rows(0, waq_s[0])
+        def move_row(s, r):
+            raw = WA_RAW + 16 * s
+            nc.sync.dma_start(
+                waq_s[s][WA_ROW[s] + r : P : 32, :].bitcast(I32), waq_rows[raw + r : raw + 16 : 4, :].bitcast(I32)
+            )
 
-        load_words(wa_w[1][:], wa_words[1])
+        moves = [(s, r) for s in (1, 0) for r in range(4)]
         nc.sync.dma_start(idx3[:], offs3)
-        waq_s.append(sb("waq_s1", [P, B * H], U8))
-        move_rows(1, waq_s[1])
+        load_scales(nc.sync, wb_s, wb_scales, WB_ROW, range(1, 4))
+        for move in moves[:2]:
+            move_row(*move)
+        load_words(wa_w[1][:], wa_words[1])
+        for move in moves[2:]:
+            move_row(*move)
         load_words(wb_w[:], wb_words[0])
         with nc.allow_non_contiguous_dma(reason="one gate value a partition and block"):
             nc.sync.dma_start(gate_col[:], gate[0, 0 : 2 * P].rearrange("(b p) -> p b", p=P))
@@ -135,10 +137,10 @@ def tile_moe_dyl_none_kernel(
         for s in range(2):
             gather(xq_w[s][:], x_w[:, s, :].bitcast(U32), idx, 0, SLOTS)
 
-        waq_first = []
-        for m in range(B):
-            waq_first.append(sb("waq_first%d" % m, [P, 4, P], U32))
-            gather(waq_first[m][:].rearrange("p t q -> p q t"), wa_w[0][:].bitcast(U32), idx2, m * H, H)
+        waq_first = sb("waq_first", [P, B, 4, P], U32)
+        gather(waq_first[:].rearrange("p m t q -> p m q t"), wa_w[0][:].bitcast(U32), idx2, 0, B * H)
+        wbq_s = sb("wbq_s", [P, B * N], U8)
+        gather(wbq_s[:], wb_s[:], idx3, 0, B * N)
 
         result = [sb("result%d" % j, [P, T], F32) for j in range(2)]
         for j in range(2):
@@ -170,16 +172,14 @@ def tile_moe_dyl_none_kernel(
                    xq_w[s][:, part(m, P)], xq_s[X_ROW[s] : P, part(m, P)],
                    s == 0 and t == 0, s == 1 and t == 3)
 
-        h_acc = []
-        for m in range(B):
-            h_acc.append(bank("h_acc", [P, 4, P], m))
-            h_pass(m, 0, waq_first[m])
+        h_acc = [bank("h_acc", [P, 4, P], m) for m in range(B)]
 
         grouped = []
 
         def close_h(m, tag):
             waq_second = reuse("waq_second%d" % m, [P, 4, P], U32, tag)
             gather(waq_second[:].rearrange("p t q -> p q t"), wa_w[1][:].bitcast(U32), idx2, m * H, H)
+            h_pass(m, 0, waq_first[:, m])
             h_pass(m, 1, waq_second)
 
         def round_h(m, tag):
@@ -190,14 +190,11 @@ def tile_moe_dyl_none_kernel(
             close_h(m, "waq_second%d" % m)
             round_h(m, "grouped%d" % m)
 
-        wbq_s = [sb("wbq_s0", [P, 2 * N], U8)]
-        gather(wbq_s[0][:], wb_s[:], idx3, 0, 2 * N)
-
         hq = []
 
         def quantise(m):
             name = "hq_w%d" % m
-            hq_w = reuse(name, [P, P], U32, (name, "hq_s0", "wbq_w1", name)[m])
+            hq_w = reuse(name, [P, P], U32, (name, "hq_s0", "hq_s1", "hq_s1")[m])
             hq_s = sb("hq_s%d" % m, [P, P], U8)
             nc.vector.quantize_mx(
                 out=hq_w[:].bitcast(FP8X4), scales=hq_s[:], in_=grouped[m][:].rearrange("p u t -> p (u t)")
@@ -208,13 +205,13 @@ def tile_moe_dyl_none_kernel(
 
         def gather_wb(m):
             name = "wbq_w%d" % m
-            behind = (name, name, "hq_s0", "grouped2")[m]
+            behind = (name, "grouped0", "hq_s0", "grouped2")[m]
             wbq_w.append(reuse(name, [P, N], U32, behind))
             gather(wbq_w[m][:], wb_w[:].bitcast(U32), idx3, m * N, N)
 
         def gate_slots(m):
             y_slots = bank("y_slots", [P, N], m)
-            mm(y_slots[:], hq[m][0][:], hq[m][1][:], wbq_w[m][:], wbq_s[0][WB_ROW:P, part(m, N)], True, True)
+            mm(y_slots[:], hq[m][0][:], hq[m][1][:], wbq_w[m][:], wbq_s[WB_ROW:P, part(m, N)], True, True)
             y_gated = sb("y_gated%d" % m, [P, N], F32)
             nc.scalar.activation(y_gated[:], y_slots[:], COPY, scale=gate_col[:, m : m + 1])
             back = bank("back", [P, 2, P], 6 + m)
@@ -230,8 +227,6 @@ def tile_moe_dyl_none_kernel(
             quantise(m)
             backs.append(gate_slots(m))
         close_h(B - 1, "wbq_w0")
-        wbq_s.append(reuse("wbq_s1", [P, 2 * N], U8, "hq_s1"))
-        gather(wbq_s[1][:], wb_s[:], idx3, 2 * N, 2 * N)
         quantise(2)
         for m in range(2, B):
             gather_wb(m)
@@ -248,7 +243,6 @@ def tile_moe_dyl_none_kernel(
         nc.scalar.copy(summed[:, :, part(0, P)], backs[0][:])
         scatter(0, 0, 1)
         round_h(B - 1, "y_gated0")
-        quantise(B - 1)
         nc.scalar.copy(summed[:, :, part(1, P)], backs[1][:])
         scatter(0, 1, 1)
 
@@ -257,7 +251,7 @@ def tile_moe_dyl_none_kernel(
         def gate_block(mb, tiles, number):
             acc = bank("y_rows", [P, 2, P], number)
             for j in tiles:
-                mm(acc[:, j, :], wbq_w[2 + mb][:, part(j, P)], wbq_s[1][WB_ROW:P, part(2 * mb + j, P)],
+                mm(acc[:, j, :], wbq_w[2 + mb][:, part(j, P)], wbq_s[WB_ROW:P, part(4 + 2 * mb + j, P)],
                    hq[2 + mb][0][:], hq[2 + mb][1][:], True, True)
             for j in tiles:
                 nc.vector.tensor_tensor(gated[:, j, part(mb, P)], acc[:, j, :], gate_rows[:, part(mb, P)], MULT)
@@ -272,6 +266,7 @@ def tile_moe_dyl_none_kernel(
             )
 
         gate_block(0, [1, 0], 1)
+        quantise(B - 1)
         add_scatter(1, 0, 1)
         scatter(1, 0, 2)
         gate_block(1, [0, 1], 6)

@@ -49,9 +49,9 @@ def tile_moe_dyl_none_kernel(
         def load_words(tile, words):
             nc.sync.dma_start(tile, words.rearrange("p n t -> p (n t)").bitcast(I32))
 
-        def load_scales(queue, tile, scales, first_row, sets=range(4)):
+        def load_scales(queue, tile, scales, first_row):
             rows = 4 * scales.shape[0]
-            for q in sets:
+            for q in range(4):
                 queue.dma_start(
                     tile[32 * q + first_row : 32 * q + first_row + rows, :].bitcast(I32),
                     scales[:, 4 * q : 4 * q + 4, :].bitcast(I32),
@@ -89,16 +89,16 @@ def tile_moe_dyl_none_kernel(
 
         nc.gpsimd.iota(diagonal[:], [[1, P]], base=0, channel_multiplier=-1)
         load_scales(nc.gpsimd, w_s, w_scales, W_ROW[0])
-        for tile in (wa_s[0:WA_RAW, :], x_s[:], wb_s[:]):
+        for tile in (x_s[:], wa_s[0:WA_RAW, :], wb_s[:]):
             nc.vector.memset(tile.bitcast(I32), 0)
         nc.vector.tensor_scalar(ident[:], diagonal[:], 0, None, mybir.AluOpType.is_equal)
-        load_scales(nc.gpsimd, wb_s, wb_scales, WB_ROW, range(1))
 
-        nc.sync.dma_start(idx2[:], offs2)
-        nc.sync.dma_start(wa_s[WA_RAW:P, :].bitcast(I32), wa_scales.rearrange("s b c -> (s b) c").bitcast(I32))
-        nc.sync.dma_start(idx[:], offs)
+        nc.scalar.dma_start(wa_s[WA_RAW:P, :].bitcast(I32), wa_scales.rearrange("s b c -> (s b) c").bitcast(I32))
         load_scales(nc.scalar, x_s, x_scales, X_ROW[0])
+        nc.sync.dma_start(idx2[:], offs2)
+        nc.sync.dma_start(idx[:], offs)
         nc.sync.dma_start(x_w[:], x_words.rearrange("s p n t -> p s (n t)").bitcast(I32))
+        nc.sync.dma_start(idx3[:], offs3)
         nc.sync.dma_start(w_w[:], w_words.rearrange("s p n t -> p s (n t)").bitcast(I32))
         load_words(wa_w[0][:], wa_words[0])
 
@@ -119,8 +119,7 @@ def tile_moe_dyl_none_kernel(
             )
 
         moves = [(s, r) for s in (1, 0) for r in range(4)]
-        nc.sync.dma_start(idx3[:], offs3)
-        load_scales(nc.sync, wb_s, wb_scales, WB_ROW, range(1, 4))
+        load_scales(nc.sync, wb_s, wb_scales, WB_ROW)
         for move in moves[:2]:
             move_row(*move)
         load_words(wa_w[1][:], wa_words[1])

@@ -88,9 +88,9 @@ def tile_moe_dyl_none_kernel(
         diagonal = sb("diagonal", [P, P], I32)
 
         nc.gpsimd.iota(diagonal[:], [[1, P]], base=0, channel_multiplier=-1)
-        load_scales(nc.gpsimd, w_s, w_scales, W_ROW[0])
-        for tile in (x_s[:], wa_s[0:WA_RAW, :], wb_s[:]):
+        for tile in (wb_s[:], x_s[:], wa_s[0:WA_RAW, :]):
             nc.vector.memset(tile.bitcast(I32), 0)
+        load_scales(nc.gpsimd, wb_s, wb_scales, WB_ROW)
         nc.vector.tensor_scalar(ident[:], diagonal[:], 0, None, mybir.AluOpType.is_equal)
 
         nc.scalar.dma_start(wa_s[WA_RAW:P, :].bitcast(I32), wa_scales.rearrange("s b c -> (s b) c").bitcast(I32))
@@ -119,7 +119,7 @@ def tile_moe_dyl_none_kernel(
             )
 
         moves = [(s, r) for s in (1, 0) for r in range(4)]
-        load_scales(nc.sync, wb_s, wb_scales, WB_ROW)
+        load_scales(nc.sync, w_s, w_scales, W_ROW[0])
         for move in moves[:2]:
             move_row(*move)
         load_words(wa_w[1][:], wa_words[1])

from contextlib import ExitStack

import concourse.mybir as mybir

K, T, E, B, H, N = 1024, 1024, 8, 4, 512, 256
P = 128
SLOTS = P * B
BANK = 512
FLOPS = 2 * K * N * T + 2 * K * H * SLOTS + 2 * H * N * SLOTS

F32 = mybir.dt.float32
BF16 = mybir.dt.bfloat16
I32 = mybir.dt.int32
U32 = mybir.dt.uint32
U16 = mybir.dt.uint16
U8 = mybir.dt.uint8
FP8X4 = mybir.dt.float8_e4m3fn_x4
MULT = mybir.AluOpType.mult
ADD = mybir.AluOpType.add
COPY = mybir.ActivationFunctionType.Copy

X_ROW = (0, 4)
W_ROW = (0, 4)
WA_ROW = (12, 8)
WB_ROW = 8
WA_RAW = 96


def tile_moe_dyl_none_kernel(
    tc, x_words, x_scales, w_words, w_scales, wa_words, wa_scales, wb_words, wb_scales, gate, offs, offs2, offs3, out
):
    nc = tc.nc
    with ExitStack() as ctx:
        keep = ctx.enter_context(tc.tile_pool(name="keep", bufs=1))
        psum = ctx.enter_context(tc.psum_pool(name="psum", bufs=1))

        def sb(name, shape, dtype):
            return keep.tile(shape, dtype, name=name, align_bytes=64)

        def reuse(name, shape, dtype, tag):
            return keep.tile(shape, dtype, name=name, tag=tag, align_bytes=64)

        def bank(name, shape, number):
            return psum.tile(shape, F32, name="%s_%d" % (name, number), offset=4 * BANK * number)

        def part(index, width):
            return slice(index * width, (index + 1) * width)

        def load_words(tile, words):
            nc.sync.dma_start(tile, words.rearrange("p n t -> p (n t)").bitcast(I32))

        def load_scales(queue, tile, scales, first_row):
            rows = 4 * scales.shape[0]
            for q in range(4):
                queue.dma_start(
                    tile[32 * q + first_row : 32 * q + first_row + rows, :].bitcast(I32),
                    scales[:, 4 * q : 4 * q + 4, :].bitcast(I32),
                )

        def gather(dst, window, offsets, entry, count):
            nc.vector.tensor_copy(dst, window.indirect(offsets[:, entry // 16 : (entry + count) // 16]))

        def mm(acc, lhs, lhs_scales, rhs, rhs_scales, start, stop):
            nc.tensor.matmul_mx(
                out=acc,
                lhsT=lhs.bitcast(FP8X4),
                lhsT_scale=lhs_scales,
                rhs=rhs.bitcast(FP8X4),
                rhs_scale=rhs_scales,
                start=start,
                stop=stop,
            )

        idx = sb("idx", [P, SLOTS // 16], U16)
        idx2 = sb("idx2", [P, B * H // 16], U16)
        idx3 = sb("idx3", [P, B * N // 16], U16)
        x_w = sb("x_w", [P, 2, T], I32)
        w_w = sb("w_w", [P, 2, N], I32)
        wa_w = [sb("wa_w%d" % s, [P, E * H], I32) for s in range(2)]
        wb_w = sb("wb_w", [P, E * N], I32)
        x_s = sb("x_s", [P, T], U8)
        w_s = sb("w_s", [P, N], U8)
        wa_s = sb("wa_s", [P, E * H], U8)
        wb_s = sb("wb_s", [P, E * N], U8)
        gate_rows = sb("gate_rows", [P, 2 * P], F32)
        gate_col = sb("gate_col", [P, 2], F32)
        ident = sb("ident", [P, P], F32)
        diagonal = sb("diagonal", [P, P], I32)

        nc.gpsimd.iota(diagonal[:], [[1, P]], base=0, channel_multiplier=-1)
        for tile in (wb_s[:], x_s[:], wa_s[0:WA_RAW, :]):
            nc.vector.memset(tile.bitcast(I32), 0)
        load_scales(nc.gpsimd, wb_s, wb_scales, WB_ROW)
        nc.vector.tensor_scalar(ident[:], diagonal[:], 0, None, mybir.AluOpType.is_equal)

        nc.scalar.dma_start(wa_s[WA_RAW:P, :].bitcast(I32), wa_scales.rearrange("s b c -> (s b) c").bitcast(I32))
        load_scales(nc.scalar, x_s, x_scales, X_ROW[0])
        nc.sync.dma_start(idx2[:], offs2)
        nc.sync.dma_start(idx[:], offs)
        nc.sync.dma_start(x_w[:], x_words.rearrange("s p n t -> p s (n t)").bitcast(I32))
        nc.sync.dma_start(idx3[:], offs3)
        nc.sync.dma_start(w_w[:], w_words.rearrange("s p n t -> p s (n t)").bitcast(I32))
        load_words(wa_w[0][:], wa_words[0])

        waq_listed = sb("waq_listed", [P, B * H], U8)
        gather(waq_listed[:], wa_s[:], idx2, 0, B * H)
        waq_rows = sb("waq_rows", [P, B * H], U8)
        nc.vector.tensor_copy(
            waq_rows[:].rearrange("p (m t q) -> p m t q", m=B, t=4),
            waq_listed[:].rearrange("p (m q t) -> p m t q", m=B, t=4),
        )

        waq_s = [sb("waq_s%d" % s, [P, B * H], U8) for s in range(2)]

        def move_row(s, r):
            raw = WA_RAW + 16 * s
            nc.sync.dma_start(
                waq_s[s][WA_ROW[s] + r : P : 32, :].bitcast(I32), waq_rows[raw + r : raw + 16 : 4, :].bitcast(I32)
            )

        moves = [(s, r) for s in (1, 0) for r in range(4)]
        load_scales(nc.sync, w_s, w_scales, W_ROW[0])
        for move in moves[:2]:
            move_row(*move)
        load_words(wa_w[1][:], wa_words[1])
        for move in moves[2:]:
            move_row(*move)
        load_words(wb_w[:], wb_words[0])
        with nc.allow_non_contiguous_dma(reason="one gate value a partition and block"):
            nc.sync.dma_start(gate_col[:], gate[0, 0 : 2 * P].rearrange("(b p) -> p b", p=P))
        nc.sync.dma_start(gate_rows[:], gate[:, 2 * P : SLOTS])

        xq_s = sb("xq_s", [P, SLOTS], U8)
        gather(xq_s[:], x_s[:], idx, 0, SLOTS)
        xq_w = [sb("xq_w%d" % s, [P, SLOTS], U32) for s in range(2)]
        for s in range(2):
            gather(xq_w[s][:], x_w[:, s, :].bitcast(U32), idx, 0, SLOTS)

        waq_first = sb("waq_first", [P, B, 4, P], U32)
        gather(waq_first[:].rearrange("p m t q -> p m q t"), wa_w[0][:].bitcast(U32), idx2, 0, B * H)
        wbq_s = sb("wbq_s", [P, B * N], U8)
        gather(wbq_s[:], wb_s[:], idx3, 0, B * N)

        result = [sb("result%d" % j, [P, T], F32) for j in range(2)]
        for j in range(2):
            for half in range(2):
                acc = bank("base_acc", [P, BANK], 2 * j + half)
                for s in range(2):
                    mm(acc[:], w_w[:, s, part(j, P)], w_s[W_ROW[s] : P, part(j, P)],
                       x_w[:, s, part(half, BANK)], x_s[X_ROW[s] : P, part(half, BANK)], s == 0, s == 1)
                nc.scalar.copy(result[j][:, part(half, BANK)], acc[:])

        base_first = sb("base_first", [P, 2, N], F32)
        acc = bank("slot_acc", [P, 2, N], 4)
        for m in range(2):
            for s in range(2):
                mm(acc[:, m, :], xq_w[s][:, part(m, P)], xq_s[X_ROW[s] : P, part(m, P)],
                   w_w[:, s, :], w_s[W_ROW[s] : P, :], s == 0, s == 1)
        nc.scalar.copy(base_first[:], acc[:])
        base_second = sb("base_second", [P, 2, 2 * P], F32)
        acc = bank("slot_acc", [P, 2, 2 * P], 5)
        for j in range(2):
            for s in range(2):
                mm(acc[:, j, :], w_w[:, s, part(j, P)], w_s[W_ROW[s] : P, part(j, P)],
                   xq_w[s][:, part(1, 2 * P)], xq_s[X_ROW[s] : P, part(1, 2 * P)], s == 0, s == 1)
        nc.scalar.copy(base_second[:], acc[:])

        def h_pass(m, s, words):
            for t in range(4):
                mm(h_acc[m][:, t, :], words[:, t, :], waq_s[s][WA_ROW[s] : P, part(4 * m + t, P)],
                   xq_w[s][:, part(m, P)], xq_s[X_ROW[s] : P, part(m, P)],
                   s == 0 and t == 0, s == 1 and t == 3)

        h_acc = [bank("h_acc", [P, 4, P], m) for m in range(B)]

        grouped = []

        def close_h(m, tag):
            waq_second = reuse("waq_second%d" % m, [P, 4, P], U32, tag)
            gather(waq_second[:].rearrange("p t q -> p q t"), wa_w[1][:].bitcast(U32), idx2, m * H, H)
            h_pass(m, 0, waq_first[:, m])
            h_pass(m, 1, waq_second)

        def round_h(m, tag):
            grouped.append(reuse("grouped%d" % m, [P, P, 4], BF16, tag))
            nc.scalar.copy(grouped[m][:], h_acc[m][:].rearrange("p t u -> p u t"))

        for m in range(B - 1):
            close_h(m, "waq_second%d" % m)
            round_h(m, "grouped%d" % m)

        hq = []

        def quantise(m):
            name = "hq_w%d" % m
            hq_w = reuse(name, [P, P], U32, (name, "hq_s0", "hq_s1", "hq_s1")[m])
            hq_s = sb("hq_s%d" % m, [P, P], U8)
            nc.vector.quantize_mx(
                out=hq_w[:].bitcast(FP8X4), scales=hq_s[:], in_=grouped[m][:].rearrange("p u t -> p (u t)")
            )
            hq.append((hq_w, hq_s))

        wbq_w = []

        def gather_wb(m):
            name = "wbq_w%d" % m
            behind = (name, "grouped0", "hq_s0", "grouped2")[m]
            wbq_w.append(reuse(name, [P, N], U32, behind))
            gather(wbq_w[m][:], wb_w[:].bitcast(U32), idx3, m * N, N)

        def gate_slots(m):
            y_slots = bank("y_slots", [P, N], m)
            mm(y_slots[:], hq[m][0][:], hq[m][1][:], wbq_w[m][:], wbq_s[WB_ROW:P, part(m, N)], True, True)
            y_gated = sb("y_gated%d" % m, [P, N], F32)
            nc.scalar.activation(y_gated[:], y_slots[:], COPY, scale=gate_col[:, m : m + 1])
            back = bank("back", [P, 2, P], 6 + m)
            for step, source in enumerate((base_first[:, m, :], y_gated[:])):
                for j in range(2):
                    nc.tensor.matmul(back[:, j, :], source[:, part(j, P)], ident[:], is_transpose=True,
                                     start=step == 0 and j == 0, stop=step == 1 and j == 1)
            return back

        backs = []
        for m in range(2):
            gather_wb(m)
            quantise(m)
            backs.append(gate_slots(m))
        close_h(B - 1, "wbq_w0")
        quantise(2)
        for m in range(2, B):
            gather_wb(m)

        summed = sb("summed", [P, 2, 2 * P], F32)

        def scatter(j, m, blocks):
            nc.scalar.activation(
                result[j][:].indirect(idx[:, m * P // 16 : (m + blocks) * P // 16]),
                summed[:, j, m * P : (m + blocks) * P],
                COPY,
            )

        nc.scalar.copy(summed[:, :, part(0, P)], backs[0][:])
        scatter(0, 0, 1)
        round_h(B - 1, "y_gated0")
        nc.scalar.copy(summed[:, :, part(1, P)], backs[1][:])
        scatter(0, 1, 1)

        gated = sb("gated", [P, 2, 2 * P], F32)

        def gate_block(mb, tiles, number):
            acc = bank("y_rows", [P, 2, P], number)
            for j in tiles:
                mm(acc[:, j, :], wbq_w[2 + mb][:, part(j, P)], wbq_s[WB_ROW:P, part(4 + 2 * mb + j, P)],
                   hq[2 + mb][0][:], hq[2 + mb][1][:], True, True)
            for j in tiles:
                nc.vector.tensor_tensor(gated[:, j, part(mb, P)], acc[:, j, :], gate_rows[:, part(mb, P)], MULT)

        def add_scatter(j, mb, blocks):
            cols = slice(mb * P, (mb + blocks) * P)
            nc.vector.tensor_tensor(
                result[j][:].indirect(idx[:, (2 + mb) * P // 16 : (2 + mb + blocks) * P // 16]),
                gated[:, j, cols],
                base_second[:, j, cols],
                ADD,
            )

        gate_block(0, [1, 0], 1)
        quantise(B - 1)
        add_scatter(1, 0, 1)
        scatter(1, 0, 2)
        gate_block(1, [0, 1], 6)
        add_scatter(0, 0, 2)
        nc.sync.dma_start(out[part(0, P), :], result[0][:])
        add_scatter(1, 1, 1)
        nc.sync.dma_start(out[part(1, P), :], result[1][:])
